import numpy as np, ml_dtypes
CORES = [40,64,80,88,96,104,120,144]
N = 8
import mx_ref
BF = ml_dtypes.bfloat16
def gcols(t, e):
    v = np.concatenate([t.reshape(8, 16, -1, 4), np.zeros((8, 16, 1, 4), BF)], axis=2)
    return np.ascontiguousarray(np.stack([v[g][:, e[g]] for g in range(8)])).reshape(128, -1)
def tile(rs):
    return np.stack(rs, axis=2).reshape(128, -1).astype(BF)
def pick(q, e):
    c = np.concatenate([q[0].reshape(128, -1, 4), np.zeros((128, 1, 4), np.uint8)], axis=1); s = np.concatenate([q[1], np.ones((16, 1), np.uint8)], axis=1)
    return (np.ascontiguousarray(c[:, e].reshape(128, -1)), np.ascontiguousarray(s[:, e]))
def join(*qs):
    return (np.concatenate([q[0] for q in qs], axis=1), np.concatenate([q[1] for q in qs], axis=1))
def put(q, e, v):
    c, s = q[0].reshape(128, -1, 4).copy(), q[1].copy(); c[:, e] = v[0].reshape(128, -1, 4); s[:, e] = v[1]
    return (c.reshape(128, -1), s)
def pk(c, s):
    return (np.ascontiguousarray(c), mx_ref.live(s))
def emit(q):
    return q[0], q[1]
def packed(v, rng):
    q = [mx_ref.quantize(np.ascontiguousarray(v[r])) for r in range(N)]
    return np.stack([a for a, b in q]), np.stack([mx_ref.plane(b, rng) for a, b in q])
def values_of_codes():
    e, c = np.zeros((128, 128, 4), np.float32), np.zeros((128, 2, 4), np.uint8)
    e[np.arange(128), np.arange(128), 0] = 1
    c[:127, :, 0] = np.arange(256).reshape(2, 128).T[:127]
    return mx_ref.matmul(mx_ref.quantize(e.reshape(128, 512).astype(BF)), (c.reshape(128, 8), np.full((16, 2), 127, np.uint8))).T.reshape(-1).astype(np.float64)
CODE_VALUE, SCALE_VALUE = values_of_codes(), 2.0 ** (np.arange(256) - 127.0)
def decode(q):
    return (CODE_VALUE[q[0]].reshape(16, 8, -1, 4) * SCALE_VALUE[q[1]][:, None, :, None] + 0.0).reshape(128, -1).astype(np.float32)
def f(rng, *shape):
    return mx_ref.flush((rng.standard_normal(shape, dtype=np.float32) * np.exp2(rng.integers(-2, 3, shape[:-1] + (1,)))).astype(BF))
def wide(rng, *shape, cols=0):
    v = rng.standard_normal(shape, dtype=np.float32) * np.exp2(rng.integers(-12, 13, shape)).astype(np.float32)
    if cols: v *= np.repeat(np.exp2(rng.integers(-cols, cols + 1, shape[:-2] + (1, shape[-1] // 4))) * (rng.random(shape[:-2] + (1, shape[-1] // 4)) > 0.0625), 4, axis=-1).astype(np.float32)
    return mx_ref.flush(v.astype(BF))
C, A, LIFE, T = 288, 128, 96, 7
STEPS = [4, 1, 2]
BEFORE = np.tri(C, k=-1, dtype=bool)
def big(v):
    v = v.astype(np.float32)
    v[np.abs(v) < np.float32(2.0 ** -16)] = 0
    return v.astype(BF)
def numbers_of(rng):
    x = f(rng, N, 128, 4 * C).astype(np.float32) + np.float32(0.5) * np.tile(f(rng, N, 128, 4).astype(np.float32), C)
    return {"x": big(x), "u": np.array(f(rng, N, 128, 512)), "v": np.array(f(rng, N, 128, 512))}
def layers(rng):
    return big(f(rng, N, 128, 2048)).reshape(N, 8, 16, 4, 8, 16, 4)
def weights(rng, w):
    c, p = packed(np.ascontiguousarray(w).reshape(N, 128, 2048), rng)
    return {"wc": c, "ws": p}
def bare(d):
    u = d["u"].astype(np.float32).reshape(N, 8, 16, 128, 4)
    u[:, :, :, np.arange(128) % 16 < 12] = 0
    return d["x"].astype(np.float32).reshape(N, 8, 16, C, 4), u
def planted(rng, d, x, u, w):
    return {"x": x.astype(np.float32).reshape(N, 128, 4 * C).astype(BF), "u": u.reshape(N, 128, 512).astype(BF), "v": d["v"], **weights(rng, w)}
def setup_inputs(rng):
    return {**numbers_of(rng), **weights(rng, layers(rng))}
def setup_inputs_ties(rng):
    d = numbers_of(rng)
    x, u = bare(d)
    o = rng.permutation(N) % 4
    q, half = C // LIFE, LIFE // 2
    sizes = [[LIFE] * q + [0] * (4 - q), [LIFE - 1] * 3 + [C - 3 * (LIFE - 1)], [half] * 3 + [C - 3 * half], [1, 1, 0, C - 2]]
    b = np.arange(4)
    x[:, :, :5] = 0
    for r in range(N):
        shared = [int(g) for g in rng.permutation(8)[:4]] if q == 3 and o[r] == 0 else []
        for g in range(8):
            k = rng.permutation(np.repeat(b, [LIFE, LIFE, half, half] if g in shared else sizes[o[r]]))[:, None]
            top = float(rng.choice([-1.0, 1.0, 2.0]))
            x[r, g, 0] = np.where(b < k, top - 1, np.where(b == k, top, top - rng.integers(0, 2, (C, 4))))
            n = rng.permutation(C)
            x[r, g, 1] = b == (n % 4)[:, None]
            x[r, g, 2, :, 0] = rng.integers(0, 3, C)
            x[r, g, 3, :, 0] = np.where(n < A, 2, 1)
            x[r, g, 4, :, 0] = (n % 4 == 2) & (n < 4 * (T - 1))
            x[r, g, 4, :, 1] = (n % 4 < q) & (n < 4 * (T - 1))
            u[r, g, 3, 16 * g, 0] = 1
            if g in shared: u[r, g, 4, 16 * g + 10:16 * g + 12, 0] = 2048
            elif o[r] == 0: u[r, g, 4, 16 * g + 8:16 * g + 12, 1] = 2048
            for j in range(4):
                u[r, g, 0, 16 * g + 4 + j, j] = 1
                u[r, g, 1, 16 * g + 8 + j, j // 2 if o[r] == 2 else j] = 1024
                u[r, g, 2, 16 * g + 8 + j, 0] = 1
    w = layers(rng)
    w[:, :, :, :, :, :8] = 0
    return planted(rng, d, x, u, w)
def setup_inputs_near(rng):
    d = numbers_of(rng)
    x, u = bare(d)
    o = rng.permutation(N) % 4
    still = [0, 1] + [i for i in range(8, 16)]
    x[:, :, still] = 0
    x[:, :, 0, :, 0] = rng.integers(0, 2, (N, 8, C)) * 2.0 - 1.0
    x[:, :, 1, :, 0] = 2.0 ** -10
    s = rng.integers(0, 16, (N, 8, 4, C))
    x[:, :, 8:12] = ((s[..., None] >> np.arange(4)) & 1) * 2.0 ** (np.arange(4) - 23.0)
    x[:, :, 12] = rng.integers(-1, 2, (N, 8, C, 4)) * 2.0 ** -29
    for r in range(N):
        for g in rng.permutation(8)[:4]: x[r, g, 0, rng.integers(C), 0] = 2.0 ** 29 * float(rng.choice([-1.0, 1.0]))
        k = 1.0 if o[r] == 0 else 2.0 ** -30
        for g in range(8):
            for i in range(9):
                j = (i - 1) % 4
                c = 16 * g + (0 if i == 0 else 3 + i)
                p = 8 if i == 0 else 8 + j if i < 5 else 8 + (j + 1) % 4
                if o[r] < 2:
                    u[r, g, 0, c, 0] = -k if i in (5, 7) else k
                    u[r, g, 1, c, 0] = k
                    u[r, g, p, c] = k
                elif o[r] == 2:
                    if i in (4, 8): u[r, g, 0, c, 0] = 1
                    else: u[r, g, p, c] = k
                else:
                    u[r, g, 12, c, p - 8] = k * (1 + 0.125 * j)
                    if i > 4: u[r, g, 12, c, (p - 7) % 4] = k * 1.125
    w = layers(rng)
    w[:, :, still] = 0
    w[:, :, :, :, :, still] = 0
    return planted(rng, d, x, u, w)
def setup_inputs_late(rng):
    d = numbers_of(rng)
    x, u = bare(d)
    x[:, :, 0] = 0
    e = rng.integers(0, 4, (N, 8))
    for r in range(N):
        for g in range(8): x[r, g, 0, :, e[r, g]] = 2.0 ** -6
    k = 1 + 0.125 * (2 * rng.integers(0, 4, (N, 8, 7, C, 4)) + 1)
    x[:, :, 9:] = k * rng.choice([-1.0, 1.0], k.shape) * 2.0 ** np.array([-14.0, -13.0, -12.0, -11.0, -10.0, -9.0, -8.0])[:, None, None]
    x[:, :, 8] = 0
    x[:, :, 8, :, 0] = 1.96875
    for g in range(8):
        u[:, g, 0, 16 * g] = 1
        for j in range(4):
            u[:, g, 0, 16 * g + 4 + j, j] = 1
            u[:, g, 9 + j, 16 * g + 8 + j] = 1
    w = layers(rng)
    w[:, :, :, :, :, 8:] = 0
    return planted(rng, d, x, u, w)
def setup_inputs_huge(rng):
    d = numbers_of(rng)
    u = bare(d)[1]
    h = rng.permutation(8)
    o = rng.permutation(N) % 3
    most = rng.integers(0, 4, (N, 8, 1, C, 1))
    x = -np.where(np.arange(4) == most, 0.95, 0.75) - 0.05 * rng.random((N, 8, 16, C, 4))
    x[:, h[6:]] *= rng.choice([-1.0, 1.0], (N, 2, 1, C, 1))
    for r in range(N):
        parts = h[6:] if o[r] == 1 else h[:6]
        k = -2.0 ** 30 if o[r] == 2 else 2.0 ** 30
        for g in range(8):
            some = rng.permutation(parts)[:len(parts) // 2]
            for m in parts:
                u[r, m, :, 16 * g] = k * (1 - 0.1 * rng.random((16, 4)))
                for j in range(4):
                    u[r, m, :, 16 * g + 4 + j] = k
                    u[r, m, :, 16 * g + 8 + j] = k
                    if m in some:
                        u[r, m, :, 16 * g + 4 + j, j] = 0.5 * k
                        u[r, m, :, 16 * g + 8 + j, (j + 1) % 4] = 0.5 * k
    a = int(h[0])
    for r in range(N): x[r, a, :, int(rng.integers(C))] = 1.0
    for i in (0, 8, 9, 10, 11):
        u[:, :, :, 16 * a + i] = 0
        u[:, a, :, 16 * a + i] = 2.0 ** 30
    w = np.zeros((N, 128, 4, 128, 4), np.float32)
    i = np.arange(128)
    for b in range(4): w[:, i, b, i, b] = -1
    return planted(rng, d, 2.0 ** 30 * x, u, w.astype(BF))
def setup_inputs_spread(rng):
    d = setup_inputs(rng)
    d["x"] = big(wide(rng, N, 128, 4 * C, cols=6))
    return d
def check_inputs(d):
    b = []
    for k in ("x", "u", "v"):
        a = np.abs(d[k].astype(np.float32))
        if not (np.isfinite(a).all() and ((a == 0) | (a >= 2.0 ** -30) & (a <= 2.0 ** 30)).all()): b.append("a value of " + k)
    none, least, most = [emit(mx_ref.quantize(np.full((128, 16), k, np.float32).astype(BF)))[1][0, 0] for k in (0.0, 2.0 ** -30, 2.0 ** 30)]
    for r in range(N):
        if ((d["wc"][r] == 0x7F) | (d["wc"][r] == 0xFF)).any(): b.append("wc: a code that is no number")
        s = mx_ref.live(d["ws"][r])
        if ((s != none) & ((s < least) | (s > most))).any(): b.append("ws: a scale out of range")
    return b
def reference(x, u, v, wc, ws):
    qu = [mx_ref.quantize(u[r]) for r in range(N)]
    lay = [pk(wc[r], ws[r]) for r in range(N)]
    now = [x[r] for r in range(N)]
    taken = np.zeros((N, 8, C), np.int64)
    g = np.arange(8)
    for step in STEPS:
        score, given = [], []
        for r in range(N):
            s = (mx_ref.matmul(qu[r], mx_ref.quantize(now[r])) + np.float32(0.0)).reshape(8, 16, C)
            o = np.argsort(-s[:, 0], axis=1, kind="stable")[:, :A]
            score.append(s)
            given.append(mx_ref.quantize(gcols(now[r], o)))
        made = []
        for r in range(N):
            came = given[r ^ step]
            objects = decode(came).astype(BF)
            kind = np.argmax(score[r][:, 4:8], axis=1)
            size = np.count_nonzero(kind[:, None] == np.arange(4)[:, None], axis=2)
            stand = np.count_nonzero((kind[:, :, None] == kind[:, None, :]) & BEFORE, axis=2)
            like = (mx_ref.matmul(qu[r], came) + np.float32(0.0)).reshape(8, 16, A)[:, 8:12]
            bites, meals = np.zeros((8, A), np.int64), np.zeros((8, 4, T), np.int64)
            for t in range(T):
                e = np.argmax(np.where((bites < LIFE)[:, None], like, -np.float32(np.inf)), axis=2)
                for k in range(4): bites[g, e[:, k]] += size[:, k]
                meals[:, :, t] = e
            taken[r] = meals[g[:, None], kind, stand % T]
            z = mx_ref.quantize(((now[r].astype(np.float32) + gcols(objects, taken[r]).astype(np.float32)) * np.float32(0.5)).astype(BF))
            made.append(tile([mx_ref.matmul(pick(lay[r], np.arange(128 * b, 128 * b + 128)), z) * np.float32(0.03125) + now[r][:, b::4].astype(np.float32) for b in range(4)]))
        now = made
    y, ol = np.zeros((N, 128, C), np.float32), np.zeros((N, 8, C), np.float32)
    oc, osc = np.zeros((N, 128, 4 * C), np.uint8), np.zeros((N, 16, C), np.uint8)
    for r in range(N):
        q = mx_ref.quantize(now[r])
        y[r] = mx_ref.matmul(mx_ref.quantize(v[r]), q)
        ol[r] = taken[r]
        oc[r], osc[r] = emit(q)
    return {"y": y, "ol": ol, "oc": oc, "osc": osc}

@@ -1,0 +1,564 @@
+from concourse.bass import DstId, RemoteDMATransfer
+from concourse.mybir import dt, AluOpType, AxisListType, ActivationFunctionType
+
+C, A, NT = 288, 128, 7
+HC = C // 2
+STEPS = [4, 1, 2]
+H = 1.0e29
+BIG = float(2 ** 20)
+CK = 448
+TS_ = CK // 4
+F32, BF, I32, U16, X4, U8 = "float32", "bfloat16", "int32", "uint16", "float8_e4m3fn_x4", "uint8"
+TW = [288, 224, 160, 128, 128]
+SLOT = {}
+for _m in range(17, 0, -1):
+    SLOT[_m] = ((18 - _m) // 4, (18 - _m) % 4)
+ON_SCALAR = (17, 16, 9)
+
+
+def sb(n, d):
+    return ("sbuf", [128, n], d)
+
+
+SCRATCH = {
+    "ps": ("psum", [128, 4096], F32),
+    "X": sb(4 * C, BF), "Y": sb(4 * C, BF), "Xh": sb(4 * C, BF), "Z": sb(4 * C, BF), "M": sb(4 * A, BF),
+    "ub": sb(512, BF), "vb": sb(512, BF),
+    "qU": sb(128, X4), "sU": sb(128, U8), "qV": sb(128, X4), "sV": sb(128, U8),
+    "qR": sb(768, X4), "sR": sb(768, U8), "qW": sb(512, X4), "sW": sb(512, U8),
+    "qX": sb(C, X4), "sX": sb(C, U8), "qZ": sb(C, X4), "sZ": sb(C, U8),
+    "Gt": sb(512, BF), "qG": sb(128, X4), "sG": sb(128, U8),
+    "Et": sb(2048, BF), "qE": sb(512, X4), "sE": sb(512, U8), "ones": sb(512, BF),
+    "ip": sb(8, I32), "fp": sb(8, F32), "col": sb(24, F32), "s16": sb(128, F32), "offQ": sb(18, U16),
+    "ofu": sb(48, F32), "offU": sb(48, U16),
+    "Mk": sb(C, F32), "K16": sb(C, F32), "Kd": sb(C, BF), "A16": sb(C, F32), "A16f": sb(3 * C, BF), "A4": sb(C, F32),
+    "val": sb(C, F32), "m16": sb(18, F32), "Rc": sb(18, F32), "IC": sb(18, F32),
+    "Bm": sb(C, F32), "hold": sb(C, F32), "rel": sb(3 * C, F32), "junk": sb(2448, BF), "rows": sb(18, F32),
+    "dseg": sb(C, BF), "R1": sb(18, F32), "ext": sb(C, F32), "offP": sb(18, U16),
+    "win": sb(C, F32), "offM": sb(32, U16), "c0": sb(C, F32),
+    "m01": sb(C, F32), "m012": sb(C, F32), "mx": sb(C, F32), "gf": sb(3 * C, BF), "gx": sb(3 * C, BF),
+    "Lw": sb(5 * C, F32), "offW": sb(6, U16), "wlo": sb(96, F32), "w1": sb(96, F32), "W": sb(96, F32),
+    "sg": sb(96, F32), "ex": sb(96, F32), "kp": sb(96, F32), "k2": sb(16, F32),
+    "f1": sb(18, F32), "f2": sb(18, F32), "offK": sb(18, U16), "vlo": sb(C, F32), "vv": sb(C, F32), "v4": sb(C, F32),
+    "z1": sb(72, F32), "z2": sb(72, I32), "offZ": sb(72, U16),
+    "LM": sb(144, F32), "NEG": sb(128, F32), "pm": sb(128, F32), "st": sb(144, F32), "ee": sb(8, F32),
+    "offE": sb(8, U16), "offT": sb(16, U16), "offD": sb(2, U16), "dw": sb(96, F32), "xn": sb(2, F32),
+    "Bh": sb(512, BF), "tab": sb(16 * TS_, BF), "tabE": sb(16 * TS_, BF), "iq": sb(512, BF),
+    "olw": sb(4 * C, F32),
+}
+for _t in range(5):
+    SCRATCH["T%d" % _t] = sb(4 * TW[_t], BF)
+    SCRATCH["qT%d" % _t] = sb(TW[_t], X4)
+    SCRATCH["sT%d" % _t] = sb(TW[_t], U8)
+for _r in range(3):
+    for _n in ("qM", "qH", "qL"):
+        SCRATCH["%s%d" % (_n, _r)] = sb(A, X4)
+    for _n in ("sM", "sH", "sL"):
+        SCRATCH["%s%d" % (_n, _r)] = sb(A, U8)
+
+POOL = {"v": 50, "s": 40, "p": 16, "g": 18, "d": 16}
+SEMAPHORES = ["loc"] + ["arr%d" % r for r in range(3)] + ["hop%d" % r for r in range(3)]
+for _q in POOL:
+    SEMAPHORES += ["%s%d" % (_q, i) for i in range(POOL[_q])]
+
+
+def helpers(topo, src, dst):
+    can = [h for h in topo.cores_of(src) if h != src and topo.may_write(h, dst)]
+    near = [h for h in can if topo.die(h) == topo.die(src)]
+    far = [h for h in can if topo.die(h) != topo.die(src)]
+    return near[0], far[0], near[1]
+
+
+def bits(engines):
+    m = 0
+    for e in engines:
+        m |= 1 << e
+    return m
+
+
+def helper_program(g, core, T, topo):
+    own = [c for c in T.cores if core in topo.cores_of(c)]
+    if not own:
+        return
+    src = own[0]
+    rank = T.rank_of(src)
+    sent = 0
+    for r, step in enumerate(STEPS):
+        dst = T.cores[rank ^ step]
+        hs = helpers(topo, src, dst)
+        if core not in hs:
+            continue
+        k = hs.index(core)
+        n_in = len(topo.engines(src, core))
+        rid, pid = topo.addr(dst, core)
+        mask = topo.mask(core, dst)
+        if k < 2:
+            g.wait_ge(T.sem["hop%d" % r], n_in // 2)
+            a = T["qH%d" % r][:, 64 * k:64 * k + 64].bitcast(dt.uint8)
+            b = T["qL%d" % r][:, 64 * k:64 * k + 64].bitcast(dt.uint8)
+        else:
+            g.wait_ge(T.sem["hop%d" % r], n_in)
+            a = T["sH%d" % r][:]
+            b = T["sL%d" % r][:]
+        g.remote_dma(b, a, T.sem["arr%d" % r], T.sem.loc, pid, rid, mask)
+        sent += len(topo.engines(core, dst))
+    if sent:
+        g.wait_ge(T.sem.loc, sent)
+
+
+def emit(g, T, ops):
+    Q = {"v": g.vector, "s": g.scalar, "p": g.tensor, "g": g, "y": g.sync}
+    last_w, readers, bank = {}, {}, {}
+    known = {q: 0 for q in Q}
+    closure, at_issue, waits, signal = [], [], [], set()
+    for i, (q, fn, rd, wr, bk, ext, dma) in enumerate(ops):
+        deps = set()
+        for k in rd:
+            if k in last_w:
+                deps.add(last_w[k])
+        for k in wr:
+            if k in last_w:
+                deps.add(last_w[k])
+            deps.update(readers.get(k, []))
+        for b in bk:
+            deps.update(j for j in bank.get(b, []) if ops[j][0] != q)
+        need = [j for j in deps if not known[q] >> j & 1]
+        need = [j for j in need if not any(j2 != j and closure[j2] >> j & 1 for j2 in need)]
+        for j in need:
+            known[q] |= closure[j]
+            signal.add(j)
+        waits.append(sorted(need))
+        at_issue.append(known[q])
+        closure.append(known[q] | 1 << i)
+        if fn is not None:
+            for k in rd:
+                readers.setdefault(k, []).append(i)
+        for k in wr:
+            last_w[k] = i
+            readers[k] = []
+        for b in bk:
+            bank[b] = [j for j in bank.get(b, []) if ops[j][0] == q] + [i]
+    user = {q: [] for q in POOL}
+    count, mark = {}, {}
+    for i, (q, fn, rd, wr, bk, ext, dma) in enumerate(ops):
+        for j in waits[i]:
+            Q[q].wait_ge(T.sem[mark[j][0]], mark[j][1])
+        for name, val in ext:
+            Q[q].wait_ge(T.sem[name], val)
+        if fn is None:
+            continue
+        ins = fn(Q[q])
+        if i in signal:
+            pool = "d" if dma else q
+            free = [n for n, j in enumerate(user[pool]) if not dma and at_issue[i] >> j & 1]
+            if free:
+                n = free[0]
+                user[pool][n] = i
+            else:
+                n = len(user[pool])
+                user[pool].append(i)
+            name = "%s%d" % (pool, n)
+            inc = 16 if dma else 1
+            count[name] = count.get(name, 0) + inc
+            mark[i] = (name, count[name])
+            ins.then_inc(T.sem[name], inc)
+
+
+def rank_program(g, core, T, topo):
+    rank = T.rank_of(core)
+    if rank is None:
+        helper_program(g, core, T, topo)
+        return
+    op = AluOpType
+    AF = ActivationFunctionType
+    ops = []
+
+    def add(q, fn, rd=(), wr=(), bk=(), ext=(), dma=False):
+        ops.append((q, fn, list(rd), list(wr), list(bk), list(ext), dma))
+
+    def ts(out, in0, s1, s2, o0, o1, rd, wr, bk=()):
+        if o1 is None:
+            add("v", lambda e: e.tensor_scalar(out, in0, s1, None, o0), rd, wr, bk)
+        else:
+            add("v", lambda e: e.tensor_scalar(out, in0, s1, s2, o0, o1), rd, wr, bk)
+
+    def tt(out, a, b, o, rd, wr, bk=()):
+        add("v", lambda e: e.tensor_tensor(out, a, b, o), rd, wr, bk)
+
+    def cp(out, a, rd, wr, bk=()):
+        add("v", lambda e: e.tensor_copy(out, a), rd, wr, bk)
+
+    def ms(out, c, wr):
+        add("v", lambda e: e.memset(out, c), (), wr)
+
+    def scan(out, d0, d1, init, o0, o1, rd, wr, bk=()):
+        add("v", lambda e: e.tensor_tensor_scan(out, d0, d1, init, o0, o1), rd, wr, bk)
+
+    def quant(qc, sc, a, rd, wr):
+        add("v", lambda e: e.quantize_mx(qc, sc, a), rd, wr)
+
+    def act(out, a, f, rd, wr, bk=(), **kw):
+        add("s", lambda e: e.activation(out, a, f, **kw), rd, wr, bk)
+
+    def mm(b, n, lc, ls, rc, rs, rd, start=True, stop=True, ext=()):
+        add("p", lambda e: e.matmul_mx(T.ps[:, 512 * b:512 * b + n], lc, ls, rc, rs, start, stop), rd, (), [b], ext)
+
+    def iota(out, pat, base, cm, wr, small=True):
+        if small:
+            add("g", lambda e: e.iota(out, pat, base, cm, allow_small_or_imprecise_dtypes=True), (), wr)
+        else:
+            add("g", lambda e: e.iota(out, pat, base, cm), (), wr)
+
+    def dma(q, out, a, rd, wr):
+        add(q, lambda e: e.dma_start(out, a), rd, wr, dma=True)
+
+    def PS(b, a, n):
+        return T.ps[:, 512 * b + a:512 * b + n]
+
+    def col(i):
+        return T.col[:, i:i + 1]
+
+    def s16(i):
+        return T.s16[:, 16 * i:16 * i + 16]
+
+    def quant_x(h):
+        quant(T.qX[:, HC * h:HC * (h + 1)], T.sX[:, HC * h:HC * (h + 1)], T.X[:, 4 * HC * h:4 * HC * (h + 1)],
+              XK[4 * h:4 * h + 4], ["qX%d" % h])
+
+    XK = ["X%d%d" % (h, b) for h in range(2) for b in range(4)]
+    YK = ["Y%d%d" % (h, b) for h in range(2) for b in range(4)]
+    dma("y", T.X[:], T.x[:], (), XK)
+    dma("s", T.ub[:], T.u[:], (), ["ub"])
+    add("y", None, XK)
+    dma("y", T.qW[:].bitcast(dt.uint8), T.wc[:], (), ["qW"])
+    dma("y", T.sW[:], T.ws[:], (), ["sW"])
+    dma("y", T.vb[:], T.v[:], (), ["vb"])
+    iota(T.ip[:, 0:2], [[15, 2]], 0, 1, ["ip0"], small=False)
+    iota(s16(0), [[1, 16]], 0, 0, ["s0"])
+    iota(T.ofu[:, 0:8], [[16, 8]], 0, 0, ["ofu0"])
+    iota(T.m16[:], [[16, 18]], 0, 0, ["m16"])
+    iota(s16(1), [[0, 4], [1, 4]], 0, 0, ["s1"])
+    for t, a in ((2, 112), (3, 48), (0, 240), (1, 176), (4, 0)):
+        iota(T["T%d" % t][:, 4 * a:], [[0, 4 * (TW[t] - a)]], 0, 0, ["T%d%d" % (t, e) for e in range(4)])
+    iota(T.val[:], [[4, C]], 0, 0, ["val"])
+    iota(T.ofu[:, 8:40], [[1, 4], [16, 8]], 4, 0, ["ofu1"])
+    iota(T.ofu[:, 40:48], [[16, 8]], 8, 0, ["ofu2"])
+    iota(T.kp[:], [[0, 6], [1, 4], [0, 4]], 0, 0, ["kp"])
+    iota(T.Lw[:, 4 * C:5 * C], [[1, C]], 1 + 6 * CK, 0, ["L4"])
+    ms(T.K16[:], H, ["K16"])
+    ts(T.ip[:, 2:4], T.ip[:, 0:2], 15, None, op.bitwise_and, None, ["ip0"], ["ip2"])
+    ts(T.ip[:, 4:5], T.ip[:, 0:1], 2, 3, op.logical_shift_right, op.bitwise_and, ["ip0"], ["ip4"])
+    ts(T.ip[:, 5:6], T.ip[:, 0:1], 3, None, op.bitwise_and, None, ["ip0"], ["ip5"])
+    ts(T.ip[:, 6:7], T.ip[:, 0:1], 112, None, op.bitwise_and, None, ["ip0"], ["ip6"])
+    ms(T.ones[:], 1.0, ["ones"])
+    cp(T.fp[:, 0:5], T.ip[:, 2:7], ["ip2", "ip4", "ip5", "ip6"], ["fp"])
+    qc, qm, kc, rc_, gc_ = [T.fp[:, i:i + 1] for i in range(5)]
+    ms(T.K16[:, 0:C:16], -H, ["K16"])
+    ts(s16(5), s16(0), qc, 0.5, op.is_equal, op.subtract, ["s0", "fp"], ["s5"])
+    ts(T.offQ[:], T.m16[:], 0.0, qc, op.mult, op.add, ["m16", "fp"], ["offQ"])
+    ts(T.col[:, 16:24], T.ofu[:, 0:8], gc_, None, op.is_equal, None, ["ofu0", "fp"], ["gcol"])
+    ts(s16(2), s16(5), 2 * H, None, op.mult, None, ["s5"], ["s2"])
+    cp(T.offU[:, 0:8], T.ofu[:, 0:8], ["ofu0"], ["offU0"])
+    ts(s16(6), s16(0), qc, 1024.0, op.is_equal, op.mult, ["s0", "fp"], ["s6"])
+    ts(s16(7), s16(0), qm, -4096.0, op.is_equal, op.mult, ["s0", "fp"], ["s7"])
+    ms(T.Kd[:], 1.0, ["Kd"])
+    tt(s16(3), s16(6), s16(7), op.add, ["s6", "s7"], ["s3"])
+    ts(col(3), kc, 1.0, None, op.add, None, ["fp"], ["col3"])
+    ts(col(4), kc, 2.5, 4096.0, op.is_lt, op.mult, ["fp"], ["col4"])
+    ts(col(0), qc, -1.0, 15.0 - 1024.0, op.mult, op.add, ["fp"], ["col0"])
+    ts(s16(6), s16(1), kc, -16384.0, op.is_equal, op.mult, ["s1", "fp"], ["s6"])
+    ts(s16(7), s16(1), col(3), 4096.0, op.is_equal, op.mult, ["s1", "col3"], ["s7"])
+    ms(T.Kd[:, 0:C:16], 0.0, ["Kd"])
+    ms(T.rows[:, 0:1], 0.0, ["rows0"])
+    tt(s16(4), s16(6), s16(7), op.add, ["s6", "s7"], ["s4"])
+    ts(T.Rc[:], T.m16[:], col(0), T.s16[:, 63:64], op.add, op.add, ["m16", "col0", "s3"], ["Rc"])
+    ts(col(1), T.s16[:, 63:64], 0.0, -1.0, op.min, op.mult, ["s3"], ["col1"])
+    ts(col(14), col(4), rc_, None, op.subtract, None, ["col4", "fp"], ["col14"])
+    act(T.Mk[:], s16(2).indirect(T.offQ[:]), AF.Copy, ["s2", "offQ"], ["Mk"])
+    for j in range(8):
+        act(T.Gt[:, 64 * j:64 * j + 64], T.ones[:, 0:64], AF.Copy, ["ones", "gcol"], ["Gt%d" % j], scale=col(16 + j))
+    act(T.A16[:], s16(3).indirect(T.offQ[:]), AF.Copy, ["s3", "offQ"], ["A16"])
+    quant(T.qU[:], T.sU[:], T.ub[:], ["ub"], ["qU"])
+    add("v", lambda e: e.tensor_copy(T.qR[:, 0:128].bitcast(dt.uint32), T.qU[:].bitcast(dt.uint32).indirect(T.offU[:, 0:8])),
+        ["qU", "offU0"], ["qR0"])
+    act(T.sR[:, 0:128], T.sU[:].indirect(T.offU[:, 0:8]), AF.Copy, ["qU", "offU0"], ["sR0"])
+    act(T.A4[:], s16(4).indirect(T.offQ[:]), AF.Copy, ["s4", "offQ"], ["A4"])
+    quant_x(0)
+
+    def e_tile(b):
+        add("g", lambda e: e.affine_select(T.Et[:, 512 * b:512 * b + 512], T.ones[:], [[1, 128], [256, 4]], op.is_equal, 0.0,
+                                           -256 * b, -1), ["ones"], ["Et%d" % b])
+    e_tile(0)
+    e_tile(1)
+
+    def late_consts():
+        cp(T.offU[:, 8:40], T.ofu[:, 8:40], ["ofu1"], ["offU1"])
+        ts(T.offU[:, 40:48], T.ofu[:, 40:48], kc, None, op.add, None, ["ofu2", "fp"], ["offU2"])
+        ms(T.sg[:], 0.0, ["sg"])
+        add("v", lambda e: e.tensor_copy(T.qR[:, 128:768].bitcast(dt.uint32), T.qU[:].bitcast(dt.uint32).indirect(T.offU[:, 8:48])),
+            ["qU", "offU1", "offU2"], ["qR1"])
+        act(T.sR[:, 128:768], T.sU[:].indirect(T.offU[:, 8:48]), AF.Copy, ["qU", "offU1", "offU2"], ["sR1"])
+        class_scores()
+        act(T.c0[:], PS(4, 0, C), AF.Copy, [], ["c0"], [4])
+        ms(T.sg[:, 0:96:4], 512.0, ["sg"])
+        ms(T.NEG[:], -H, ["NEG"])
+        ms(T.LM[:, 128:144], 0.0, ["LMd"])
+        ms(T.st[:, 0:1], 1.0, ["st0"])
+        ts(T.w1[:, 0:16], T.kp[:, 80:96], kc, None, op.is_ge, None, ["kp", "fp"], ["w1"])
+        ts(T.k2[:], T.kp[:, 80:96], kc, -BIG / 512, op.is_lt, op.mult, ["kp", "fp"], ["k2"])
+        ms(T.sg[:, 1:96:4], -512.0, ["sg"])
+        ts(col(5), rc_, 1.5, None, op.is_lt, None, ["fp"], ["col5"])
+        ts(col(6), rc_, 1.0, None, op.is_equal, None, ["fp"], ["col6"])
+        ts(col(8), rc_, 0.0, BIG - 95.5 * 512, op.is_equal, op.mult, ["fp"], ["col8"])
+        tt(T.k2[:], T.k2[:], T.sg[:, 80:96], op.mult, ["k2", "sg"], ["k2"])
+        ts(T.offW[:], T.m16[:, 0:6], 0.0, col(13), op.mult, op.add, ["m16", "col13"], ["offW"])
+        ts(T.IC[:], T.m16[:], col(11), qc, op.add, op.add, ["m16", "col11", "fp"], ["IC"])
+        tt(T.sg[:, 80:96], T.sg[:, 80:96], T.w1[:, 0:16], op.mult, ["w1", "sg"], ["sg"])
+        ts(T.k2[:, 2:3], col(8), -BIG, None, op.add, None, ["col8", "k2"], ["k2"])
+        tt(T.ex[:], T.kp[:], T.sg[:], op.mult, ["kp", "sg"], ["ex"])
+        ts(col(12), col(10), col(4), None, op.subtract, None, ["col10", "col4"], ["col12"])
+        ts(T.ex[:], T.ex[:], -float(CK), None, op.mult, None, ["ex"], ["ex"])
+        tt(T.ex[:, 80:96], T.ex[:, 80:96], T.k2[:], op.add, ["ex", "k2"], ["ex"])
+        act(T.A16f[:, 0:C], s16(3).indirect(T.offQ[:]), AF.Copy, ["s3", "offQ"], ["A16f0"], scale=1.0 / 512)
+        for j in (1, 2):
+            act(T.A16f[:, C * j:C * j + C], T.A16f[:, 0:C], AF.Copy, ["A16f0"], ["A16f%d" % j])
+
+    def late_columns():
+        ts(col(7), qc, 128.0, None, op.add, None, ["fp"], ["col7"])
+        ts(col(9), col(4), 4.0, None, op.add, None, ["col4"], ["col9"])
+        ts(col(10), rc_, float(TS_), -1.0, op.mult, op.add, ["fp"], ["col10"])
+        ts(col(11), col(1), -24.0 * C / 4096, 9.0 * C, op.mult, op.add, ["col1"], ["col11"])
+        ts(col(13), kc, float(C), C - 1.0, op.mult, op.add, ["fp"], ["col13"])
+
+    def class_scores():
+        for k in range(4):
+            mm(4 + k, C, T.qR[:, 128 * (k + 1):128 * (k + 2)], T.sR[:, 128 * (k + 1):128 * (k + 2)], T.qX[:], T.sX[:],
+               ["qR1", "sR1"] + QX)
+
+    n_loc = [0]
+
+    def send(r, step):
+        dst = T.cores[rank ^ step]
+        hs = helpers(topo, core, dst)
+        tr = []
+        for k in range(2):
+            en = topo.engines(core, hs[k])
+            half = len(en) // 2
+            rid, pid = topo.addr(hs[k], core)
+            tr.append(RemoteDMATransfer(dst_ids=[DstId(rid=rid, pnc=pid)], dma_engine_mask=bits(en[half * k:half * k + half]),
+                                        remote_sem=T.sem["hop%d" % r],
+                                        src=T["qM%d" % r][:, 64 * k:64 * k + 64].bitcast(dt.uint8),
+                                        dst=T["qH%d" % r][:, 64 * k:64 * k + 64].bitcast(dt.uint8)))
+            n_loc[0] += half
+        add("g", lambda e: e.remote_dma_fused(tr, local_sem=T.sem.loc), ["qM%d" % r])
+        rid, pid = topo.addr(hs[2], core)
+        add("g", lambda e: e.remote_dma(T["sH%d" % r][:], T["sM%d" % r][:], T.sem["hop%d" % r], T.sem.loc, pid, rid,
+                                        topo.mask(core, hs[2])), ["qM%d" % r])
+        n_loc[0] += len(topo.engines(core, hs[2]))
+        return sum(len(topo.engines(h, core)) for h in helpers(topo, dst, core))
+
+    QX = ["qX0", "qX1"]
+    u0c, u0s = T.qR[:, 0:128], T.sR[:, 0:128]
+    mm(7, HC, u0c, u0s, T.qX[:, 0:HC], T.sX[:, 0:HC], ["qR0", "sR0", "qX0"])
+    for r, step in enumerate(STEPS):
+        last = r == len(STEPS) - 1
+        def slot(m, w):
+            t, e = SLOT[m]
+            return T["T%d" % t][:, e:4 * w:4], "T%d%d" % (t, e)
+
+        def compare(m, b):
+            view, key = slot(m, 16 * m)
+            ts(view, PS(b, 0, 16 * m), T.hold[:, 16 * m + 15:16 * m + 16], None, op.is_lt, None, ["hold%d" % (m // 9)], [key], [b])
+            j0 = 8 * m * (m - 1)
+            act(T.junk[:, j0:j0 + 16 * m], view, AF.Copy, [key], ["junk%d" % m, "rows%d" % m], accum_out=T.rows[:, m:m + 1])
+
+        def colsum(t):
+            quant(T["qT%d" % t][:], T["sT%d" % t][:], T["T%d" % t][:], ["T%d%d" % (t, e) for e in range(4)], ["qT%d" % t])
+            mm(2, TW[t], T.qG[:], T.sG[:], T["qT%d" % t][:], T["sT%d" % t][:], ["qG", "qT%d" % t], t == 0, t == 4)
+        if r == 0:
+            quant_x(1)
+        tt(T.Bm[:, 0:HC], PS(7, 0, HC), T.Mk[:, 0:HC], op.min, ["Mk"], ["Bm0"], [7])
+        if r > 0:
+            quant_x(1)
+        for b in (0, 1):
+            mm(b, C, u0c, u0s, T.qX[:], T.sX[:], ["qR0", "sR0"] + QX)
+        scan(T.hold[:, 0:HC], T.K16[:, 0:HC], T.Bm[:, 0:HC], -H, op.min, op.max, ["K16", "Bm0"], ["hold0"])
+        for m in (8, 7, 6, 5):
+            compare(m, 7)
+        if r > 0:
+            class_scores()
+        tt(T.Bm[:, HC:C], PS(0, HC, C), T.Mk[:, HC:C], op.min, ["Mk"], ["Bm1"], [0])
+        compare(4, 0)
+        scan(T.hold[:, HC:C], T.K16[:, HC:C], T.Bm[:, HC:C], -H, op.min, op.max, ["K16", "Bm1"], ["hold1"])
+        for n, m in enumerate(ON_SCALAR):
+            act(T.rel[:, C * n:C * n + 16 * m], PS(1, 0, 16 * m), AF.Relu, ["hold1"], ["rel%d" % n], [1],
+                bias=T.hold[:, 16 * m + 15:16 * m + 16], scale=-1.0)
+        for n, m in enumerate(ON_SCALAR):
+            view, key = slot(m, 16 * m)
+            act(view, T.rel[:, C * n:C * n + 16 * m], AF.Sign, ["rel%d" % n], [key, "rows%d" % m], accum_out=T.rows[:, m:m + 1])
+        if r == 0:
+            quant(T.qG[:], T.sG[:], T.Gt[:], ["Gt%d" % j for j in range(8)], ["qG"])
+        compare(3, 0)
+        for m in (15, 14, 13, 12, 11):
+            compare(m, 0)
+        tt(T.T0[:, 0:4 * C:4], PS(0, 0, C), T.hold[:], op.is_le, ["hold0", "hold1"], ["T00"], [0])
+        compare(10, 0)
+        scan(T.dseg[:], T.Kd[:], T.T0[:, 0:4 * C:4], 0.0, op.mult, op.add, ["Kd", "T00"], ["dseg"])
+        compare(2, 0)
+        compare(1, 0)
+        colsum(0)
+        colsum(1)
+        tt(T.R1[:], T.Rc[:], T.dseg[:, 15:C:16], op.subtract, ["Rc", "dseg"], ["R1"])
+        colsum(2)
+        colsum(3)
+        colsum(4)
+        if r > 0:
+            cp(T.c0[:], PS(4, 0, C), [], ["c0"], [4])
+        else:
+            late_columns()
+        tt(T.A16[:, 15:C:16], T.R1[:], T.rows[:], op.subtract, ["R1"] + ["rows%d" % m for m in range(18)], ["A16"])
+        scan(T.ext[:], PS(2, 0, C), T.A16[:], -4096.0, op.max, op.add, ["A16"], ["ext"], [2])
+        ts(T.offP[:], T.ext[:, 15:C:16], col(1), None, op.add, None, ["ext", "col1"], ["offP"])
+        cp(T.win[:].indirect(T.offP[:]), T.val[:], ["offP", "val"], ["win"])
+        scan(T.ext[:, 0:A], T.A4[:, 0:A], T.win[:, 0:A], 0.0, op.add, op.max, ["A4", "win"], ["ext"])
+        ts(T.offM[:], T.ext[:, 3:A:4], col(14), None, op.subtract, None, ["ext", "col14"], ["offM"])
+        cp(T.M[:, 0:256], T.X[:].indirect(T.offM[:, 0:16]), XK + ["offM"], ["M0"])
+        act(T.M[:, 256:512], T.X[:].indirect(T.offM[:, 16:32]), AF.Copy, XK + ["offM"], ["M1"])
+        quant(T["qM%d" % r][:], T["sM%d" % r][:], T.M[:], ["M0", "M1"], ["qM%d" % r])
+        n_arr = send(r, step)
+        if r == 0:
+            iota(T.Lw[:, 0:C], [[0, C]], 0, 0, ["L0"])
+            e_tile(2)
+            e_tile(3)
+            iota(T.iq[:], [[1, 128], [0, 4]], 0, 0, ["iq"])
+            late_consts()
+        tt(T.m01[:], PS(5, 0, C), T.c0[:], op.max, ["c0"], ["m01"], [5])
+        tt(T.m012[:], PS(6, 0, C), T.m01[:], op.max, ["m01"], ["m012"], [6])
+        tt(T.mx[:], PS(7, 0, C), T.m012[:], op.max, ["m012"], ["mx"], [7])
+        tt(T.gf[:, 2 * C:3 * C], PS(7, 0, C), T.m012[:], op.is_le, ["m012"], ["gf2"], [7])
+        tt(T.gf[:, 0:C], PS(4, 0, C), T.mx[:], op.is_ge, ["mx"], ["gf0"], [4])
+        tt(T.gf[:, C:2 * C], T.m01[:], T.mx[:], op.is_ge, ["m01", "mx"], ["gf1"])
+        act(T.Xh[:], T.X[:], AF.Copy, XK, ["Xh"], scale=0.5)
+        for j, c in ((2, 3 * CK), (0, 0), (1, CK)):
+            scan(T.Lw[:, C * (j + 1):C * (j + 2)], T.gf[:, C * j:C * j + C], T.Lw[:, 0:C], float(c), op.add, op.add,
+                 ["gf%d" % j, "L0"], ["L%d" % (j + 1)])
+        LK = ["L0", "L1", "L2", "L3", "L4"]
+        act(T.wlo[:], T.Lw[:, 0:4 * C].indirect(T.offW[:]), AF.Copy, LK + ["offW"], ["wlo"])
+        scan(T.gx[:], T.gf[:], T.A16f[:], -8.0, op.max, op.add, ["A16f0", "A16f1", "A16f2", "gf0", "gf1", "gf2"], ["gx"])
+        tt(T.w1[:], T.Lw[:, C:5 * C].indirect(T.offW[:]), T.wlo[:], op.subtract, LK + ["offW", "wlo"], ["w1"])
+        tt(T.f1[:], T.gx[:, 15:C:16], T.gx[:, C + 15:2 * C:16], op.add, ["gx"], ["f1"])
+        tt(T.w1[:], T.w1[:], T.sg[:], op.mult, ["w1", "sg"], ["w1"])
+        tt(T.f2[:], T.f1[:], T.gx[:, 2 * C + 15:3 * C:16], op.add, ["gx", "f1"], ["f2"])
+        tt(T.W[:], T.w1[:], T.ex[:], op.add, ["w1", "ex"], ["W"])
+        ts(T.f1[:], T.f2[:], -float(C), None, op.mult, None, ["f2"], ["f1"])
+        tt(T.f2[:], T.f1[:], T.IC[:], op.add, ["f1", "IC"], ["f2"])
+        cp(T.offK[:], T.f2[:], ["f2"], ["offK"])
+        act(T.vlo[:], T.Lw[:, 0:4 * C].indirect(T.offK[:]), AF.Copy, LK + ["offK"], ["vlo"])
+        if r == 0:
+            for h in range(2):
+                quant(T.qE[:, 256 * h:256 * h + 256], T.sE[:, 256 * h:256 * h + 256], T.Et[:, 1024 * h:1024 * h + 1024],
+                      ["Et%d" % (2 * h), "Et%d" % (2 * h + 1)], ["qE%d" % h])
+        if r == 1:
+            quant(T.qV[:], T.sV[:], T.vb[:], ["vb"], ["qV"])
+        tt(T.vv[:], T.Lw[:, C:5 * C].indirect(T.offK[:]), T.vlo[:], op.subtract, LK + ["offK", "vlo"], ["vv"])
+        gaps = [
+            [lambda: scan(T.v4[:], T.A4[:], T.vv[:], 0.0, op.add, op.max, ["A4", "vv"], ["v4"])],
+            [lambda: ts(T.z1[:], T.v4[:, 3:C:4], col(9), 1.0 / 7, op.subtract, op.mult, ["v4", "col9"], ["z1"])],
+            [lambda: cp(T.z2[:], T.z1[:], ["z1"], ["z2"])],
+            [lambda: ts(T.z2[:], T.z2[:], 63, None, op.bitwise_and, None, ["z2"], ["z2"])],
+            [lambda: ts(T.z1[:], T.z2[:], -7.0, col(12), op.mult, op.add, ["z2", "col12"], ["z1"])],
+            [lambda: tt(T.z1[:], T.z1[:], T.v4[:, 3:C:4], op.add, ["z1", "v4"], ["z1"])],
+            [lambda: cp(T.offZ[:], T.z1[:], ["z1"], ["offZ"])],
+        ]
+        qL, sL = T["qL%d" % r][:], T["sL%d" % r][:]
+        mm(3, A, T.qR[:, 640:768], T.sR[:, 640:768], qL, sL, ["qR1", "sR1"], ext=[("arr%d" % r, n_arr)])
+        mm(2, A, T.qR[:, 640:768], T.sR[:, 640:768], qL, sL, ["qR1", "sR1"])
+        for b in range(4):
+            mm(4 + b, A, T.qE[:, 128 * b:128 * b + 128], T.sE[:, 128 * b:128 * b + 128], qL, sL, ["qE%d" % (b // 2)])
+        act(T.LM[:, 0:A], PS(2, 0, A), AF.Copy, [], ["LM"], [2])
+        BK = ["Bh0", "Bh1", "Bh2", "Bh3"]
+
+        def table(t, q):
+            out = T.tab[:, t:16 * TS_:TS_]
+            src = T.Bh[:].indirect(T.offT[:, 2 * t:2 * t + 1])
+            if q == "v":
+                cp(out, src, BK + ["offT%d" % t], ["tab%d" % t])
+            else:
+                act(out, src, AF.Copy, BK + ["offT%d" % t], ["tab%d" % t])
+            if last:
+                act(T.tabE[:, t:16 * TS_:TS_], T.iq[:].indirect(T.offT[:, 2 * t:2 * t + 1]), AF.Copy, ["iq", "offT%d" % t],
+                    ["tabE%d" % t])
+
+        def meal_offsets(t):
+            ts(T.offT[:, 2 * t:2 * t + 1], T.ee[:, t:t + 1], 4.0, rc_, op.mult, op.add, ["ee%d" % t, "fp"], ["offT%d" % t])
+        for t in range(NT):
+            if t == 0:
+                scan(T.pm[:], PS(3, 0, A), T.NEG[:], -H, op.max, op.max, ["NEG"], ["pm"], [3])
+            else:
+                scan(T.pm[:], T.LM[:, 0:A], T.NEG[:], -H, op.max, op.max, ["NEG", "LM"], ["pm"])
+            e = T.ee[:, t:t + 1]
+            act(T.st[:, 1:A + 1], T.pm[:], AF.Sign, ["pm"], ["st", "ee%d" % t], bias=T.pm[:, A - 1:A], scale=-1.0, accum_out=e)
+            if t > 0:
+                meal_offsets(t - 1)
+            for f in gaps[t]:
+                f()
+            if t < 2:
+                for b in (2 * t, 2 * t + 1):
+                    act(T.Bh[:, b:512:4], PS(4 + b, 0, A), AF.Copy, [], ["Bh%d" % b], [4 + b], scale=0.5)
+            else:
+                if t == 2:
+                    table(0, "s")
+                table(t - 1, "s")
+            if r == 0 and 2 <= t < 6:
+                a = C * (t - 2)
+                act(T.Y[:, a:a + C], T.X[:, a:a + C], AF.Copy, XK, YK[4 * ((t - 2) // 2):4 * ((t - 2) // 2) + 4], scale=32.0)
+            if t < NT - 1:
+                n = 16 * (t + 1)
+                ts(T.offE[:, t:t + 1], e, col(5), col(6), op.mult, op.add, ["ee%d" % t, "col5", "col6"], ["offE%d" % t])
+                tt(T.dw[:, 0:n], T.st[:, 0:A + 1].indirect(T.offE[:, 0:t + 1]), T.W[:, 96 - n:96], op.mult,
+                   ["st", "st0", "W"] + ["offE%d" % j for j in range(t + 1)], ["dw"])
+                add("v", lambda e_, n=n: e_.tensor_reduce(T.xn[:, 0:1], T.dw[:, 0:n], AxisListType.X, op.add, negate=True),
+                    ["dw"], ["xn"])
+                ts(T.offD[:, 0:1], T.xn[:, 0:1], e, col(7), op.max, op.min, ["xn", "ee%d" % t, "col7"], ["offD"])
+                cp(T.LM[:].indirect(T.offD[:, 0:1]), T.NEG[:, 0:16], ["offD", "NEG"], ["LM", "LMd"])
+            else:
+                meal_offsets(t)
+                table(t, "v")
+        TK = ["tab%d" % t for t in range(NT)]
+        if last:
+            act(T.olw[:], T.tabE[:].indirect(T.offZ[:]), AF.Copy, ["tabE%d" % t for t in range(NT)] + ["offZ"], ["olw"])
+            act(T.vlo[:], T.olw[:, 0:4 * C:4], AF.Copy, ["olw"], ["vlo"])
+            dma("y", T.ol[:], T.vlo[0:128:16, :], ["vlo"], ["o0"])
+        for h in range(2):
+            tt(T.Z[:, 4 * HC * h:4 * HC * (h + 1)], T.tab[:].indirect(T.offZ[:, 36 * h:36 * h + 36]),
+               T.Xh[:, 4 * HC * h:4 * HC * (h + 1)], op.add, TK + ["offZ", "Xh"], ["Z%d" % h])
+            qz, sz = T.qZ[:, HC * h:HC * (h + 1)], T.sZ[:, HC * h:HC * (h + 1)]
+            quant(qz, sz, T.Z[:, 4 * HC * h:4 * HC * (h + 1)], ["Z%d" % h], ["qZ%d" % h])
+            for b in range(4):
+                mm(4 * (1 - h) + b, HC, T.qW[:, 128 * b:128 * b + 128], T.sW[:, 128 * b:128 * b + 128], qz, sz,
+                   ["qW", "sW", "qZ%d" % h])
+        for h in range(2):
+            for b in range(4):
+                bk = 4 * (1 - h) + b
+                yv = T.Y[:, 4 * HC * h + b:4 * HC * (h + 1):4]
+                tt(yv, PS(bk, 0, HC), yv, op.add, ["Y%d%d" % (h, b)], ["Y%d%d" % (h, b)], [bk])
+                act(T.X[:, 4 * HC * h + b:4 * HC * (h + 1):4], yv, AF.Copy, ["Y%d%d" % (h, b)], ["X%d%d" % (h, b)], scale=0.03125)
+                if (h, b) == (1, 1):
+                    quant_x(0)
+                    if last:
+                        mm(7, HC, T.qV[:], T.sV[:], T.qX[:, 0:HC], T.sX[:, 0:HC], ["qV", "qX0"])
+                    else:
+                        mm(7, HC, u0c, u0s, T.qX[:, 0:HC], T.sX[:, 0:HC], ["qR0", "sR0", "qX0"])
+    dma("y", T.oc[:, 0:4 * HC], T.qX[:, 0:HC].bitcast(dt.uint8), ["qX0"], ["o1"])
+    cp(T.c0[:, 0:HC], PS(7, 0, HC), [], ["c0"], [7])
+    dma("y", T.y[:, 0:HC], T.c0[:, 0:HC], ["c0"], ["o2"])
+    quant_x(1)
+    mm(0, HC, T.qV[:], T.sV[:], T.qX[:, HC:C], T.sX[:, HC:C], ["qV", "qX1"])
+    dma("y", T.oc[:, 4 * HC:4 * C], T.qX[:, HC:C].bitcast(dt.uint8), ["qX1"], ["o3"])
+    for k in range(4):
+        dma("s", T.osc[4 * k:4 * k + 4, :], T.sX[32 * k:32 * k + 4, :], QX, ["o%d" % (k + 5)])
+    cp(T.m01[:, 0:HC], PS(0, 0, HC), [], ["m01"], [0])
+    dma("y", T.y[:, HC:C], T.m01[:, 0:HC], ["m01"], ["o4"])
+    add("y", None, ["o%d" % k for k in range(9)])
+    add("g", None, ext=[("loc", n_loc[0])])
+    emit(g, T, ops)

@@ -13,7 +13,8 @@ TW = [288, 224, 160, 128, 128]
 SLOT = {}
 for _m in range(17, 0, -1):
     SLOT[_m] = ((18 - _m) // 4, (18 - _m) % 4)
-ON_SCALAR = (17, 16, 9)
+ON_SCALAR = (17, 16)
+HOP, TRIP, LOAD = 210, (5000, 3500, 3500), 2800
 
 
 def sb(n, d):
@@ -29,9 +30,9 @@ SCRATCH = {
     "qX": sb(C, X4), "sX": sb(C, U8), "qZ": sb(C, X4), "sZ": sb(C, U8),
     "Gt": sb(512, BF), "qG": sb(128, X4), "sG": sb(128, U8),
     "Et": sb(2048, BF), "qE": sb(512, X4), "sE": sb(512, U8), "ones": sb(512, BF),
-    "ip": sb(8, I32), "fp": sb(8, F32), "col": sb(24, F32), "s16": sb(128, F32), "offQ": sb(18, U16),
+    "ip": sb(8, I32), "fp": sb(8, F32), "col": sb(24, F32), "s16": sb(160, F32), "offQ": sb(18, U16),
     "ofu": sb(48, F32), "offU": sb(48, U16),
-    "Mk": sb(C, F32), "K16": sb(C, F32), "Kd": sb(C, BF), "A16": sb(C, F32), "A16f": sb(3 * C, BF), "A4": sb(C, F32),
+    "Mk": sb(C, F32), "K16": sb(C, F32), "Kd": sb(C, BF), "A16": sb(C, F32), "A16f": sb(C, BF), "A4": sb(C, F32),
     "val": sb(C, F32), "m16": sb(18, F32), "Rc": sb(18, F32), "IC": sb(18, F32),
     "Bm": sb(C, F32), "hold": sb(C, F32), "rel": sb(3 * C, F32), "junk": sb(2448, BF), "rows": sb(18, F32),
     "dseg": sb(C, BF), "R1": sb(18, F32), "ext": sb(C, F32), "offP": sb(18, U16),
@@ -56,7 +57,7 @@ for _r in range(3):
     for _n in ("sM", "sH", "sL"):
         SCRATCH["%s%d" % (_n, _r)] = sb(A, U8)
 
-POOL = {"v": 50, "s": 40, "p": 16, "g": 18, "d": 16}
+POOL = {"v": 55, "s": 40, "p": 16, "g": 16, "d": 16}
 SEMAPHORES = ["loc"] + ["arr%d" % r for r in range(3)] + ["hop%d" % r for r in range(3)]
 for _q in POOL:
     SEMAPHORES += ["%s%d" % (_q, i) for i in range(POOL[_q])]
@@ -106,13 +107,12 @@ def helper_program(g, core, T, topo):
         g.wait_ge(T.sem.loc, sent)
 
 
-def emit(g, T, ops):
-    Q = {"v": g.vector, "s": g.scalar, "p": g.tensor, "g": g, "y": g.sync}
-    last_w, readers, bank = {}, {}, {}
-    known = {q: 0 for q in Q}
-    closure, at_issue, waits, signal = [], [], [], set()
-    for i, (q, fn, rd, wr, bk, ext, dma) in enumerate(ops):
+def depend(ops, order=False):
+    last_w, readers, bank, out = {}, {}, {}, []
+    for i, (q, fn, rd, wr, bk, ext, dma, c) in enumerate(ops):
         deps = set()
+        rd = [k for k in rd if (k[0] == "~") == order]
+        wr = [k for k in wr if (k[0] == "~") == order]
         for k in rd:
             if k in last_w:
                 deps.add(last_w[k])
@@ -120,8 +120,64 @@ def emit(g, T, ops):
             if k in last_w:
                 deps.add(last_w[k])
             deps.update(readers.get(k, []))
-        for b in bk:
-            deps.update(j for j in bank.get(b, []) if ops[j][0] != q)
+        for b in ([] if order else bk):
+            now, before = bank.get(b, ([], []))
+            if now and ops[now[0]][0] != q:
+                now, before = [], now
+            deps.update(before)
+            bank[b] = (now + [i], before)
+        out.append(deps)
+        if fn is not None:
+            for k in rd:
+                readers.setdefault(k, []).append(i)
+        for k in wr:
+            last_w[k] = i
+            readers[k] = []
+    return out
+
+
+def arrange(ops):
+    n = len(ops)
+    pred = [[(j, (LOAD if ops[j][6] else 0) + HOP) for j in d] for d in depend(ops)]
+    for i, d in enumerate(depend(ops, True)):
+        pred[i] += [(j, 0) for j in d]
+    prev, sends = {}, {}
+    for i, (q, fn, rd, wr, bk, ext, dma, c) in enumerate(ops):
+        keys = [q] if q in "gy" else [("p", b) for b in bk] if q == "p" else []
+        for k in keys:
+            if k in prev:
+                pred[i].append((prev[k], 0))
+            prev[k] = i
+        for k in rd:
+            if q == "g" and k.startswith("qM"):
+                sends.setdefault("arr" + k[2:], i)
+        for name, val in ext:
+            if name in sends:
+                pred[i].append((sends[name], TRIP[int(name[3:])]))
+    tail = [float(ops[i][7]) + (LOAD if ops[i][6] else 0) for i in range(n)]
+    for i in range(n - 1, -1, -1):
+        for j, lat in pred[i]:
+            tail[j] = max(tail[j], ops[j][7] + lat + tail[i])
+    busy = {q: [] for q in "vspgy"}
+    start = [0.0] * n
+    for i in sorted(range(n), key=lambda i: (-tail[i], i)):
+        t = max([start[j] + ops[j][7] + lat for j, lat in pred[i]] + [0.0])
+        for a, b in busy[ops[i][0]]:
+            if t + ops[i][7] <= a:
+                break
+            t = max(t, b)
+        start[i] = t
+        busy[ops[i][0]].append((t, t + ops[i][7]))
+        busy[ops[i][0]].sort()
+    return [ops[i] for i in sorted(range(n), key=lambda i: (start[i], i))]
+
+
+def emit(g, T, ops):
+    Q = {"v": g.vector, "s": g.scalar, "p": g.tensor, "g": g, "y": g.sync}
+    known = {q: 0 for q in Q}
+    closure, at_issue, waits, signal = [], [], [], set()
+    for i, deps in enumerate(depend(ops)):
+        q = ops[i][0]
         need = [j for j in deps if not known[q] >> j & 1]
         need = [j for j in need if not any(j2 != j and closure[j2] >> j & 1 for j2 in need)]
         for j in need:
@@ -130,17 +186,9 @@ def emit(g, T, ops):
         waits.append(sorted(need))
         at_issue.append(known[q])
         closure.append(known[q] | 1 << i)
-        if fn is not None:
-            for k in rd:
-                readers.setdefault(k, []).append(i)
-        for k in wr:
-            last_w[k] = i
-            readers[k] = []
-        for b in bk:
-            bank[b] = [j for j in bank.get(b, []) if ops[j][0] == q] + [i]
     user = {q: [] for q in POOL}
     count, mark = {}, {}
-    for i, (q, fn, rd, wr, bk, ext, dma) in enumerate(ops):
+    for i, (q, fn, rd, wr, bk, ext, dma, c) in enumerate(ops):
         for j in waits[i]:
             Q[q].wait_ge(T.sem[mark[j][0]], mark[j][1])
         for name, val in ext:
@@ -173,44 +221,50 @@ def rank_program(g, core, T, topo):
     AF = ActivationFunctionType
     ops = []
 
-    def add(q, fn, rd=(), wr=(), bk=(), ext=(), dma=False):
-        ops.append((q, fn, list(rd), list(wr), list(bk), list(ext), dma))
+    def add(q, fn, rd=(), wr=(), bk=(), ext=(), dma=False, c=64):
+        ops.append((q, fn, list(rd), list(wr), list(bk), list(ext), dma, max(c, 64)))
 
-    def ts(out, in0, s1, s2, o0, o1, rd, wr, bk=()):
+    def ts(out, in0, s1, s2, o0, o1, rd, wr, bk=(), c=64):
         if o1 is None:
-            add("v", lambda e: e.tensor_scalar(out, in0, s1, None, o0), rd, wr, bk)
+            add("v", lambda e: e.tensor_scalar(out, in0, s1, None, o0), rd, wr, bk, c=c)
         else:
-            add("v", lambda e: e.tensor_scalar(out, in0, s1, s2, o0, o1), rd, wr, bk)
+            add("v", lambda e: e.tensor_scalar(out, in0, s1, s2, o0, o1), rd, wr, bk, c=c)
 
-    def tt(out, a, b, o, rd, wr, bk=()):
-        add("v", lambda e: e.tensor_tensor(out, a, b, o), rd, wr, bk)
+    def tt(out, a, b, o, rd, wr, bk=(), c=64):
+        add("v", lambda e: e.tensor_tensor(out, a, b, o), rd, wr, bk, c=c)
 
-    def cp(out, a, rd, wr, bk=()):
-        add("v", lambda e: e.tensor_copy(out, a), rd, wr, bk)
+    def cp(out, a, rd, wr, bk=(), c=64):
+        add("v", lambda e: e.tensor_copy(out, a), rd, wr, bk, c=c)
 
-    def ms(out, c, wr):
-        add("v", lambda e: e.memset(out, c), (), wr)
+    def ms(out, v, wr, c=64):
+        add("v", lambda e: e.memset(out, v), (), wr, c=c)
 
-    def scan(out, d0, d1, init, o0, o1, rd, wr, bk=()):
-        add("v", lambda e: e.tensor_tensor_scan(out, d0, d1, init, o0, o1), rd, wr, bk)
+    def scan(out, d0, d1, init, o0, o1, rd, wr, bk=(), c=64):
+        add("v", lambda e: e.tensor_tensor_scan(out, d0, d1, init, o0, o1), rd, wr, bk, c=c)
 
-    def quant(qc, sc, a, rd, wr):
-        add("v", lambda e: e.quantize_mx(qc, sc, a), rd, wr)
+    def quant(qc, sc, a, n, rd, wr):
+        add("v", lambda e: e.quantize_mx(qc, sc, a), rd, wr, c=15 + 1.06 * n)
 
-    def act(out, a, f, rd, wr, bk=(), **kw):
-        add("s", lambda e: e.activation(out, a, f, **kw), rd, wr, bk)
+    def act(out, a, f, rd, wr, bk=(), c=64, **kw):
+        add("s", lambda e: e.activation(out, a, f, **kw), rd, wr, bk, c=c + (24 if "accum_out" in kw else 0))
 
     def mm(b, n, lc, ls, rc, rs, rd, start=True, stop=True, ext=()):
-        add("p", lambda e: e.matmul_mx(T.ps[:, 512 * b:512 * b + n], lc, ls, rc, rs, start, stop), rd, (), [b], ext)
+        add("p", lambda e: e.matmul_mx(T.ps[:, 512 * b:512 * b + n], lc, ls, rc, rs, start, stop), rd, (), [b], ext, c=1.3 * (n + 16))
 
     def iota(out, pat, base, cm, wr, small=True):
+        n = 1
+        for s, k in pat:
+            n *= k
         if small:
-            add("g", lambda e: e.iota(out, pat, base, cm, allow_small_or_imprecise_dtypes=True), (), wr)
+            add("g", lambda e: e.iota(out, pat, base, cm, allow_small_or_imprecise_dtypes=True), (), wr, c=157 + 2 * n)
         else:
-            add("g", lambda e: e.iota(out, pat, base, cm), (), wr)
+            add("g", lambda e: e.iota(out, pat, base, cm), (), wr, c=157 + 2 * n)
 
     def dma(q, out, a, rd, wr):
         add(q, lambda e: e.dma_start(out, a), rd, wr, dma=True)
+
+    def gat(n):
+        return 60 + 1.5 * n
 
     def PS(b, a, n):
         return T.ps[:, 512 * b + a:512 * b + n]
@@ -221,9 +275,9 @@ def rank_program(g, core, T, topo):
     def s16(i):
         return T.s16[:, 16 * i:16 * i + 16]
 
-    def quant_x(h):
-        quant(T.qX[:, HC * h:HC * (h + 1)], T.sX[:, HC * h:HC * (h + 1)], T.X[:, 4 * HC * h:4 * HC * (h + 1)],
-              XK[4 * h:4 * h + 4], ["qX%d" % h])
+    def quant_x(h, more=()):
+        quant(T.qX[:, HC * h:HC * (h + 1)], T.sX[:, HC * h:HC * (h + 1)], T.X[:, 4 * HC * h:4 * HC * (h + 1)], HC,
+              XK[4 * h:4 * h + 4], ["qX%d" % h] + list(more))
 
     XK = ["X%d%d" % (h, b) for h in range(2) for b in range(4)]
     YK = ["Y%d%d" % (h, b) for h in range(2) for b in range(4)]
@@ -234,23 +288,24 @@ def rank_program(g, core, T, topo):
     dma("y", T.sW[:], T.ws[:], (), ["sW"])
     dma("y", T.vb[:], T.v[:], (), ["vb"])
     iota(T.ip[:, 0:2], [[15, 2]], 0, 1, ["ip0"], small=False)
-    iota(s16(0), [[1, 16]], 0, 0, ["s0"])
     iota(T.ofu[:, 0:8], [[16, 8]], 0, 0, ["ofu0"])
+    iota(s16(0), [[1, 16]], 0, 0, ["s0"])
     iota(T.m16[:], [[16, 18]], 0, 0, ["m16"])
     iota(s16(1), [[0, 4], [1, 4]], 0, 0, ["s1"])
+    iota(T.ofu[:, 8:40], [[1, 4], [16, 8]], 4, 0, ["ofu1"])
+    iota(T.ofu[:, 40:48], [[16, 8]], 8, 0, ["ofu2"])
     for t, a in ((2, 112), (3, 48), (0, 240), (1, 176), (4, 0)):
         iota(T["T%d" % t][:, 4 * a:], [[0, 4 * (TW[t] - a)]], 0, 0, ["T%d%d" % (t, e) for e in range(4)])
     iota(T.val[:], [[4, C]], 0, 0, ["val"])
-    iota(T.ofu[:, 8:40], [[1, 4], [16, 8]], 4, 0, ["ofu1"])
-    iota(T.ofu[:, 40:48], [[16, 8]], 8, 0, ["ofu2"])
     iota(T.kp[:], [[0, 6], [1, 4], [0, 4]], 0, 0, ["kp"])
     iota(T.Lw[:, 4 * C:5 * C], [[1, C]], 1 + 6 * CK, 0, ["L4"])
-    ms(T.K16[:], H, ["K16"])
+    iota(T.Lw[:, 0:C], [[0, C]], 0, 0, ["L0"])
+    ms(T.K16[:], H, ["K16"], c=C)
     ts(T.ip[:, 2:4], T.ip[:, 0:2], 15, None, op.bitwise_and, None, ["ip0"], ["ip2"])
     ts(T.ip[:, 4:5], T.ip[:, 0:1], 2, 3, op.logical_shift_right, op.bitwise_and, ["ip0"], ["ip4"])
     ts(T.ip[:, 5:6], T.ip[:, 0:1], 3, None, op.bitwise_and, None, ["ip0"], ["ip5"])
     ts(T.ip[:, 6:7], T.ip[:, 0:1], 112, None, op.bitwise_and, None, ["ip0"], ["ip6"])
-    ms(T.ones[:], 1.0, ["ones"])
+    ms(T.ones[:], 1.0, ["ones"], c=256)
     cp(T.fp[:, 0:5], T.ip[:, 2:7], ["ip2", "ip4", "ip5", "ip6"], ["fp"])
     qc, qm, kc, rc_, gc_ = [T.fp[:, i:i + 1] for i in range(5)]
     ms(T.K16[:, 0:C:16], -H, ["K16"])
@@ -261,79 +316,75 @@ def rank_program(g, core, T, topo):
     cp(T.offU[:, 0:8], T.ofu[:, 0:8], ["ofu0"], ["offU0"])
     ts(s16(6), s16(0), qc, 1024.0, op.is_equal, op.mult, ["s0", "fp"], ["s6"])
     ts(s16(7), s16(0), qm, -4096.0, op.is_equal, op.mult, ["s0", "fp"], ["s7"])
-    ms(T.Kd[:], 1.0, ["Kd"])
+    ms(T.Kd[:], 1.0, ["Kd"], c=HC)
     tt(s16(3), s16(6), s16(7), op.add, ["s6", "s7"], ["s3"])
     ts(col(3), kc, 1.0, None, op.add, None, ["fp"], ["col3"])
     ts(col(4), kc, 2.5, 4096.0, op.is_lt, op.mult, ["fp"], ["col4"])
     ts(col(0), qc, -1.0, 15.0 - 1024.0, op.mult, op.add, ["fp"], ["col0"])
-    ts(s16(6), s16(1), kc, -16384.0, op.is_equal, op.mult, ["s1", "fp"], ["s6"])
-    ts(s16(7), s16(1), col(3), 4096.0, op.is_equal, op.mult, ["s1", "col3"], ["s7"])
+    ts(s16(8), s16(1), kc, -16384.0, op.is_equal, op.mult, ["s1", "fp"], ["s8"])
+    ts(s16(9), s16(1), col(3), 4096.0, op.is_equal, op.mult, ["s1", "col3"], ["s9"])
     ms(T.Kd[:, 0:C:16], 0.0, ["Kd"])
     ms(T.rows[:, 0:1], 0.0, ["rows0"])
-    tt(s16(4), s16(6), s16(7), op.add, ["s6", "s7"], ["s4"])
+    tt(s16(4), s16(8), s16(9), op.add, ["s8", "s9"], ["s4"])
     ts(T.Rc[:], T.m16[:], col(0), T.s16[:, 63:64], op.add, op.add, ["m16", "col0", "s3"], ["Rc"])
     ts(col(1), T.s16[:, 63:64], 0.0, -1.0, op.min, op.mult, ["s3"], ["col1"])
     ts(col(14), col(4), rc_, None, op.subtract, None, ["col4", "fp"], ["col14"])
-    act(T.Mk[:], s16(2).indirect(T.offQ[:]), AF.Copy, ["s2", "offQ"], ["Mk"])
+    act(T.Mk[:], s16(2).indirect(T.offQ[:]), AF.Copy, ["s2", "offQ"], ["Mk"], c=gat(C))
     for j in range(8):
         act(T.Gt[:, 64 * j:64 * j + 64], T.ones[:, 0:64], AF.Copy, ["ones", "gcol"], ["Gt%d" % j], scale=col(16 + j))
-    act(T.A16[:], s16(3).indirect(T.offQ[:]), AF.Copy, ["s3", "offQ"], ["A16"])
-    quant(T.qU[:], T.sU[:], T.ub[:], ["ub"], ["qU"])
-    add("v", lambda e: e.tensor_copy(T.qR[:, 0:128].bitcast(dt.uint32), T.qU[:].bitcast(dt.uint32).indirect(T.offU[:, 0:8])),
-        ["qU", "offU0"], ["qR0"])
-    act(T.sR[:, 0:128], T.sU[:].indirect(T.offU[:, 0:8]), AF.Copy, ["qU", "offU0"], ["sR0"])
-    act(T.A4[:], s16(4).indirect(T.offQ[:]), AF.Copy, ["s4", "offQ"], ["A4"])
-    quant_x(0)
+    act(T.A16[:], s16(3).indirect(T.offQ[:]), AF.Copy, ["s3", "offQ"], ["A16"], c=gat(C))
+    act(T.A4[:], s16(4).indirect(T.offQ[:]), AF.Copy, ["s4", "offQ"], ["A4"], c=gat(C))
+    act(T.A16f[:], s16(3).indirect(T.offQ[:]), AF.Copy, ["s3", "offQ"], ["A16f"], c=gat(C), scale=1.0 / 512)
+    quant(T.qG[:], T.sG[:], T.Gt[:], 128, ["Gt%d" % j for j in range(8)], ["qG"])
+    ts(col(7), qc, 128.0, None, op.add, None, ["fp"], ["col7"])
+    ts(col(9), col(4), 4.0, None, op.add, None, ["col4"], ["col9"])
+    ts(col(10), rc_, float(TS_), -1.0, op.mult, op.add, ["fp"], ["col10"])
+    ts(col(11), col(1), -24.0 * C / 4096, 9.0 * C, op.mult, op.add, ["col1"], ["col11"])
+    ts(col(13), kc, float(C), C - 1.0, op.mult, op.add, ["fp"], ["col13"])
+    cp(T.offU[:, 8:40], T.ofu[:, 8:40], ["ofu1"], ["offU1"])
+    ts(T.offU[:, 40:48], T.ofu[:, 40:48], kc, None, op.add, None, ["ofu2", "fp"], ["offU5"])
+    ms(T.sg[:], 0.0, ["sg"], c=96)
+    ms(T.sg[:, 0:96:4], 512.0, ["sg"])
+    ms(T.NEG[:], -H, ["NEG"], c=128)
+    ms(T.LM[:, 128:144], 0.0, ["LMd"])
+    ms(T.st[:, 0:1], 1.0, ["st0"])
+    ts(T.w1[:, 0:16], T.kp[:, 80:96], kc, None, op.is_ge, None, ["kp", "fp"], ["w1"])
+    ts(T.k2[:], T.kp[:, 80:96], kc, -BIG / 512, op.is_lt, op.mult, ["kp", "fp"], ["k2"])
+    ms(T.sg[:, 1:96:4], -512.0, ["sg"])
+    ts(col(5), rc_, 1.5, None, op.is_lt, None, ["fp"], ["col5"])
+    ts(col(6), rc_, 1.0, None, op.is_equal, None, ["fp"], ["col6"])
+    ts(col(8), rc_, 0.0, BIG - 95.5 * 512, op.is_equal, op.mult, ["fp"], ["col8"])
+    tt(T.k2[:], T.k2[:], T.sg[:, 80:96], op.mult, ["k2", "sg"], ["k2"])
+    ts(T.offW[:], T.m16[:, 0:6], 0.0, col(13), op.mult, op.add, ["m16", "col13"], ["offW"])
+    ts(T.IC[:], T.m16[:], col(11), qc, op.add, op.add, ["m16", "col11", "fp"], ["IC"])
+    tt(T.sg[:, 80:96], T.sg[:, 80:96], T.w1[:, 0:16], op.mult, ["w1", "sg"], ["sg"])
+    ts(T.k2[:, 2:3], col(8), -BIG, None, op.add, None, ["col8", "k2"], ["k2"])
+    tt(T.ex[:], T.kp[:], T.sg[:], op.mult, ["kp", "sg"], ["ex"], c=192)
+    ts(col(12), col(10), col(4), None, op.subtract, None, ["col10", "col4"], ["col12"])
+    ts(T.ex[:], T.ex[:], -float(CK), None, op.mult, None, ["ex"], ["ex"], c=96)
+    tt(T.ex[:, 80:96], T.ex[:, 80:96], T.k2[:], op.add, ["ex", "k2"], ["ex"])
+    quant(T.qU[:], T.sU[:], T.ub[:], 128, ["ub"], ["qU"])
+    quant(T.qV[:], T.sV[:], T.vb[:], 128, ["vb"], ["qV"])
+
+    def pick(s):
+        key = "offU%d" % (s if s in (0, 5) else 1)
+        off = T.offU[:, 8 * s:8 * s + 8]
+        add("v", lambda e: e.tensor_copy(T.qR[:, 128 * s:128 * s + 128].bitcast(dt.uint32), T.qU[:].bitcast(dt.uint32).indirect(off)),
+            ["qU", key], ["qR%d" % s], c=gat(128))
+        act(T.sR[:, 128 * s:128 * s + 128], T.sU[:].indirect(off), AF.Copy, ["qU", key], ["sR%d" % s], c=gat(128))
+    for s in range(6):
+        pick(s)
+
+    def ur(s):
+        return T.qR[:, 128 * s:128 * s + 128], T.sR[:, 128 * s:128 * s + 128]
 
     def e_tile(b):
         add("g", lambda e: e.affine_select(T.Et[:, 512 * b:512 * b + 512], T.ones[:], [[1, 128], [256, 4]], op.is_equal, 0.0,
-                                           -256 * b, -1), ["ones"], ["Et%d" % b])
+                                           -256 * b, -1), ["ones"], ["Et%d" % b], c=1230)
+        quant(T.qE[:, 128 * b:128 * b + 128], T.sE[:, 128 * b:128 * b + 128], T.Et[:, 512 * b:512 * b + 512], 128,
+              ["Et%d" % b], ["qE%d" % b])
     e_tile(0)
     e_tile(1)
-
-    def late_consts():
-        cp(T.offU[:, 8:40], T.ofu[:, 8:40], ["ofu1"], ["offU1"])
-        ts(T.offU[:, 40:48], T.ofu[:, 40:48], kc, None, op.add, None, ["ofu2", "fp"], ["offU2"])
-        ms(T.sg[:], 0.0, ["sg"])
-        add("v", lambda e: e.tensor_copy(T.qR[:, 128:768].bitcast(dt.uint32), T.qU[:].bitcast(dt.uint32).indirect(T.offU[:, 8:48])),
-            ["qU", "offU1", "offU2"], ["qR1"])
-        act(T.sR[:, 128:768], T.sU[:].indirect(T.offU[:, 8:48]), AF.Copy, ["qU", "offU1", "offU2"], ["sR1"])
-        class_scores()
-        act(T.c0[:], PS(4, 0, C), AF.Copy, [], ["c0"], [4])
-        ms(T.sg[:, 0:96:4], 512.0, ["sg"])
-        ms(T.NEG[:], -H, ["NEG"])
-        ms(T.LM[:, 128:144], 0.0, ["LMd"])
-        ms(T.st[:, 0:1], 1.0, ["st0"])
-        ts(T.w1[:, 0:16], T.kp[:, 80:96], kc, None, op.is_ge, None, ["kp", "fp"], ["w1"])
-        ts(T.k2[:], T.kp[:, 80:96], kc, -BIG / 512, op.is_lt, op.mult, ["kp", "fp"], ["k2"])
-        ms(T.sg[:, 1:96:4], -512.0, ["sg"])
-        ts(col(5), rc_, 1.5, None, op.is_lt, None, ["fp"], ["col5"])
-        ts(col(6), rc_, 1.0, None, op.is_equal, None, ["fp"], ["col6"])
-        ts(col(8), rc_, 0.0, BIG - 95.5 * 512, op.is_equal, op.mult, ["fp"], ["col8"])
-        tt(T.k2[:], T.k2[:], T.sg[:, 80:96], op.mult, ["k2", "sg"], ["k2"])
-        ts(T.offW[:], T.m16[:, 0:6], 0.0, col(13), op.mult, op.add, ["m16", "col13"], ["offW"])
-        ts(T.IC[:], T.m16[:], col(11), qc, op.add, op.add, ["m16", "col11", "fp"], ["IC"])
-        tt(T.sg[:, 80:96], T.sg[:, 80:96], T.w1[:, 0:16], op.mult, ["w1", "sg"], ["sg"])
-        ts(T.k2[:, 2:3], col(8), -BIG, None, op.add, None, ["col8", "k2"], ["k2"])
-        tt(T.ex[:], T.kp[:], T.sg[:], op.mult, ["kp", "sg"], ["ex"])
-        ts(col(12), col(10), col(4), None, op.subtract, None, ["col10", "col4"], ["col12"])
-        ts(T.ex[:], T.ex[:], -float(CK), None, op.mult, None, ["ex"], ["ex"])
-        tt(T.ex[:, 80:96], T.ex[:, 80:96], T.k2[:], op.add, ["ex", "k2"], ["ex"])
-        act(T.A16f[:, 0:C], s16(3).indirect(T.offQ[:]), AF.Copy, ["s3", "offQ"], ["A16f0"], scale=1.0 / 512)
-        for j in (1, 2):
-            act(T.A16f[:, C * j:C * j + C], T.A16f[:, 0:C], AF.Copy, ["A16f0"], ["A16f%d" % j])
-
-    def late_columns():
-        ts(col(7), qc, 128.0, None, op.add, None, ["fp"], ["col7"])
-        ts(col(9), col(4), 4.0, None, op.add, None, ["col4"], ["col9"])
-        ts(col(10), rc_, float(TS_), -1.0, op.mult, op.add, ["fp"], ["col10"])
-        ts(col(11), col(1), -24.0 * C / 4096, 9.0 * C, op.mult, op.add, ["col1"], ["col11"])
-        ts(col(13), kc, float(C), C - 1.0, op.mult, op.add, ["fp"], ["col13"])
-
-    def class_scores():
-        for k in range(4):
-            mm(4 + k, C, T.qR[:, 128 * (k + 1):128 * (k + 2)], T.sR[:, 128 * (k + 1):128 * (k + 2)], T.qX[:], T.sX[:],
-               ["qR1", "sR1"] + QX)
 
     n_loc = [0]
 
@@ -358,8 +409,11 @@ def rank_program(g, core, T, topo):
         return sum(len(topo.engines(h, core)) for h in helpers(topo, dst, core))
 
     QX = ["qX0", "qX1"]
-    u0c, u0s = T.qR[:, 0:128], T.sR[:, 0:128]
-    mm(7, HC, u0c, u0s, T.qX[:, 0:HC], T.sX[:, 0:HC], ["qR0", "sR0", "qX0"])
+    U0 = ["qR0", "sR0"]
+    u0c, u0s = ur(0)
+    quant_x(0)
+    quant_x(1)
+    mm(7, HC, u0c, u0s, T.qX[:, 0:HC], T.sX[:, 0:HC], U0 + ["qX0"])
     for r, step in enumerate(STEPS):
         last = r == len(STEPS) - 1
         def slot(m, w):
@@ -368,197 +422,163 @@ def rank_program(g, core, T, topo):
 
         def compare(m, b):
             view, key = slot(m, 16 * m)
-            ts(view, PS(b, 0, 16 * m), T.hold[:, 16 * m + 15:16 * m + 16], None, op.is_lt, None, ["hold%d" % (m // 9)], [key], [b])
+            ts(view, PS(b, 0, 16 * m), T.hold[:, 16 * m + 15:16 * m + 16], None, op.is_lt, None, ["hold%d" % (m // 9)], [key], [b],
+               c=16 * m)
             j0 = 8 * m * (m - 1)
-            act(T.junk[:, j0:j0 + 16 * m], view, AF.Copy, [key], ["junk%d" % m, "rows%d" % m], accum_out=T.rows[:, m:m + 1])
-
-        def colsum(t):
-            quant(T["qT%d" % t][:], T["sT%d" % t][:], T["T%d" % t][:], ["T%d%d" % (t, e) for e in range(4)], ["qT%d" % t])
-            mm(2, TW[t], T.qG[:], T.sG[:], T["qT%d" % t][:], T["sT%d" % t][:], ["qG", "qT%d" % t], t == 0, t == 4)
-        if r == 0:
-            quant_x(1)
-        tt(T.Bm[:, 0:HC], PS(7, 0, HC), T.Mk[:, 0:HC], op.min, ["Mk"], ["Bm0"], [7])
-        if r > 0:
-            quant_x(1)
+            act(T.junk[:, j0:j0 + 16 * m], view, AF.Copy, [key], ["junk%d" % m, "rows%d" % m], c=max(64, 16 * m),
+                accum_out=T.rows[:, m:m + 1])
+        tt(T.Bm[:, 0:HC], PS(7, 0, HC), T.Mk[:, 0:HC], op.min, ["Mk"], ["Bm0"], [7], c=HC)
         for b in (0, 1):
-            mm(b, C, u0c, u0s, T.qX[:], T.sX[:], ["qR0", "sR0"] + QX)
-        scan(T.hold[:, 0:HC], T.K16[:, 0:HC], T.Bm[:, 0:HC], -H, op.min, op.max, ["K16", "Bm0"], ["hold0"])
+            mm(b, C, u0c, u0s, T.qX[:], T.sX[:], U0 + QX)
+        scan(T.hold[:, 0:HC], T.K16[:, 0:HC], T.Bm[:, 0:HC], -H, op.min, op.max, ["K16", "Bm0"], ["hold0"], c=HC)
         for m in (8, 7, 6, 5):
             compare(m, 7)
-        if r > 0:
-            class_scores()
-        tt(T.Bm[:, HC:C], PS(0, HC, C), T.Mk[:, HC:C], op.min, ["Mk"], ["Bm1"], [0])
-        compare(4, 0)
-        scan(T.hold[:, HC:C], T.K16[:, HC:C], T.Bm[:, HC:C], -H, op.min, op.max, ["K16", "Bm1"], ["hold1"])
+        for k in range(4):
+            mm(4 + k, C, ur(k + 1)[0], ur(k + 1)[1], T.qX[:], T.sX[:], ["qR%d" % (k + 1), "sR%d" % (k + 1)] + QX)
+        tt(T.Bm[:, HC:C], PS(0, HC, C), T.Mk[:, HC:C], op.min, ["Mk"], ["Bm1"], [0], c=HC)
+        scan(T.hold[:, HC:C], T.K16[:, HC:C], T.Bm[:, HC:C], -H, op.min, op.max, ["K16", "Bm1"], ["hold1"], c=HC)
         for n, m in enumerate(ON_SCALAR):
-            act(T.rel[:, C * n:C * n + 16 * m], PS(1, 0, 16 * m), AF.Relu, ["hold1"], ["rel%d" % n], [1],
+            act(T.rel[:, C * n:C * n + 16 * m], PS(1, 0, 16 * m), AF.Relu, ["hold1"], ["rel%d" % n], [1], c=16 * m,
                 bias=T.hold[:, 16 * m + 15:16 * m + 16], scale=-1.0)
-        for n, m in enumerate(ON_SCALAR):
             view, key = slot(m, 16 * m)
-            act(view, T.rel[:, C * n:C * n + 16 * m], AF.Sign, ["rel%d" % n], [key, "rows%d" % m], accum_out=T.rows[:, m:m + 1])
-        if r == 0:
-            quant(T.qG[:], T.sG[:], T.Gt[:], ["Gt%d" % j for j in range(8)], ["qG"])
-        compare(3, 0)
-        for m in (15, 14, 13, 12, 11):
-            compare(m, 0)
-        tt(T.T0[:, 0:4 * C:4], PS(0, 0, C), T.hold[:], op.is_le, ["hold0", "hold1"], ["T00"], [0])
-        compare(10, 0)
-        scan(T.dseg[:], T.Kd[:], T.T0[:, 0:4 * C:4], 0.0, op.mult, op.add, ["Kd", "T00"], ["dseg"])
-        compare(2, 0)
-        compare(1, 0)
-        colsum(0)
-        colsum(1)
+            act(view, T.rel[:, C * n:C * n + 16 * m], AF.Sign, ["rel%d" % n], [key, "rows%d" % m], c=16 * m,
+                accum_out=T.rows[:, m:m + 1])
+        for m in range(17, 0, -1):
+            if m not in ON_SCALAR + (8, 7, 6, 5):
+                compare(m, 0)
+        tt(T.T0[:, 0:4 * C:4], PS(0, 0, C), T.hold[:], op.is_le, ["hold0", "hold1"], ["T00"], [0], c=C)
+        scan(T.dseg[:], T.Kd[:], T.T0[:, 0:4 * C:4], 0.0, op.mult, op.add, ["Kd", "T00"], ["dseg"], c=HC)
+        for t in range(5):
+            quant(T["qT%d" % t][:], T["sT%d" % t][:], T["T%d" % t][:], TW[t], ["T%d%d" % (t, e) for e in range(4)], ["qT%d" % t])
+            mm(2, TW[t], T.qG[:], T.sG[:], T["qT%d" % t][:], T["sT%d" % t][:], ["qG", "qT%d" % t], t == 0, t == 4)
         tt(T.R1[:], T.Rc[:], T.dseg[:, 15:C:16], op.subtract, ["Rc", "dseg"], ["R1"])
-        colsum(2)
-        colsum(3)
-        colsum(4)
-        if r > 0:
-            cp(T.c0[:], PS(4, 0, C), [], ["c0"], [4])
-        else:
-            late_columns()
         tt(T.A16[:, 15:C:16], T.R1[:], T.rows[:], op.subtract, ["R1"] + ["rows%d" % m for m in range(18)], ["A16"])
-        scan(T.ext[:], PS(2, 0, C), T.A16[:], -4096.0, op.max, op.add, ["A16"], ["ext"], [2])
+        scan(T.ext[:], PS(2, 0, C), T.A16[:], -4096.0, op.max, op.add, ["A16"], ["ext"], [2], c=C)
         ts(T.offP[:], T.ext[:, 15:C:16], col(1), None, op.add, None, ["ext", "col1"], ["offP"])
-        cp(T.win[:].indirect(T.offP[:]), T.val[:], ["offP", "val"], ["win"])
-        scan(T.ext[:, 0:A], T.A4[:, 0:A], T.win[:, 0:A], 0.0, op.add, op.max, ["A4", "win"], ["ext"])
+        cp(T.win[:].indirect(T.offP[:]), T.val[:], ["offP", "val"], ["win"], c=60 + 3.5 * C)
+        scan(T.ext[:, 0:A], T.A4[:, 0:A], T.win[:, 0:A], 0.0, op.add, op.max, ["A4", "win"], ["ext"], c=A)
         ts(T.offM[:], T.ext[:, 3:A:4], col(14), None, op.subtract, None, ["ext", "col14"], ["offM"])
-        cp(T.M[:, 0:256], T.X[:].indirect(T.offM[:, 0:16]), XK + ["offM"], ["M0"])
-        act(T.M[:, 256:512], T.X[:].indirect(T.offM[:, 16:32]), AF.Copy, XK + ["offM"], ["M1"])
-        quant(T["qM%d" % r][:], T["sM%d" % r][:], T.M[:], ["M0", "M1"], ["qM%d" % r])
-        n_arr = send(r, step)
+        cp(T.M[:, 0:256], T.X[:].indirect(T.offM[:, 0:16]), XK + ["offM"], ["M0"], c=gat(256))
+        act(T.M[:, 256:512], T.X[:].indirect(T.offM[:, 16:32]), AF.Copy, XK + ["offM"], ["M1"], c=gat(256))
+        quant(T["qM%d" % r][:], T["sM%d" % r][:], T.M[:], A, ["M0", "M1"], ["qM%d" % r])
+        arr = [("arr%d" % r, send(r, step))]
         if r == 0:
-            iota(T.Lw[:, 0:C], [[0, C]], 0, 0, ["L0"])
             e_tile(2)
             e_tile(3)
             iota(T.iq[:], [[1, 128], [0, 4]], 0, 0, ["iq"])
-            late_consts()
-        tt(T.m01[:], PS(5, 0, C), T.c0[:], op.max, ["c0"], ["m01"], [5])
-        tt(T.m012[:], PS(6, 0, C), T.m01[:], op.max, ["m01"], ["m012"], [6])
-        tt(T.mx[:], PS(7, 0, C), T.m012[:], op.max, ["m012"], ["mx"], [7])
-        tt(T.gf[:, 2 * C:3 * C], PS(7, 0, C), T.m012[:], op.is_le, ["m012"], ["gf2"], [7])
-        tt(T.gf[:, 0:C], PS(4, 0, C), T.mx[:], op.is_ge, ["mx"], ["gf0"], [4])
-        tt(T.gf[:, C:2 * C], T.m01[:], T.mx[:], op.is_ge, ["m01", "mx"], ["gf1"])
-        act(T.Xh[:], T.X[:], AF.Copy, XK, ["Xh"], scale=0.5)
+            for j in range(4):
+                act(T.Y[:, C * j:C * j + C], T.X[:, C * j:C * j + C], AF.Copy, XK + ["offM"], YK[4 * (j // 2):4 * (j // 2) + 4], c=C,
+                    scale=32.0)
+        for j in range(4):
+            act(T.Xh[:, C * j:C * j + C], T.X[:, C * j:C * j + C], AF.Copy, XK + ["offM"], ["Xh%d" % j], c=C, scale=0.5)
+        act(T.c0[:], PS(4, 0, C), AF.Copy, [], ["c0"], [4], c=C)
+        for h in range(2):
+            a, b = HC * h, HC * (h + 1)
+            tt(T.m01[:, a:b], PS(5, a, b), T.c0[:, a:b], op.max, ["c0"], ["m01%d" % h], [5], c=HC)
+            tt(T.m012[:, a:b], PS(6, a, b), T.m01[:, a:b], op.max, ["m01%d" % h], ["m012%d" % h], [6], c=HC)
+            tt(T.mx[:, a:b], PS(7, a, b), T.m012[:, a:b], op.max, ["m012%d" % h], ["mx%d" % h], [7], c=HC)
+        tt(T.gf[:, 2 * C:3 * C], PS(7, 0, C), T.m012[:], op.is_le, ["m0120", "m0121"], ["gf2"], [7], c=C)
+        tt(T.gf[:, 0:C], PS(4, 0, C), T.mx[:], op.is_ge, ["mx0", "mx1"], ["gf0"], [4], c=C)
+        tt(T.gf[:, C:2 * C], T.m01[:], T.mx[:], op.is_ge, ["m010", "m011", "mx0", "mx1"], ["gf1"], c=2 * C)
         for j, c in ((2, 3 * CK), (0, 0), (1, CK)):
             scan(T.Lw[:, C * (j + 1):C * (j + 2)], T.gf[:, C * j:C * j + C], T.Lw[:, 0:C], float(c), op.add, op.add,
-                 ["gf%d" % j, "L0"], ["L%d" % (j + 1)])
+                 ["gf%d" % j, "L0"], ["L%d" % (j + 1)], c=C)
+            scan(T.gx[:, C * j:C * j + C], T.gf[:, C * j:C * j + C], T.A16f[:], -8.0, op.max, op.add, ["A16f", "gf%d" % j],
+                 ["gx%d" % j], c=HC)
         LK = ["L0", "L1", "L2", "L3", "L4"]
-        act(T.wlo[:], T.Lw[:, 0:4 * C].indirect(T.offW[:]), AF.Copy, LK + ["offW"], ["wlo"])
-        scan(T.gx[:], T.gf[:], T.A16f[:], -8.0, op.max, op.add, ["A16f0", "A16f1", "A16f2", "gf0", "gf1", "gf2"], ["gx"])
-        tt(T.w1[:], T.Lw[:, C:5 * C].indirect(T.offW[:]), T.wlo[:], op.subtract, LK + ["offW", "wlo"], ["w1"])
-        tt(T.f1[:], T.gx[:, 15:C:16], T.gx[:, C + 15:2 * C:16], op.add, ["gx"], ["f1"])
-        tt(T.w1[:], T.w1[:], T.sg[:], op.mult, ["w1", "sg"], ["w1"])
-        tt(T.f2[:], T.f1[:], T.gx[:, 2 * C + 15:3 * C:16], op.add, ["gx", "f1"], ["f2"])
-        tt(T.W[:], T.w1[:], T.ex[:], op.add, ["w1", "ex"], ["W"])
+        act(T.wlo[:], T.Lw[:, 0:4 * C].indirect(T.offW[:]), AF.Copy, LK + ["offW"], ["wlo"], c=gat(96))
+        tt(T.w1[:], T.Lw[:, C:5 * C].indirect(T.offW[:]), T.wlo[:], op.subtract, LK + ["offW", "wlo"], ["w1"], c=gat(96))
+        tt(T.w1[:], T.w1[:], T.sg[:], op.mult, ["w1", "sg"], ["w1"], c=192)
+        tt(T.W[:], T.w1[:], T.ex[:], op.add, ["w1", "ex"], ["W"], c=192)
+        tt(T.f1[:], T.gx[:, 15:C:16], T.gx[:, C + 15:2 * C:16], op.add, ["gx0", "gx1"], ["f1"])
+        tt(T.f2[:], T.f1[:], T.gx[:, 2 * C + 15:3 * C:16], op.add, ["gx2", "f1"], ["f2"])
         ts(T.f1[:], T.f2[:], -float(C), None, op.mult, None, ["f2"], ["f1"])
         tt(T.f2[:], T.f1[:], T.IC[:], op.add, ["f1", "IC"], ["f2"])
         cp(T.offK[:], T.f2[:], ["f2"], ["offK"])
-        act(T.vlo[:], T.Lw[:, 0:4 * C].indirect(T.offK[:]), AF.Copy, LK + ["offK"], ["vlo"])
-        if r == 0:
-            for h in range(2):
-                quant(T.qE[:, 256 * h:256 * h + 256], T.sE[:, 256 * h:256 * h + 256], T.Et[:, 1024 * h:1024 * h + 1024],
-                      ["Et%d" % (2 * h), "Et%d" % (2 * h + 1)], ["qE%d" % h])
-        if r == 1:
-            quant(T.qV[:], T.sV[:], T.vb[:], ["vb"], ["qV"])
-        tt(T.vv[:], T.Lw[:, C:5 * C].indirect(T.offK[:]), T.vlo[:], op.subtract, LK + ["offK", "vlo"], ["vv"])
-        gaps = [
-            [lambda: scan(T.v4[:], T.A4[:], T.vv[:], 0.0, op.add, op.max, ["A4", "vv"], ["v4"])],
-            [lambda: ts(T.z1[:], T.v4[:, 3:C:4], col(9), 1.0 / 7, op.subtract, op.mult, ["v4", "col9"], ["z1"])],
-            [lambda: cp(T.z2[:], T.z1[:], ["z1"], ["z2"])],
-            [lambda: ts(T.z2[:], T.z2[:], 63, None, op.bitwise_and, None, ["z2"], ["z2"])],
-            [lambda: ts(T.z1[:], T.z2[:], -7.0, col(12), op.mult, op.add, ["z2", "col12"], ["z1"])],
-            [lambda: tt(T.z1[:], T.z1[:], T.v4[:, 3:C:4], op.add, ["z1", "v4"], ["z1"])],
-            [lambda: cp(T.offZ[:], T.z1[:], ["z1"], ["offZ"])],
-        ]
+        act(T.vlo[:], T.Lw[:, 0:4 * C].indirect(T.offK[:]), AF.Copy, LK + ["offK"], ["vlo"], c=gat(C))
+        for j in range(3):
+            a, b = 96 * j, 96 * j + 96
+            tt(T.vv[:, a:b], T.Lw[:, C:5 * C].indirect(T.offK[:, 6 * j:6 * j + 6]), T.vlo[:, a:b], op.subtract,
+               LK + ["offK", "vlo"], ["vv%d" % j], c=gat(96))
+        for h in range(2):
+            a, b = HC * h, HC * (h + 1)
+            scan(T.v4[:, a:b], T.A4[:, a:b], T.vv[:, a:b], 0.0, op.add, op.max, ["A4", "vv%d" % h, "vv%d" % (h + 1)],
+                 ["v4%d" % h], c=HC)
+        ts(T.z1[:], T.v4[:, 3:C:4], col(9), 1.0 / 7, op.subtract, op.mult, ["v40", "v41", "col9"], ["z1"], c=72)
+        cp(T.z2[:], T.z1[:], ["z1"], ["z2"], c=72)
+        ts(T.z2[:], T.z2[:], 63, None, op.bitwise_and, None, ["z2"], ["z2"], c=72)
+        ts(T.z1[:], T.z2[:], -7.0, col(12), op.mult, op.add, ["z2", "col12"], ["z1"], c=72)
+        tt(T.z1[:], T.z1[:], T.v4[:, 3:C:4], op.add, ["z1", "v40", "v41"], ["z1"], c=144)
+        cp(T.offZ[:], T.z1[:], ["z1"], ["offZ"], c=72)
         qL, sL = T["qL%d" % r][:], T["sL%d" % r][:]
-        mm(3, A, T.qR[:, 640:768], T.sR[:, 640:768], qL, sL, ["qR1", "sR1"], ext=[("arr%d" % r, n_arr)])
-        mm(2, A, T.qR[:, 640:768], T.sR[:, 640:768], qL, sL, ["qR1", "sR1"])
+        mm(3, A, ur(5)[0], ur(5)[1], qL, sL, ["qR5", "sR5"], ext=arr)
+        mm(2, A, ur(5)[0], ur(5)[1], qL, sL, ["qR5", "sR5"], ext=arr)
         for b in range(4):
-            mm(4 + b, A, T.qE[:, 128 * b:128 * b + 128], T.sE[:, 128 * b:128 * b + 128], qL, sL, ["qE%d" % (b // 2)])
-        act(T.LM[:, 0:A], PS(2, 0, A), AF.Copy, [], ["LM"], [2])
+            mm(4 + b, A, T.qE[:, 128 * b:128 * b + 128], T.sE[:, 128 * b:128 * b + 128], qL, sL, ["qE%d" % b], ext=arr)
+            act(T.Bh[:, b:512:4], PS(4 + b, 0, A), AF.Copy, [], ["Bh%d" % b], [4 + b], c=A, scale=0.5)
+        act(T.LM[:, 0:A], PS(2, 0, A), AF.Copy, [], ["LM"], [2], c=A)
         BK = ["Bh0", "Bh1", "Bh2", "Bh3"]
-
-        def table(t, q):
-            out = T.tab[:, t:16 * TS_:TS_]
-            src = T.Bh[:].indirect(T.offT[:, 2 * t:2 * t + 1])
-            if q == "v":
-                cp(out, src, BK + ["offT%d" % t], ["tab%d" % t])
-            else:
-                act(out, src, AF.Copy, BK + ["offT%d" % t], ["tab%d" % t])
-            if last:
-                act(T.tabE[:, t:16 * TS_:TS_], T.iq[:].indirect(T.offT[:, 2 * t:2 * t + 1]), AF.Copy, ["iq", "offT%d" % t],
-                    ["tabE%d" % t])
-
-        def meal_offsets(t):
-            ts(T.offT[:, 2 * t:2 * t + 1], T.ee[:, t:t + 1], 4.0, rc_, op.mult, op.add, ["ee%d" % t, "fp"], ["offT%d" % t])
         for t in range(NT):
             if t == 0:
-                scan(T.pm[:], PS(3, 0, A), T.NEG[:], -H, op.max, op.max, ["NEG"], ["pm"], [3])
+                scan(T.pm[:], PS(3, 0, A), T.NEG[:], -H, op.max, op.max, ["NEG"], ["pm"], [3], c=A)
             else:
-                scan(T.pm[:], T.LM[:, 0:A], T.NEG[:], -H, op.max, op.max, ["NEG", "LM"], ["pm"])
+                scan(T.pm[:], T.LM[:, 0:A], T.NEG[:], -H, op.max, op.max, ["NEG", "LM"], ["pm"], c=A)
             e = T.ee[:, t:t + 1]
-            act(T.st[:, 1:A + 1], T.pm[:], AF.Sign, ["pm"], ["st", "ee%d" % t], bias=T.pm[:, A - 1:A], scale=-1.0, accum_out=e)
-            if t > 0:
-                meal_offsets(t - 1)
-            for f in gaps[t]:
-                f()
-            if t < 2:
-                for b in (2 * t, 2 * t + 1):
-                    act(T.Bh[:, b:512:4], PS(4 + b, 0, A), AF.Copy, [], ["Bh%d" % b], [4 + b], scale=0.5)
-            else:
-                if t == 2:
-                    table(0, "s")
-                table(t - 1, "s")
-            if r == 0 and 2 <= t < 6:
-                a = C * (t - 2)
-                act(T.Y[:, a:a + C], T.X[:, a:a + C], AF.Copy, XK, YK[4 * ((t - 2) // 2):4 * ((t - 2) // 2) + 4], scale=32.0)
+            act(T.st[:, 1:A + 1], T.pm[:], AF.Sign, ["pm"], ["st", "ee%d" % t], c=A, bias=T.pm[:, A - 1:A], scale=-1.0, accum_out=e)
             if t < NT - 1:
                 n = 16 * (t + 1)
                 ts(T.offE[:, t:t + 1], e, col(5), col(6), op.mult, op.add, ["ee%d" % t, "col5", "col6"], ["offE%d" % t])
                 tt(T.dw[:, 0:n], T.st[:, 0:A + 1].indirect(T.offE[:, 0:t + 1]), T.W[:, 96 - n:96], op.mult,
-                   ["st", "st0", "W"] + ["offE%d" % j for j in range(t + 1)], ["dw"])
+                   ["st", "st0", "W"] + ["offE%d" % j for j in range(t + 1)], ["dw"], c=gat(n))
                 add("v", lambda e_, n=n: e_.tensor_reduce(T.xn[:, 0:1], T.dw[:, 0:n], AxisListType.X, op.add, negate=True),
-                    ["dw"], ["xn"])
+                    ["dw"], ["xn"], c=n)
                 ts(T.offD[:, 0:1], T.xn[:, 0:1], e, col(7), op.max, op.min, ["xn", "ee%d" % t, "col7"], ["offD"])
-                cp(T.LM[:].indirect(T.offD[:, 0:1]), T.NEG[:, 0:16], ["offD", "NEG"], ["LM", "LMd"])
+                cp(T.LM[:].indirect(T.offD[:, 0:1]), T.NEG[:, 0:16], ["offD", "NEG"], ["LM", "LMd"], c=120)
+            ts(T.offT[:, 2 * t:2 * t + 1], e, 4.0, rc_, op.mult, op.add, ["ee%d" % t, "fp"], ["offT%d" % t])
+            out = T.tab[:, t:16 * TS_:TS_]
+            src = T.Bh[:].indirect(T.offT[:, 2 * t:2 * t + 1])
+            if t == NT - 1:
+                cp(out, src, BK + ["offT%d" % t], ["tab%d" % t], c=90)
             else:
-                meal_offsets(t)
-                table(t, "v")
+                act(out, src, AF.Copy, BK + ["offT%d" % t], ["tab%d" % t], c=100)
+            if last:
+                act(T.tabE[:, t:16 * TS_:TS_], T.iq[:].indirect(T.offT[:, 2 * t:2 * t + 1]), AF.Copy, ["iq", "offT%d" % t],
+                    ["tabE%d" % t], c=100)
         TK = ["tab%d" % t for t in range(NT)]
         if last:
-            act(T.olw[:], T.tabE[:].indirect(T.offZ[:]), AF.Copy, ["tabE%d" % t for t in range(NT)] + ["offZ"], ["olw"])
-            act(T.vlo[:], T.olw[:, 0:4 * C:4], AF.Copy, ["olw"], ["vlo"])
+            act(T.olw[:], T.tabE[:].indirect(T.offZ[:]), AF.Copy, ["tabE%d" % t for t in range(NT)] + ["offZ"], ["olw", "~o"],
+                c=gat(4 * C))
+            act(T.vlo[:], T.olw[:, 0:4 * C:4], AF.Copy, ["olw"], ["vlo"], c=C)
             dma("y", T.ol[:], T.vlo[0:128:16, :], ["vlo"], ["o0"])
         for h in range(2):
-            tt(T.Z[:, 4 * HC * h:4 * HC * (h + 1)], T.tab[:].indirect(T.offZ[:, 36 * h:36 * h + 36]),
-               T.Xh[:, 4 * HC * h:4 * HC * (h + 1)], op.add, TK + ["offZ", "Xh"], ["Z%d" % h])
-            qz, sz = T.qZ[:, HC * h:HC * (h + 1)], T.sZ[:, HC * h:HC * (h + 1)]
-            quant(qz, sz, T.Z[:, 4 * HC * h:4 * HC * (h + 1)], ["Z%d" % h], ["qZ%d" % h])
+            for j in (2 * h, 2 * h + 1):
+                tt(T.Z[:, C * j:C * j + C], T.tab[:].indirect(T.offZ[:, 18 * j:18 * j + 18]), T.Xh[:, C * j:C * j + C], op.add,
+                   TK + ["offZ", "Xh%d" % j] + ["~z"] * (j == 3), ["Z%d" % j] + ["~w"] * (j == 2), c=gat(C))
+                if j == 2:
+                    quant(T.qZ[:, 0:HC], T.sZ[:, 0:HC], T.Z[:, 0:4 * HC], HC, ["Z0", "Z1", "~w"], ["qZ0", "~z"])
+        quant(T.qZ[:, HC:C], T.sZ[:, HC:C], T.Z[:, 4 * HC:4 * C], HC, ["Z2", "Z3"], ["qZ1"])
+        for h in range(2):
             for b in range(4):
-                mm(4 * (1 - h) + b, HC, T.qW[:, 128 * b:128 * b + 128], T.sW[:, 128 * b:128 * b + 128], qz, sz,
-                   ["qW", "sW", "qZ%d" % h])
+                mm(4 * (1 - h) + b, HC, T.qW[:, 128 * b:128 * b + 128], T.sW[:, 128 * b:128 * b + 128],
+                   T.qZ[:, HC * h:HC * (h + 1)], T.sZ[:, HC * h:HC * (h + 1)], ["qW", "sW", "qZ%d" % h])
         for h in range(2):
             for b in range(4):
                 bk = 4 * (1 - h) + b
                 yv = T.Y[:, 4 * HC * h + b:4 * HC * (h + 1):4]
-                tt(yv, PS(bk, 0, HC), yv, op.add, ["Y%d%d" % (h, b)], ["Y%d%d" % (h, b)], [bk])
-                act(T.X[:, 4 * HC * h + b:4 * HC * (h + 1):4], yv, AF.Copy, ["Y%d%d" % (h, b)], ["X%d%d" % (h, b)], scale=0.03125)
-                if (h, b) == (1, 1):
-                    quant_x(0)
-                    if last:
-                        mm(7, HC, T.qV[:], T.sV[:], T.qX[:, 0:HC], T.sX[:, 0:HC], ["qV", "qX0"])
-                    else:
-                        mm(7, HC, u0c, u0s, T.qX[:, 0:HC], T.sX[:, 0:HC], ["qR0", "sR0", "qX0"])
-    dma("y", T.oc[:, 0:4 * HC], T.qX[:, 0:HC].bitcast(dt.uint8), ["qX0"], ["o1"])
-    cp(T.c0[:, 0:HC], PS(7, 0, HC), [], ["c0"], [7])
-    dma("y", T.y[:, 0:HC], T.c0[:, 0:HC], ["c0"], ["o2"])
-    quant_x(1)
-    mm(0, HC, T.qV[:], T.sV[:], T.qX[:, HC:C], T.sX[:, HC:C], ["qV", "qX1"])
-    dma("y", T.oc[:, 4 * HC:4 * C], T.qX[:, HC:C].bitcast(dt.uint8), ["qX1"], ["o3"])
+                tt(yv, PS(bk, 0, HC), yv, op.add, ["Y%d%d" % (h, b)] + ["~x"] * ((h, b) == (1, 2)), ["Y%d%d" % (h, b)], [bk], c=HC)
+                act(T.X[:, 4 * HC * h + b:4 * HC * (h + 1):4], yv, AF.Copy, ["Y%d%d" % (h, b), "~o"], ["X%d%d" % (h, b)], c=HC,
+                    scale=0.03125)
+            quant_x(h, ["~x"] * (h == 0))
+            if not last and h == 0:
+                mm(7, HC, u0c, u0s, T.qX[:, 0:HC], T.sX[:, 0:HC], U0 + ["qX0"])
+    for h, (bk, buf, key) in enumerate(((7, T.c0, "c0"), (0, T.hold, "hold0"))):
+        a, b = HC * h, HC * (h + 1)
+        mm(bk, HC, T.qV[:], T.sV[:], T.qX[:, a:b], T.sX[:, a:b], ["qV", "qX%d" % h])
+        dma("y", T.oc[:, 4 * a:4 * b], T.qX[:, a:b].bitcast(dt.uint8), ["qX%d" % h], ["o%d" % (1 + h)])
+        cp(buf[:, 0:HC], PS(bk, 0, HC), [], [key], [bk], c=HC)
+        dma("y", T.y[:, a:b], buf[:, 0:HC], [key], ["o%d" % (3 + h)])
     for k in range(4):
         dma("s", T.osc[4 * k:4 * k + 4, :], T.sX[32 * k:32 * k + 4, :], QX, ["o%d" % (k + 5)])
-    cp(T.m01[:, 0:HC], PS(0, 0, HC), [], ["m01"], [0])
-    dma("y", T.y[:, HC:C], T.m01[:, 0:HC], ["m01"], ["o4"])
     add("y", None, ["o%d" % k for k in range(9)])
     add("g", None, ext=[("loc", n_loc[0])])
-    emit(g, T, ops)
+    emit(g, T, arrange(ops))

@@ -9,12 +9,16 @@ BIG = float(2 ** 20)
 CK = 448
 TS_ = CK // 4
 F32, BF, I32, U16, X4, U8 = "float32", "bfloat16", "int32", "uint16", "float8_e4m3fn_x4", "uint8"
-TW = [288, 224, 160, 128, 128]
-SLOT = {}
-for _m in range(17, 0, -1):
-    SLOT[_m] = ((18 - _m) // 4, (18 - _m) % 4)
-ON_SCALAR = (17, 16)
-HOP, TRIP, LOAD = 210, (5000, 3500, 3500), 2800
+INNER = [[(2, 0, 2), (8, 2, 8), (1, 8, 9)], [(1, 0, 1), (7, 1, 7), (0, 7, 9)], [(6, 0, 6)], [(5, 0, 5)], [(4, 0, 4)], [(3, 0, 3)]]
+WIDTH = [32, 32, 32, 48, 64, 80, 96, 96, 96]
+TW = {"B0": HC, "B1": 128, "A0": HC, "A1": HC, "A2": HC, "A3": 128}
+T0 = {t: HC * i for i, t in enumerate(TW)}
+ON_SCALAR = (9, 10)
+IN_SCALAR = ((), (8, 7, 6, 5))
+ZCUT = ((0, 6, 20, 36), (0, 36))
+HOP, TRIP, LOAD = 240, (4500, 3000, 3000), 1800
+TRIES, SEED, SLACK, LESS = 5000, 1, 60, (0, 40, 80)
+ORDER = []
 
 
 def sb(n, d):
@@ -32,25 +36,22 @@ SCRATCH = {
     "Et": sb(2048, BF), "qE": sb(512, X4), "sE": sb(512, U8), "ones": sb(512, BF),
     "ip": sb(8, I32), "fp": sb(8, F32), "col": sb(24, F32), "s16": sb(160, F32), "offQ": sb(18, U16),
     "ofu": sb(48, F32), "offU": sb(48, U16),
-    "Mk": sb(C, F32), "K16": sb(C, F32), "Kd": sb(C, BF), "A16": sb(C, F32), "A16f": sb(C, BF), "A4": sb(C, F32),
+    "Mk": sb(HC, F32), "K16": sb(HC, F32), "Kd": sb(HC, BF), "A16": sb(C, F32), "A16f": sb(C, BF), "A4": sb(C, F32),
     "val": sb(C, F32), "m16": sb(18, F32), "Rc": sb(18, F32), "IC": sb(18, F32),
-    "Bm": sb(C, F32), "hold": sb(C, F32), "rel": sb(3 * C, F32), "junk": sb(2448, BF), "rows": sb(18, F32),
-    "dseg": sb(C, BF), "R1": sb(18, F32), "ext": sb(C, F32), "offP": sb(18, U16),
+    "Bm": sb(C, F32), "hold": sb(C, F32), "rel": sb(2448, F32), "junk": sb(2448, BF), "rows": sb(30, F32),
+    "dseg": sb(C, BF), "R1": sb(18, F32), "R2": sb(18, F32), "ext": sb(C, F32), "ex2": sb(A, F32), "offP": sb(20, U16),
+    "Tt": sb(4 * 6 * HC, BF), "qT": sb(6 * HC, X4), "sT": sb(6 * HC, U8),
     "win": sb(C, F32), "offM": sb(32, U16), "c0": sb(C, F32),
     "m01": sb(C, F32), "m012": sb(C, F32), "mx": sb(C, F32), "gf": sb(3 * C, BF), "gx": sb(3 * C, BF),
-    "Lw": sb(5 * C, F32), "offW": sb(6, U16), "wlo": sb(96, F32), "w1": sb(96, F32), "W": sb(96, F32),
-    "sg": sb(96, F32), "ex": sb(96, F32), "kp": sb(96, F32), "k2": sb(16, F32),
+    "Lw": sb(5 * C, F32), "offW": sb(2, U16), "wlo": sb(16, F32), "w1": sb(16, F32), "W": sb(48, F32),
+    "sg": sb(16, F32), "ex": sb(16, F32), "kp": sb(16, F32), "k2": sb(16, F32), "k3": sb(4, F32), "sv": sb(16, F32),
     "f1": sb(18, F32), "f2": sb(18, F32), "offK": sb(18, U16), "vlo": sb(C, F32), "vv": sb(C, F32), "v4": sb(C, F32),
     "z1": sb(72, F32), "z2": sb(72, I32), "offZ": sb(72, U16),
     "LM": sb(144, F32), "NEG": sb(128, F32), "pm": sb(128, F32), "st": sb(144, F32), "ee": sb(8, F32),
-    "offE": sb(8, U16), "offT": sb(16, U16), "offD": sb(2, U16), "dw": sb(96, F32), "xn": sb(2, F32),
+    "offE": sb(6 * NT, U16), "offD": sb(2, U16), "dw": sb(24, F32), "xn": sb(2, F32),
     "Bh": sb(512, BF), "tab": sb(16 * TS_, BF), "tabE": sb(16 * TS_, BF), "iq": sb(512, BF),
     "olw": sb(4 * C, F32),
 }
-for _t in range(5):
-    SCRATCH["T%d" % _t] = sb(4 * TW[_t], BF)
-    SCRATCH["qT%d" % _t] = sb(TW[_t], X4)
-    SCRATCH["sT%d" % _t] = sb(TW[_t], U8)
 for _r in range(3):
     for _n in ("qM", "qH", "qL"):
         SCRATCH["%s%d" % (_n, _r)] = sb(A, X4)
@@ -154,22 +155,80 @@ def arrange(ops):
         for name, val in ext:
             if name in sends:
                 pred[i].append((sends[name], TRIP[int(name[3:])]))
-    tail = [float(ops[i][7]) + (LOAD if ops[i][6] else 0) for i in range(n)]
+    cost, queue = [o[7] for o in ops], [o[0] for o in ops]
+    tail = [float(cost[i]) + (LOAD if ops[i][6] else 0) for i in range(n)]
+    above = [0] * n
+    for i in range(n):
+        for j, lat in pred[i]:
+            above[i] |= above[j] | 1 << j
+    for i in range(n):
+        pred[i] = [(j, lat) for j, lat in pred[i] if lat > HOP or not any(above[k] >> j & 1 and l2 for k, l2 in pred[i])]
     for i in range(n - 1, -1, -1):
         for j, lat in pred[i]:
-            tail[j] = max(tail[j], ops[j][7] + lat + tail[i])
+            tail[j] = max(tail[j], cost[j] + lat + tail[i])
     busy = {q: [] for q in "vspgy"}
-    start = [0.0] * n
+    end = [0.0] * n
     for i in sorted(range(n), key=lambda i: (-tail[i], i)):
-        t = max([start[j] + ops[j][7] + lat for j, lat in pred[i]] + [0.0])
-        for a, b in busy[ops[i][0]]:
-            if t + ops[i][7] <= a:
-                break
-            t = max(t, b)
-        start[i] = t
-        busy[ops[i][0]].append((t, t + ops[i][7]))
-        busy[ops[i][0]].sort()
-    return [ops[i] for i in sorted(range(n), key=lambda i: (start[i], i))]
+        t, c, line = max([end[j] + lat for j, lat in pred[i]] + [0.0]), cost[i], busy[queue[i]]
+        k = 0
+        while k < len(line) and t + c > line[k][0]:
+            t = max(t, line[k][1])
+            k += 1
+        end[i] = t + c
+        line.insert(k, (t, t + c))
+
+    def play(order):
+        total, holds = 0.0, []
+        for less in LESS:
+            last = {q: -1 for q in "vspgy"}
+            why = [-1] * n
+            for i in order:
+                w = last[queue[i]]
+                t = end[w] if w >= 0 else 0.0
+                for j, lat in pred[i]:
+                    if lat and end[j] + lat - less > t:
+                        t, w = end[j] + lat - less, j
+                end[i] = t + cost[i]
+                why[i] = w
+                last[queue[i]] = i
+            i = max(range(n), key=lambda i: end[i])
+            total += end[i]
+            while why[i] >= 0:
+                if not above[i] >> why[i] & 1:
+                    holds.append((why[i], i))
+                i = why[i]
+        return total, holds, order
+
+    now = best = play(sorted(range(n), key=lambda i: (end[i] - cost[i], i)))
+    seed = SEED
+    for k in range(TRIES):
+        seed = (seed * 1103515245 + 12345) % 2 ** 31
+        a, b = now[1][(seed >> 8) % len(now[1])]
+        order = now[2]
+        pa, pb = order.index(a), order.index(b)
+        reach = (seed >> 5) % 8 - 3
+        if seed >> 4 & 1:
+            for m in range(pb + 1, n):
+                if reach <= 0 or above[order[m]] >> a & 1 and queue[order[m]] == queue[a]:
+                    break
+                if queue[order[m]] == queue[a]:
+                    pb, reach = m, reach - 1
+            mid = order[pa:pb + 1]
+            new = [i for i in mid if i != a and not above[i] >> a & 1] + [i for i in mid if i == a or above[i] >> a & 1]
+        else:
+            for m in range(pa - 1, -1, -1):
+                if reach <= 0 or above[b] >> order[m] & 1 and queue[order[m]] == queue[a]:
+                    break
+                if queue[order[m]] == queue[a]:
+                    pa, reach = m, reach - 1
+            mid = order[pa:pb + 1]
+            new = [i for i in mid if i == b or above[b] >> i & 1] + [i for i in mid if i != b and not above[b] >> i & 1]
+        got = play(order[:pa] + new + order[pb + 1:])
+        if got[0] <= now[0] + SLACK * (1 - k / TRIES) * ((seed >> 12) % 8) / 4:
+            now = got
+            if now[0] < best[0]:
+                best = now
+    return best[2]
 
 
 def emit(g, T, ops):
@@ -246,7 +305,7 @@ def rank_program(g, core, T, topo):
         add("v", lambda e: e.quantize_mx(qc, sc, a), rd, wr, c=15 + 1.06 * n)
 
     def act(out, a, f, rd, wr, bk=(), c=64, **kw):
-        add("s", lambda e: e.activation(out, a, f, **kw), rd, wr, bk, c=c + (24 if "accum_out" in kw else 0))
+        add("s", lambda e: e.activation(out, a, f, **kw), rd, wr, bk, c=c + (24 if "accum_out" in kw else 0) + 18 * (c % 8 > 0))
 
     def mm(b, n, lc, ls, rc, rs, rd, start=True, stop=True, ext=()):
         add("p", lambda e: e.matmul_mx(T.ps[:, 512 * b:512 * b + n], lc, ls, rc, rs, start, stop), rd, (), [b], ext, c=1.3 * (n + 16))
@@ -264,7 +323,7 @@ def rank_program(g, core, T, topo):
         add(q, lambda e: e.dma_start(out, a), rd, wr, dma=True)
 
     def gat(n):
-        return 60 + 1.5 * n
+        return 60 + 1.56 * n
 
     def PS(b, a, n):
         return T.ps[:, 512 * b + a:512 * b + n]
@@ -275,14 +334,15 @@ def rank_program(g, core, T, topo):
     def s16(i):
         return T.s16[:, 16 * i:16 * i + 16]
 
-    def quant_x(h, more=()):
+    def quant_x(h):
         quant(T.qX[:, HC * h:HC * (h + 1)], T.sX[:, HC * h:HC * (h + 1)], T.X[:, 4 * HC * h:4 * HC * (h + 1)], HC,
-              XK[4 * h:4 * h + 4], ["qX%d" % h] + list(more))
+              XK[4 * h:4 * h + 4], ["qX%d" % h])
 
     XK = ["X%d%d" % (h, b) for h in range(2) for b in range(4)]
     YK = ["Y%d%d" % (h, b) for h in range(2) for b in range(4)]
-    dma("y", T.X[:], T.x[:], (), XK)
     dma("s", T.ub[:], T.u[:], (), ["ub"])
+    dma("y", T.X[:, 4 * HC:], T.x[:, 4 * HC:], (), XK[4:])
+    dma("y", T.X[:, 0:4 * HC], T.x[:, 0:4 * HC], (), XK[:4])
     add("y", None, XK)
     dma("y", T.qW[:].bitcast(dt.uint8), T.wc[:], (), ["qW"])
     dma("y", T.sW[:], T.ws[:], (), ["sW"])
@@ -294,13 +354,13 @@ def rank_program(g, core, T, topo):
     iota(s16(1), [[0, 4], [1, 4]], 0, 0, ["s1"])
     iota(T.ofu[:, 8:40], [[1, 4], [16, 8]], 4, 0, ["ofu1"])
     iota(T.ofu[:, 40:48], [[16, 8]], 8, 0, ["ofu2"])
-    for t, a in ((2, 112), (3, 48), (0, 240), (1, 176), (4, 0)):
-        iota(T["T%d" % t][:, 4 * a:], [[0, 4 * (TW[t] - a)]], 0, 0, ["T%d%d" % (t, e) for e in range(4)])
     iota(T.val[:], [[4, C]], 0, 0, ["val"])
-    iota(T.kp[:], [[0, 6], [1, 4], [0, 4]], 0, 0, ["kp"])
+    iota(T.kp[:], [[1, 4], [0, 4]], 0, 0, ["kp"])
     iota(T.Lw[:, 4 * C:5 * C], [[1, C]], 1 + 6 * CK, 0, ["L4"])
     iota(T.Lw[:, 0:C], [[0, C]], 0, 0, ["L0"])
-    ms(T.K16[:], H, ["K16"], c=C)
+    for t, a in (("B0", 96), ("B1", 0), ("A3", 48)):
+        ms(T.Tt[:, 4 * (T0[t] + a):4 * (T0[t] + TW[t])], 0.0, ["T%s%d" % (t, e) for e in range(4)], c=2 * (TW[t] - a))
+    ms(T.K16[:], H, ["K16"], c=HC)
     ts(T.ip[:, 2:4], T.ip[:, 0:2], 15, None, op.bitwise_and, None, ["ip0"], ["ip2"])
     ts(T.ip[:, 4:5], T.ip[:, 0:1], 2, 3, op.logical_shift_right, op.bitwise_and, ["ip0"], ["ip4"])
     ts(T.ip[:, 5:6], T.ip[:, 0:1], 3, None, op.bitwise_and, None, ["ip0"], ["ip5"])
@@ -308,7 +368,7 @@ def rank_program(g, core, T, topo):
     ms(T.ones[:], 1.0, ["ones"], c=256)
     cp(T.fp[:, 0:5], T.ip[:, 2:7], ["ip2", "ip4", "ip5", "ip6"], ["fp"])
     qc, qm, kc, rc_, gc_ = [T.fp[:, i:i + 1] for i in range(5)]
-    ms(T.K16[:, 0:C:16], -H, ["K16"])
+    ms(T.K16[:, 0:HC:16], -H, ["K16"])
     ts(s16(5), s16(0), qc, 0.5, op.is_equal, op.subtract, ["s0", "fp"], ["s5"])
     ts(T.offQ[:], T.m16[:], 0.0, qc, op.mult, op.add, ["m16", "fp"], ["offQ"])
     ts(T.col[:, 16:24], T.ofu[:, 0:8], gc_, None, op.is_equal, None, ["ofu0", "fp"], ["gcol"])
@@ -316,20 +376,23 @@ def rank_program(g, core, T, topo):
     cp(T.offU[:, 0:8], T.ofu[:, 0:8], ["ofu0"], ["offU0"])
     ts(s16(6), s16(0), qc, 1024.0, op.is_equal, op.mult, ["s0", "fp"], ["s6"])
     ts(s16(7), s16(0), qm, -4096.0, op.is_equal, op.mult, ["s0", "fp"], ["s7"])
-    ms(T.Kd[:], 1.0, ["Kd"], c=HC)
+    ms(T.Kd[:], 1.0, ["Kd"], c=72)
     tt(s16(3), s16(6), s16(7), op.add, ["s6", "s7"], ["s3"])
     ts(col(3), kc, 1.0, None, op.add, None, ["fp"], ["col3"])
     ts(col(4), kc, 2.5, 4096.0, op.is_lt, op.mult, ["fp"], ["col4"])
     ts(col(0), qc, -1.0, 15.0 - 1024.0, op.mult, op.add, ["fp"], ["col0"])
     ts(s16(8), s16(1), kc, -16384.0, op.is_equal, op.mult, ["s1", "fp"], ["s8"])
     ts(s16(9), s16(1), col(3), 4096.0, op.is_equal, op.mult, ["s1", "col3"], ["s9"])
-    ms(T.Kd[:, 0:C:16], 0.0, ["Kd"])
-    ms(T.rows[:, 0:1], 0.0, ["rows0"])
+    ms(T.Kd[:, 0:HC:16], 0.0, ["Kd"])
+    for w in sorted(set(WIDTH)):
+        a, b = WIDTH.index(w), WIDTH.index(w) + WIDTH.count(w)
+        ms(T.R2[:, a:b], float(w), ["R2w%d" % w])
+    ts(T.R2[:, 9:18], T.R2[:, 0:9], float(HC), None, op.add, None, ["R2w%d" % w for w in set(WIDTH)], ["R2"])
     tt(s16(4), s16(8), s16(9), op.add, ["s8", "s9"], ["s4"])
-    ts(T.Rc[:], T.m16[:], col(0), T.s16[:, 63:64], op.add, op.add, ["m16", "col0", "s3"], ["Rc"])
+    ts(T.Rc[:], T.R2[:], col(0), T.s16[:, 63:64], op.add, op.add, ["R2", "col0", "s3"], ["Rc"])
     ts(col(1), T.s16[:, 63:64], 0.0, -1.0, op.min, op.mult, ["s3"], ["col1"])
     ts(col(14), col(4), rc_, None, op.subtract, None, ["col4", "fp"], ["col14"])
-    act(T.Mk[:], s16(2).indirect(T.offQ[:]), AF.Copy, ["s2", "offQ"], ["Mk"], c=gat(C))
+    act(T.Mk[:], s16(2).indirect(T.offQ[:, 0:9]), AF.Copy, ["s2", "offQ"], ["Mk"], c=gat(HC))
     for j in range(8):
         act(T.Gt[:, 64 * j:64 * j + 64], T.ones[:, 0:64], AF.Copy, ["ones", "gcol"], ["Gt%d" % j], scale=col(16 + j))
     act(T.A16[:], s16(3).indirect(T.offQ[:]), AF.Copy, ["s3", "offQ"], ["A16"], c=gat(C))
@@ -340,29 +403,29 @@ def rank_program(g, core, T, topo):
     ts(col(9), col(4), 4.0, None, op.add, None, ["col4"], ["col9"])
     ts(col(10), rc_, float(TS_), -1.0, op.mult, op.add, ["fp"], ["col10"])
     ts(col(11), col(1), -24.0 * C / 4096, 9.0 * C, op.mult, op.add, ["col1"], ["col11"])
-    ts(col(13), kc, float(C), C - 1.0, op.mult, op.add, ["fp"], ["col13"])
+    ts(T.offW[:, 0:1], kc, float(C), C - 1.0, op.mult, op.add, ["fp"], ["offW"])
     cp(T.offU[:, 8:40], T.ofu[:, 8:40], ["ofu1"], ["offU1"])
     ts(T.offU[:, 40:48], T.ofu[:, 40:48], kc, None, op.add, None, ["ofu2", "fp"], ["offU5"])
-    ms(T.sg[:], 0.0, ["sg"], c=96)
-    ms(T.sg[:, 0:96:4], 512.0, ["sg"])
+    ms(T.sg[:], 0.0, ["sg"])
+    ms(T.sg[:, 0:16:4], 512.0, ["sg"])
     ms(T.NEG[:], -H, ["NEG"], c=128)
     ms(T.LM[:, 128:144], 0.0, ["LMd"])
     ms(T.st[:, 0:1], 1.0, ["st0"])
-    ts(T.w1[:, 0:16], T.kp[:, 80:96], kc, None, op.is_ge, None, ["kp", "fp"], ["w1"])
-    ts(T.k2[:], T.kp[:, 80:96], kc, -BIG / 512, op.is_lt, op.mult, ["kp", "fp"], ["k2"])
-    ms(T.sg[:, 1:96:4], -512.0, ["sg"])
-    ts(col(5), rc_, 1.5, None, op.is_lt, None, ["fp"], ["col5"])
-    ts(col(6), rc_, 1.0, None, op.is_equal, None, ["fp"], ["col6"])
+    ms(T.k3[:, 1:2], 0.0, ["k31"])
+    ts(T.w1[:], T.kp[:], kc, None, op.is_ge, None, ["kp", "fp"], ["w1"])
+    ts(T.k2[:], T.kp[:], kc, -BIG / 512, op.is_lt, op.mult, ["kp", "fp"], ["k2"])
+    ms(T.sg[:, 1:16:4], -512.0, ["sg"])
+    ts(T.k3[:, 0:1], rc_, 1.0, None, op.is_equal, None, ["fp"], ["k30"])
+    ts(T.k3[:, 2:3], rc_, float(A), None, op.mult, None, ["fp"], ["k32"])
     ts(col(8), rc_, 0.0, BIG - 95.5 * 512, op.is_equal, op.mult, ["fp"], ["col8"])
-    tt(T.k2[:], T.k2[:], T.sg[:, 80:96], op.mult, ["k2", "sg"], ["k2"])
-    ts(T.offW[:], T.m16[:, 0:6], 0.0, col(13), op.mult, op.add, ["m16", "col13"], ["offW"])
+    tt(T.k2[:], T.k2[:], T.sg[:], op.mult, ["k2", "sg"], ["k2"])
     ts(T.IC[:], T.m16[:], col(11), qc, op.add, op.add, ["m16", "col11", "fp"], ["IC"])
-    tt(T.sg[:, 80:96], T.sg[:, 80:96], T.w1[:, 0:16], op.mult, ["w1", "sg"], ["sg"])
-    ts(T.k2[:, 2:3], col(8), -BIG, None, op.add, None, ["col8", "k2"], ["k2"])
-    tt(T.ex[:], T.kp[:], T.sg[:], op.mult, ["kp", "sg"], ["ex"], c=192)
+    tt(T.sg[:], T.sg[:], T.w1[:], op.mult, ["w1", "sg"], ["sg"])
+    ts(T.dw[:, 16:17], col(8), -BIG, None, op.add, None, ["col8"], ["dwc"])
+    tt(T.ex[:], T.kp[:], T.sg[:], op.mult, ["kp", "sg"], ["ex"])
     ts(col(12), col(10), col(4), None, op.subtract, None, ["col10", "col4"], ["col12"])
-    ts(T.ex[:], T.ex[:], -float(CK), None, op.mult, None, ["ex"], ["ex"], c=96)
-    tt(T.ex[:, 80:96], T.ex[:, 80:96], T.k2[:], op.add, ["ex", "k2"], ["ex"])
+    ts(T.ex[:], T.ex[:], -float(CK), None, op.mult, None, ["ex"], ["ex"])
+    tt(T.ex[:], T.ex[:], T.k2[:], op.add, ["ex", "k2"], ["ex"])
     quant(T.qU[:], T.sU[:], T.ub[:], 128, ["ub"], ["qU"])
     quant(T.qV[:], T.sV[:], T.vb[:], 128, ["vb"], ["qV"])
 
@@ -411,53 +474,92 @@ def rank_program(g, core, T, topo):
     QX = ["qX0", "qX1"]
     U0 = ["qR0", "sR0"]
     u0c, u0s = ur(0)
+    CB = [3, 6, 7, 0]
+
+    def slot(t, e, lo, hi):
+        return T.Tt[:, 4 * T0[t] + 64 * lo + e:4 * T0[t] + 64 * hi:4], "T%s%d" % (t, e), "T%s%dw%d" % (t, e, lo)
+
+    def piece(bank, pivot, lo, hi, t, e, row, j0, o):
+        n = 16 * (hi - lo)
+        view, zero, key = slot(t, e, lo, hi)
+        p = T.hold[:, 16 * pivot + 15:16 * pivot + 16]
+        if o is None:
+            act(T.rel[:, j0:j0 + n], PS(bank, 16 * lo, 16 * hi), AF.Relu, ["hold%d" % (pivot // 9)], ["rel%d" % j0], [bank], c=n,
+                bias=p, scale=-1.0)
+            act(view, T.rel[:, j0:j0 + n], AF.Sign, ["rel%d" % j0, zero], [key, "rows%d" % row], c=max(64, n),
+                accum_out=T.rows[:, row:row + 1])
+        else:
+            ts(view, PS(bank, 16 * lo, 16 * hi), p, None, o, None, ["hold%d" % (pivot // 9), zero], [key], [bank], c=n)
+            act(T.junk[:, j0:j0 + n], view, AF.Copy, [key], ["junk%d" % j0, "rows%d" % row], c=max(64, n),
+                accum_out=T.rows[:, row:row + 1])
+        return key
+
+    def inner(h, bank, bank2, slots):
+        a, b = HC * h, HC * (h + 1)
+        keys = {}
+        tt(T.Bm[:, a:b], PS(bank, 0, HC), T.Mk[:], op.min, ["Mk"], ["Bm%d" % h], [bank], c=HC)
+        scan(T.hold[:, a:b], T.K16[:], T.Bm[:, a:b], -H, op.min, op.max, ["K16", "Bm%d" % h], ["hold%d" % h], c=HC)
+        view, zero, key = slot(slots[0][0], slots[0][1], 0, 9)
+        tt(view, PS(bank, 0, HC), T.hold[:, a:b], op.is_le, ["hold%d" % h, zero], [key], [bank], c=HC)
+        scan(T.dseg[:, a:b], T.Kd[:], view, 0.0, op.mult, op.add, ["Kd", key], ["dseg%d" % h], c=72)
+        keys.setdefault(slots[0][0], []).append(key)
+        j0 = 576 * h
+        for (t, e), run in zip(slots[1:], INNER):
+            for m, lo, hi in run:
+                row = 10 * h + (9 if (m, lo) == (1, 8) else m)
+                o = op.is_le if lo > m else None if m in IN_SCALAR[h] else op.is_lt
+                keys.setdefault(t, []).append(piece(bank if o else bank2, 9 * h + m, lo, hi, t, e, row, j0, o))
+                j0 += 16 * (hi - lo)
+        tt(T.R1[:, 9 * h:9 * h + 9], T.Rc[:, 9 * h:9 * h + 9], T.dseg[:, a + 15:b:16], op.subtract, ["Rc", "dseg%d" % h],
+           ["R1%d" % h])
+        ts(T.R1[:, 9 * h + 1:9 * h + 2], T.R1[:, 9 * h + 1:9 * h + 2], T.rows[:, 10 * h + 9:10 * h + 10], None, op.subtract, None,
+           ["R1%d" % h, "rows%d" % (10 * h + 9)], ["R1%d" % h])
+        return keys
+
+    def sums(bank, tiles, keys):
+        for i, t in enumerate(tiles):
+            a, b = T0[t], T0[t] + TW[t]
+            quant(T.qT[:, a:b], T.sT[:, a:b], T.Tt[:, 4 * a:4 * b], TW[t], keys[t] + ["T%s%d" % (t, e) for e in range(4)], ["qT" + t])
+            mm(bank, TW[t], T.qG[:], T.sG[:], T.qT[:, a:b], T.sT[:, a:b], ["qG", "qT" + t], i == 0, i == len(tiles) - 1)
+
+    def upper_half():
+        quant_x(1)
+        for b in (0, 2):
+            mm(b, HC, u0c, u0s, T.qX[:, HC:C], T.sX[:, HC:C], U0 + ["qX1"])
+        keys = inner(1, 0, 2, [("B0", 0), ("B0", 1), ("B0", 2), ("B0", 3), ("B1", 0), ("B1", 1), ("B1", 2)])
+        sums(1, ["B0", "B1"], keys)
+        tt(T.R2[:, 9:18], T.R1[:, 9:18], T.rows[:, 10:19], op.subtract, ["R11"] + ["rows%d" % m for m in range(10, 19)], ["R2"])
+
+    def places(h, bank, rd):
+        a, b = HC * h, HC * (h + 1)
+        off = T.offP[:, 10 * h:10 * h + 9]
+        scan(T.ext[:, a:b], PS(bank, 0, HC), T.A16[:, a:b], -4096.0, op.max, op.add, rd, ["ext%d" % h], [bank], c=HC)
+        ts(off, T.ext[:, a + 15:b:16], col(1), None, op.add, None, ["ext%d" % h, "col1"], ["offP%d" % h])
+        cp(T.win[:].indirect(off), T.val[:, a:b], ["offP%d" % h, "val"], ["win"], c=60 + 3.8 * HC)
+
+    upper_half()
     quant_x(0)
-    quant_x(1)
-    mm(7, HC, u0c, u0s, T.qX[:, 0:HC], T.sX[:, 0:HC], U0 + ["qX0"])
     for r, step in enumerate(STEPS):
         last = r == len(STEPS) - 1
-        def slot(m, w):
-            t, e = SLOT[m]
-            return T["T%d" % t][:, e:4 * w:4], "T%d%d" % (t, e)
-
-        def compare(m, b):
-            view, key = slot(m, 16 * m)
-            ts(view, PS(b, 0, 16 * m), T.hold[:, 16 * m + 15:16 * m + 16], None, op.is_lt, None, ["hold%d" % (m // 9)], [key], [b],
-               c=16 * m)
-            j0 = 8 * m * (m - 1)
-            act(T.junk[:, j0:j0 + 16 * m], view, AF.Copy, [key], ["junk%d" % m, "rows%d" % m], c=max(64, 16 * m),
-                accum_out=T.rows[:, m:m + 1])
-        tt(T.Bm[:, 0:HC], PS(7, 0, HC), T.Mk[:, 0:HC], op.min, ["Mk"], ["Bm0"], [7], c=HC)
-        for b in (0, 1):
-            mm(b, C, u0c, u0s, T.qX[:], T.sX[:], U0 + QX)
-        scan(T.hold[:, 0:HC], T.K16[:, 0:HC], T.Bm[:, 0:HC], -H, op.min, op.max, ["K16", "Bm0"], ["hold0"], c=HC)
-        for m in (8, 7, 6, 5):
-            compare(m, 7)
+        for b in (4, 5):
+            mm(b, HC, u0c, u0s, T.qX[:, 0:HC], T.sX[:, 0:HC], U0 + ["qX0"])
         for k in range(4):
-            mm(4 + k, C, ur(k + 1)[0], ur(k + 1)[1], T.qX[:], T.sX[:], ["qR%d" % (k + 1), "sR%d" % (k + 1)] + QX)
-        tt(T.Bm[:, HC:C], PS(0, HC, C), T.Mk[:, HC:C], op.min, ["Mk"], ["Bm1"], [0], c=HC)
-        scan(T.hold[:, HC:C], T.K16[:, HC:C], T.Bm[:, HC:C], -H, op.min, op.max, ["K16", "Bm1"], ["hold1"], c=HC)
-        for n, m in enumerate(ON_SCALAR):
-            act(T.rel[:, C * n:C * n + 16 * m], PS(1, 0, 16 * m), AF.Relu, ["hold1"], ["rel%d" % n], [1], c=16 * m,
-                bias=T.hold[:, 16 * m + 15:16 * m + 16], scale=-1.0)
-            view, key = slot(m, 16 * m)
-            act(view, T.rel[:, C * n:C * n + 16 * m], AF.Sign, ["rel%d" % n], [key, "rows%d" % m], c=16 * m,
-                accum_out=T.rows[:, m:m + 1])
-        for m in range(17, 0, -1):
-            if m not in ON_SCALAR + (8, 7, 6, 5):
-                compare(m, 0)
-        tt(T.T0[:, 0:4 * C:4], PS(0, 0, C), T.hold[:], op.is_le, ["hold0", "hold1"], ["T00"], [0], c=C)
-        scan(T.dseg[:], T.Kd[:], T.T0[:, 0:4 * C:4], 0.0, op.mult, op.add, ["Kd", "T00"], ["dseg"], c=HC)
-        for t in range(5):
-            quant(T["qT%d" % t][:], T["sT%d" % t][:], T["T%d" % t][:], TW[t], ["T%d%d" % (t, e) for e in range(4)], ["qT%d" % t])
-            mm(2, TW[t], T.qG[:], T.sG[:], T["qT%d" % t][:], T["sT%d" % t][:], ["qG", "qT%d" % t], t == 0, t == 4)
-        tt(T.R1[:], T.Rc[:], T.dseg[:, 15:C:16], op.subtract, ["Rc", "dseg"], ["R1"])
-        tt(T.A16[:, 15:C:16], T.R1[:], T.rows[:], op.subtract, ["R1"] + ["rows%d" % m for m in range(18)], ["A16"])
-        scan(T.ext[:], PS(2, 0, C), T.A16[:], -4096.0, op.max, op.add, ["A16"], ["ext"], [2], c=C)
-        ts(T.offP[:], T.ext[:, 15:C:16], col(1), None, op.add, None, ["ext", "col1"], ["offP"])
-        cp(T.win[:].indirect(T.offP[:]), T.val[:], ["offP", "val"], ["win"], c=60 + 3.5 * C)
-        scan(T.ext[:, 0:A], T.A4[:, 0:A], T.win[:, 0:A], 0.0, op.add, op.max, ["A4", "win"], ["ext"], c=A)
-        ts(T.offM[:], T.ext[:, 3:A:4], col(14), None, op.subtract, None, ["ext", "col14"], ["offM"])
+            mm(CB[k], C, ur(k + 1)[0], ur(k + 1)[1], T.qX[:], T.sX[:], ["qR%d" % (k + 1), "sR%d" % (k + 1)] + QX)
+        keys = {}
+        for n, m in enumerate(range(17, 8, -1)):
+            t = "A%d" % (n // 4)
+            keys.setdefault(t, []).append(piece(5 if m in ON_SCALAR else 4, m, 0, 9, t, n % 4, 11 + m, 1152 + HC * n,
+                                                None if m in ON_SCALAR else op.is_lt))
+        tt(T.A16[:, HC + 15:C:16], T.R2[:, 9:18], T.rows[:, 20:29], op.subtract,
+           ["R2", "A16"] + ["rows%d" % m for m in range(20, 29)], ["A161"])
+        for t, k in inner(0, 4, 5, [("A2", 1), ("A2", 2), ("A2", 3), ("A3", 0), ("A3", 1), ("A3", 2), ("A3", 3)]).items():
+            keys.setdefault(t, []).extend(k)
+        tt(T.A16[:, 15:HC:16], T.R1[:, 0:9], T.rows[:, 0:9], op.subtract, ["R10", "A16"] + ["rows%d" % m for m in range(9)], ["A160"])
+        sums(2, ["A0", "A1", "A2", "A3"], keys)
+        places(1, 1, ["A161"])
+        places(0, 2, ["A160"])
+        scan(T.ex2[:], T.A4[:, 0:A], T.win[:, 0:A], 0.0, op.add, op.max, ["A4", "win"], ["ex2"], c=A)
+        ts(T.offM[:], T.ex2[:, 3:A:4], col(14), None, op.subtract, None, ["ex2", "col14"], ["offM"])
         cp(T.M[:, 0:256], T.X[:].indirect(T.offM[:, 0:16]), XK + ["offM"], ["M0"], c=gat(256))
         act(T.M[:, 256:512], T.X[:].indirect(T.offM[:, 16:32]), AF.Copy, XK + ["offM"], ["M1"], c=gat(256))
         quant(T["qM%d" % r][:], T["sM%d" % r][:], T.M[:], A, ["M0", "M1"], ["qM%d" % r])
@@ -465,20 +567,20 @@ def rank_program(g, core, T, topo):
         if r == 0:
             e_tile(2)
             e_tile(3)
-            iota(T.iq[:], [[1, 128], [0, 4]], 0, 0, ["iq"])
+            iota(T.iq[:], [[0, 4], [1, 128]], 0, 0, ["iq"])
             for j in range(4):
                 act(T.Y[:, C * j:C * j + C], T.X[:, C * j:C * j + C], AF.Copy, XK + ["offM"], YK[4 * (j // 2):4 * (j // 2) + 4], c=C,
                     scale=32.0)
         for j in range(4):
             act(T.Xh[:, C * j:C * j + C], T.X[:, C * j:C * j + C], AF.Copy, XK + ["offM"], ["Xh%d" % j], c=C, scale=0.5)
-        act(T.c0[:], PS(4, 0, C), AF.Copy, [], ["c0"], [4], c=C)
+        act(T.c0[:], PS(CB[0], 0, C), AF.Copy, [], ["c0"], [CB[0]], c=C)
         for h in range(2):
             a, b = HC * h, HC * (h + 1)
-            tt(T.m01[:, a:b], PS(5, a, b), T.c0[:, a:b], op.max, ["c0"], ["m01%d" % h], [5], c=HC)
-            tt(T.m012[:, a:b], PS(6, a, b), T.m01[:, a:b], op.max, ["m01%d" % h], ["m012%d" % h], [6], c=HC)
-            tt(T.mx[:, a:b], PS(7, a, b), T.m012[:, a:b], op.max, ["m012%d" % h], ["mx%d" % h], [7], c=HC)
-        tt(T.gf[:, 2 * C:3 * C], PS(7, 0, C), T.m012[:], op.is_le, ["m0120", "m0121"], ["gf2"], [7], c=C)
-        tt(T.gf[:, 0:C], PS(4, 0, C), T.mx[:], op.is_ge, ["mx0", "mx1"], ["gf0"], [4], c=C)
+            tt(T.m01[:, a:b], PS(CB[1], a, b), T.c0[:, a:b], op.max, ["c0"], ["m01%d" % h], [CB[1]], c=HC)
+            tt(T.m012[:, a:b], PS(CB[2], a, b), T.m01[:, a:b], op.max, ["m01%d" % h], ["m012%d" % h], [CB[2]], c=HC)
+            tt(T.mx[:, a:b], PS(CB[3], a, b), T.m012[:, a:b], op.max, ["m012%d" % h], ["mx%d" % h], [CB[3]], c=HC)
+        tt(T.gf[:, 2 * C:3 * C], PS(CB[3], 0, C), T.m012[:], op.is_le, ["m0120", "m0121"], ["gf2"], [CB[3]], c=C)
+        tt(T.gf[:, 0:C], PS(CB[0], 0, C), T.mx[:], op.is_ge, ["mx0", "mx1"], ["gf0"], [CB[0]], c=C)
         tt(T.gf[:, C:2 * C], T.m01[:], T.mx[:], op.is_ge, ["m010", "m011", "mx0", "mx1"], ["gf1"], c=2 * C)
         for j, c in ((2, 3 * CK), (0, 0), (1, CK)):
             scan(T.Lw[:, C * (j + 1):C * (j + 2)], T.gf[:, C * j:C * j + C], T.Lw[:, 0:C], float(c), op.add, op.add,
@@ -486,10 +588,10 @@ def rank_program(g, core, T, topo):
             scan(T.gx[:, C * j:C * j + C], T.gf[:, C * j:C * j + C], T.A16f[:], -8.0, op.max, op.add, ["A16f", "gf%d" % j],
                  ["gx%d" % j], c=HC)
         LK = ["L0", "L1", "L2", "L3", "L4"]
-        act(T.wlo[:], T.Lw[:, 0:4 * C].indirect(T.offW[:]), AF.Copy, LK + ["offW"], ["wlo"], c=gat(96))
-        tt(T.w1[:], T.Lw[:, C:5 * C].indirect(T.offW[:]), T.wlo[:], op.subtract, LK + ["offW", "wlo"], ["w1"], c=gat(96))
-        tt(T.w1[:], T.w1[:], T.sg[:], op.mult, ["w1", "sg"], ["w1"], c=192)
-        tt(T.W[:], T.w1[:], T.ex[:], op.add, ["w1", "ex"], ["W"], c=192)
+        act(T.wlo[:], T.Lw[:, 0:4 * C].indirect(T.offW[:, 0:1]), AF.Copy, LK + ["offW"], ["wlo"], c=gat(16))
+        tt(T.w1[:], T.Lw[:, C:5 * C].indirect(T.offW[:, 0:1]), T.wlo[:], op.subtract, LK + ["offW", "wlo"], ["w1"], c=gat(16))
+        tt(T.w1[:], T.w1[:], T.sg[:], op.mult, ["w1", "sg"], ["w1"])
+        tt(T.W[:, 0:16], T.w1[:], T.ex[:], op.add, ["w1", "ex"], ["W0"])
         tt(T.f1[:], T.gx[:, 15:C:16], T.gx[:, C + 15:2 * C:16], op.add, ["gx0", "gx1"], ["f1"])
         tt(T.f2[:], T.f1[:], T.gx[:, 2 * C + 15:3 * C:16], op.add, ["gx2", "f1"], ["f2"])
         ts(T.f1[:], T.f2[:], -float(C), None, op.mult, None, ["f2"], ["f1"])
@@ -511,67 +613,71 @@ def rank_program(g, core, T, topo):
         tt(T.z1[:], T.z1[:], T.v4[:, 3:C:4], op.add, ["z1", "v40", "v41"], ["z1"], c=144)
         cp(T.offZ[:], T.z1[:], ["z1"], ["offZ"], c=72)
         qL, sL = T["qL%d" % r][:], T["sL%d" % r][:]
-        mm(3, A, ur(5)[0], ur(5)[1], qL, sL, ["qR5", "sR5"], ext=arr)
+        mm(1, A, ur(5)[0], ur(5)[1], qL, sL, ["qR5", "sR5"], ext=arr)
         mm(2, A, ur(5)[0], ur(5)[1], qL, sL, ["qR5", "sR5"], ext=arr)
         for b in range(4):
             mm(4 + b, A, T.qE[:, 128 * b:128 * b + 128], T.sE[:, 128 * b:128 * b + 128], qL, sL, ["qE%d" % b], ext=arr)
-            act(T.Bh[:, b:512:4], PS(4 + b, 0, A), AF.Copy, [], ["Bh%d" % b], [4 + b], c=A, scale=0.5)
+            act(T.Bh[:, A * b:A * b + A], PS(4 + b, 0, A), AF.Copy, [], ["Bh%d" % b], [4 + b], c=A, scale=0.5)
         act(T.LM[:, 0:A], PS(2, 0, A), AF.Copy, [], ["LM"], [2], c=A)
         BK = ["Bh0", "Bh1", "Bh2", "Bh3"]
         for t in range(NT):
             if t == 0:
-                scan(T.pm[:], PS(3, 0, A), T.NEG[:], -H, op.max, op.max, ["NEG"], ["pm"], [3], c=A)
+                scan(T.pm[:], PS(1, 0, A), T.NEG[:], -H, op.max, op.max, ["NEG"], ["pm"], [1], c=A)
             else:
                 scan(T.pm[:], T.LM[:, 0:A], T.NEG[:], -H, op.max, op.max, ["NEG", "LM"], ["pm"], c=A)
             e = T.ee[:, t:t + 1]
+            offE, offS, offT = [T.offE[:, 6 * t + 2 * j:6 * t + 2 * j + 1] for j in range(3)]
+            ok = "off%d" % t
             act(T.st[:, 1:A + 1], T.pm[:], AF.Sign, ["pm"], ["st", "ee%d" % t], c=A, bias=T.pm[:, A - 1:A], scale=-1.0, accum_out=e)
+            ts(T.offE[:, 6 * t:6 * t + 6:2], T.k3[:, 0:3], e, None, op.add, None, ["ee%d" % t, "k30", "k31", "k32"], [ok])
             if t < NT - 1:
-                n = 16 * (t + 1)
-                ts(T.offE[:, t:t + 1], e, col(5), col(6), op.mult, op.add, ["ee%d" % t, "col5", "col6"], ["offE%d" % t])
-                tt(T.dw[:, 0:n], T.st[:, 0:A + 1].indirect(T.offE[:, 0:t + 1]), T.W[:, 96 - n:96], op.mult,
-                   ["st", "st0", "W"] + ["offE%d" % j for j in range(t + 1)], ["dw"], c=gat(n))
-                add("v", lambda e_, n=n: e_.tensor_reduce(T.xn[:, 0:1], T.dw[:, 0:n], AxisListType.X, op.add, negate=True),
-                    ["dw"], ["xn"], c=n)
+                W, wk = (T.W[:, 0:16], "W0") if t == 0 else (T.W[:, 16:32], "W1")
+                tt(T.dw[:, 0:16], T.st[:, 0:A + 1].indirect(offE), W, op.mult, ["st", "st0", wk, ok], ["dw"], c=gat(16))
+                add("v", lambda e_: e_.tensor_reduce(T.xn[:, 0:1], T.dw[:, 0:17], AxisListType.X, op.add, negate=True),
+                    ["dw", "dwc"], ["xn"])
                 ts(T.offD[:, 0:1], T.xn[:, 0:1], e, col(7), op.max, op.min, ["xn", "ee%d" % t, "col7"], ["offD"])
                 cp(T.LM[:].indirect(T.offD[:, 0:1]), T.NEG[:, 0:16], ["offD", "NEG"], ["LM", "LMd"], c=120)
-            ts(T.offT[:, 2 * t:2 * t + 1], e, 4.0, rc_, op.mult, op.add, ["ee%d" % t, "fp"], ["offT%d" % t])
+            if t < NT - 2:
+                act(T.sv[:], T.LM[:].indirect(offS), AF.Relu, ["LM", "LMd", ok], ["sv"], c=100, bias=1.0, scale=2.0 ** -96)
+                tt(T.W[:, 32:48], T.sv[:], W, op.mult, ["sv", wk], ["W2"])
+                tt(T.W[:, 16:32], T.W[:, 32:48], T.W[:, 0:16], op.add, ["W2", "W0"], ["W1"])
             out = T.tab[:, t:16 * TS_:TS_]
-            src = T.Bh[:].indirect(T.offT[:, 2 * t:2 * t + 1])
+            src = T.Bh[:].indirect(offT)
             if t == NT - 1:
-                cp(out, src, BK + ["offT%d" % t], ["tab%d" % t], c=90)
+                cp(out, src, BK + [ok], ["tab%d" % t], c=90)
             else:
-                act(out, src, AF.Copy, BK + ["offT%d" % t], ["tab%d" % t], c=100)
+                act(out, src, AF.Copy, BK + [ok], ["tab%d" % t], c=100)
             if last:
-                act(T.tabE[:, t:16 * TS_:TS_], T.iq[:].indirect(T.offT[:, 2 * t:2 * t + 1]), AF.Copy, ["iq", "offT%d" % t],
-                    ["tabE%d" % t], c=100)
+                act(T.tabE[:, t:16 * TS_:TS_], T.iq[:].indirect(offT), AF.Copy, ["iq", ok], ["tabE%d" % t], c=100)
         TK = ["tab%d" % t for t in range(NT)]
         if last:
             act(T.olw[:], T.tabE[:].indirect(T.offZ[:]), AF.Copy, ["tabE%d" % t for t in range(NT)] + ["offZ"], ["olw", "~o"],
                 c=gat(4 * C))
             act(T.vlo[:], T.olw[:, 0:4 * C:4], AF.Copy, ["olw"], ["vlo"], c=C)
             dma("y", T.ol[:], T.vlo[0:128:16, :], ["vlo"], ["o0"])
-        for h in range(2):
-            for j in (2 * h, 2 * h + 1):
-                tt(T.Z[:, C * j:C * j + C], T.tab[:].indirect(T.offZ[:, 18 * j:18 * j + 18]), T.Xh[:, C * j:C * j + C], op.add,
-                   TK + ["offZ", "Xh%d" % j] + ["~z"] * (j == 3), ["Z%d" % j] + ["~w"] * (j == 2), c=gat(C))
-                if j == 2:
-                    quant(T.qZ[:, 0:HC], T.sZ[:, 0:HC], T.Z[:, 0:4 * HC], HC, ["Z0", "Z1", "~w"], ["qZ0", "~z"])
-        quant(T.qZ[:, HC:C], T.sZ[:, HC:C], T.Z[:, 4 * HC:4 * C], HC, ["Z2", "Z3"], ["qZ1"])
-        for h in range(2):
+        for h in (1, 0):
+            a, b = HC * h, HC * (h + 1)
+            cut = [36 * h + j for j in ZCUT[h]]
+            for i, j in zip(cut, cut[1:]):
+                tt(T.Z[:, 16 * i:16 * j], T.tab[:].indirect(T.offZ[:, i:j]), T.Xh[:, 16 * i:16 * j], op.add,
+                   TK + ["offZ", "Xh%d" % (2 * h), "Xh%d" % (2 * h + 1)], ["Z%d" % i], c=gat(16 * (j - i)))
+            quant(T.qZ[:, a:b], T.sZ[:, a:b], T.Z[:, 4 * a:4 * b], HC, ["Z%d" % i for i in cut[:-1]], ["qZ%d" % h])
+        for h in (1, 0):
             for b in range(4):
                 mm(4 * (1 - h) + b, HC, T.qW[:, 128 * b:128 * b + 128], T.sW[:, 128 * b:128 * b + 128],
                    T.qZ[:, HC * h:HC * (h + 1)], T.sZ[:, HC * h:HC * (h + 1)], ["qW", "sW", "qZ%d" % h])
-        for h in range(2):
+        for h in (1, 0):
             for b in range(4):
                 bk = 4 * (1 - h) + b
                 yv = T.Y[:, 4 * HC * h + b:4 * HC * (h + 1):4]
-                tt(yv, PS(bk, 0, HC), yv, op.add, ["Y%d%d" % (h, b)] + ["~x"] * ((h, b) == (1, 2)), ["Y%d%d" % (h, b)], [bk], c=HC)
+                tt(yv, PS(bk, 0, HC), yv, op.add, ["Y%d%d" % (h, b)], ["Y%d%d" % (h, b)], [bk], c=HC)
                 act(T.X[:, 4 * HC * h + b:4 * HC * (h + 1):4], yv, AF.Copy, ["Y%d%d" % (h, b), "~o"], ["X%d%d" % (h, b)], c=HC,
                     scale=0.03125)
-            quant_x(h, ["~x"] * (h == 0))
-            if not last and h == 0:
-                mm(7, HC, u0c, u0s, T.qX[:, 0:HC], T.sX[:, 0:HC], U0 + ["qX0"])
-    for h, (bk, buf, key) in enumerate(((7, T.c0, "c0"), (0, T.hold, "hold0"))):
+            if not last and h == 1:
+                upper_half()
+            else:
+                quant_x(h)
+    for h, bk, buf, key in ((1, 0, T.c0, "c0"), (0, 4, T.hold, "hold0")):
         a, b = HC * h, HC * (h + 1)
         mm(bk, HC, T.qV[:], T.sV[:], T.qX[:, a:b], T.sX[:, a:b], ["qV", "qX%d" % h])
         dma("y", T.oc[:, 4 * a:4 * b], T.qX[:, a:b].bitcast(dt.uint8), ["qX%d" % h], ["o%d" % (1 + h)])
@@ -581,4 +687,6 @@ def rank_program(g, core, T, topo):
         dma("s", T.osc[4 * k:4 * k + 4, :], T.sX[32 * k:32 * k + 4, :], QX, ["o%d" % (k + 5)])
     add("y", None, ["o%d" % k for k in range(9)])
     add("g", None, ext=[("loc", n_loc[0])])
-    emit(g, T, arrange(ops))
+    if not ORDER:
+        ORDER.extend(arrange(ops))
+    emit(g, T, [ops[i] for i in ORDER])

@@ -9,15 +9,22 @@ BIG = float(2 ** 20)
 CK = 448
 TS_ = CK // 4
 F32, BF, I32, U16, X4, U8 = "float32", "bfloat16", "int32", "uint16", "float8_e4m3fn_x4", "uint8"
-INNER = [[(2, 0, 2), (8, 2, 8), (1, 8, 9)], [(1, 0, 1), (7, 1, 7), (0, 7, 9)], [(6, 0, 6)], [(5, 0, 5)], [(4, 0, 4)], [(3, 0, 3)]]
-WIDTH = [32, 32, 32, 48, 64, 80, 96, 96, 96]
-TW = {"B0": HC, "B1": 128, "A0": HC, "A1": HC, "A2": HC, "A3": 128}
-T0 = {t: HC * i for i, t in enumerate(TW)}
-ON_SCALAR = (9, 10)
-IN_SCALAR = ((), (8, 7, 6, 5))
-ZCUT = ((0, 6, 20, 36), (0, 36))
-HOP, TRIP, LOAD = 240, (4500, 3000, 3000), 1800
-TRIES, SEED, SLACK, LESS = 5000, 1, 60, (0, 40, 80)
+PART = [(0, 160), (160, C)]
+NL = PART[0][1] // 16
+UPPER = [[10, 17, 16, 15], [14, 13, 12, 11]]
+INNER = [[(2, 0, 2), (9, 2, 9), (1, 9, 10)], [(1, 0, 1), (8, 1, 8), (0, 8, 10)],
+         [(7, 0, 7)], [(6, 0, 6)], [(5, 0, 5)], [(4, 0, 4)], [(3, 0, 3)]]
+TW = [288, 224, 160, 128]
+T0 = [0, 288, 512, 672]
+ZERO = [240, 176, 112, 48]
+UP0 = 96
+ON_SCALAR = (10, 11, 12, 13)
+ZCUT = [[("s", 0, 16), ("s", 16, 32), ("v", 32, 40)], [("v", 40, 72)]]
+PACES = [dict(cycle=0.83, gather=1.3, scatter=2.5, product=1.2, one=1.0, hop=200, dma=1500, first=3300, trip=2200),
+         dict(cycle=1.0, gather=1.56, scatter=3.8, product=1.5, one=1.0, hop=200, dma=1700, first=3800, trip=2600),
+         dict(cycle=1.2, gather=1.9, scatter=5.0, product=1.8, one=1.0, hop=180, dma=1900, first=4500, trip=3200)]
+SWEEPS, SHAKE, TRIES, SEED, SLACK = 1500, 0.12, 10000, 1, 60
+BITE = float(2 ** 97)
 ORDER = []
 
 
@@ -36,19 +43,19 @@ SCRATCH = {
     "Et": sb(2048, BF), "qE": sb(512, X4), "sE": sb(512, U8), "ones": sb(512, BF),
     "ip": sb(8, I32), "fp": sb(8, F32), "col": sb(24, F32), "s16": sb(160, F32), "offQ": sb(18, U16),
     "ofu": sb(48, F32), "offU": sb(48, U16),
-    "Mk": sb(HC, F32), "K16": sb(HC, F32), "Kd": sb(HC, BF), "A16": sb(C, F32), "A16f": sb(C, BF), "A4": sb(C, F32),
+    "Mk": sb(160, F32), "K16": sb(160, F32), "Kd": sb(160, BF), "A16": sb(C, F32), "A16f": sb(C, BF), "A4": sb(C, F32),
     "val": sb(C, F32), "m16": sb(18, F32), "Rc": sb(18, F32), "IC": sb(18, F32),
     "Bm": sb(C, F32), "hold": sb(C, F32), "rel": sb(2448, F32), "junk": sb(2448, BF), "rows": sb(30, F32),
     "dseg": sb(C, BF), "R1": sb(18, F32), "R2": sb(18, F32), "ext": sb(C, F32), "ex2": sb(A, F32), "offP": sb(20, U16),
-    "Tt": sb(4 * 6 * HC, BF), "qT": sb(6 * HC, X4), "sT": sb(6 * HC, U8),
+    "Tt": sb(4 * 800, BF), "qT": sb(800, X4), "sT": sb(800, U8),
     "win": sb(C, F32), "offM": sb(32, U16), "c0": sb(C, F32),
     "m01": sb(C, F32), "m012": sb(C, F32), "mx": sb(C, F32), "gf": sb(3 * C, BF), "gx": sb(3 * C, BF),
-    "Lw": sb(5 * C, F32), "offW": sb(2, U16), "wlo": sb(16, F32), "w1": sb(16, F32), "W": sb(48, F32),
-    "sg": sb(16, F32), "ex": sb(16, F32), "kp": sb(16, F32), "k2": sb(16, F32), "k3": sb(4, F32), "sv": sb(16, F32),
+    "Lw": sb(5 * C, F32), "offW": sb(2, U16), "wlo": sb(16, F32), "w1": sb(16, F32), "W": sb(80, F32),
+    "ex": sb(32, F32), "kp": sb(16, F32), "k3": sb(4, F32), "sv": sb(16, F32), "Zo": sb(4 * C, BF),
     "f1": sb(18, F32), "f2": sb(18, F32), "offK": sb(18, U16), "vlo": sb(C, F32), "vv": sb(C, F32), "v4": sb(C, F32),
     "z1": sb(72, F32), "z2": sb(72, I32), "offZ": sb(72, U16),
-    "LM": sb(144, F32), "NEG": sb(128, F32), "pm": sb(128, F32), "st": sb(144, F32), "ee": sb(8, F32),
-    "offE": sb(6 * NT, U16), "offD": sb(2, U16), "dw": sb(24, F32), "xn": sb(2, F32),
+    "KS": sb(20 * A, F32), "KO": sb(4 * A, F32), "NEG": sb(128, F32), "pm": sb(128, F32), "st": sb(128, F32), "ee": sb(8, F32),
+    "offE": sb(6 * NT, U16),
     "Bh": sb(512, BF), "tab": sb(16 * TS_, BF), "tabE": sb(16 * TS_, BF), "iq": sb(512, BF),
     "olw": sb(4 * C, F32),
 }
@@ -68,14 +75,7 @@ def helpers(topo, src, dst):
     can = [h for h in topo.cores_of(src) if h != src and topo.may_write(h, dst)]
     near = [h for h in can if topo.die(h) == topo.die(src)]
     far = [h for h in can if topo.die(h) != topo.die(src)]
-    return near[0], far[0], near[1]
-
-
-def bits(engines):
-    m = 0
-    for e in engines:
-        m |= 1 << e
-    return m
+    return near[0], far[0]
 
 
 def helper_program(g, core, T, topo):
@@ -94,12 +94,11 @@ def helper_program(g, core, T, topo):
         n_in = len(topo.engines(src, core))
         rid, pid = topo.addr(dst, core)
         mask = topo.mask(core, dst)
-        if k < 2:
-            g.wait_ge(T.sem["hop%d" % r], n_in // 2)
-            a = T["qH%d" % r][:, 64 * k:64 * k + 64].bitcast(dt.uint8)
-            b = T["qL%d" % r][:, 64 * k:64 * k + 64].bitcast(dt.uint8)
+        g.wait_ge(T.sem["hop%d" % r], n_in)
+        if k == 0:
+            a = T["qH%d" % r][:].bitcast(dt.uint8)
+            b = T["qL%d" % r][:].bitcast(dt.uint8)
         else:
-            g.wait_ge(T.sem["hop%d" % r], n_in)
             a = T["sH%d" % r][:]
             b = T["sL%d" % r][:]
         g.remote_dma(b, a, T.sem["arr%d" % r], T.sem.loc, pid, rid, mask)
@@ -137,57 +136,77 @@ def depend(ops, order=False):
     return out
 
 
+def length(c, p):
+    kind, n, fixed = c
+    if kind == "dma":
+        return 60.0
+    if kind == "":
+        return fixed + max(n, 64) * p["cycle"]
+    return fixed + n * p[kind] * p["cycle"]
+
+
 def arrange(ops):
     n = len(ops)
-    pred = [[(j, (LOAD if ops[j][6] else 0) + HOP) for j in d] for d in depend(ops)]
+    pred = [[(j, "dma" if ops[j][6] else "hop") for j in d] for d in depend(ops)]
     for i, d in enumerate(depend(ops, True)):
-        pred[i] += [(j, 0) for j in d]
+        pred[i] += [(j, "") for j in d]
     prev, sends = {}, {}
     for i, (q, fn, rd, wr, bk, ext, dma, c) in enumerate(ops):
         keys = [q] if q in "gy" else [("p", b) for b in bk] if q == "p" else []
         for k in keys:
             if k in prev:
-                pred[i].append((prev[k], 0))
+                pred[i].append((prev[k], ""))
             prev[k] = i
         for k in rd:
             if q == "g" and k.startswith("qM"):
                 sends.setdefault("arr" + k[2:], i)
         for name, val in ext:
             if name in sends:
-                pred[i].append((sends[name], TRIP[int(name[3:])]))
-    cost, queue = [o[7] for o in ops], [o[0] for o in ops]
-    tail = [float(cost[i]) + (LOAD if ops[i][6] else 0) for i in range(n)]
+                pred[i].append((sends[name], "first" if name == "arr0" else "trip"))
+    queue = [o[0] for o in ops]
     above = [0] * n
     for i in range(n):
         for j, lat in pred[i]:
             above[i] |= above[j] | 1 << j
     for i in range(n):
-        pred[i] = [(j, lat) for j, lat in pred[i] if lat > HOP or not any(above[k] >> j & 1 and l2 for k, l2 in pred[i])]
+        pred[i] = [(j, lat) for j, lat in pred[i] if lat not in ("", "hop") or not any(above[k] >> j & 1 and l2 for k, l2 in pred[i])]
+    plans = []
+    for p in PACES:
+        wait = lambda j, lat: 0 if not lat else p[lat] + (p["hop"] + ops[j][7][1] if lat == "dma" else 0)
+        plans.append(([length(o[7], p) for o in ops], [[(j, wait(j, lat)) for j, lat in d] for d in pred]))
+    cost, pre = plans[1]
+    tail = list(cost)
     for i in range(n - 1, -1, -1):
-        for j, lat in pred[i]:
+        for j, lat in pre[i]:
             tail[j] = max(tail[j], cost[j] + lat + tail[i])
-    busy = {q: [] for q in "vspgy"}
     end = [0.0] * n
-    for i in sorted(range(n), key=lambda i: (-tail[i], i)):
-        t, c, line = max([end[j] + lat for j, lat in pred[i]] + [0.0]), cost[i], busy[queue[i]]
-        k = 0
-        while k < len(line) and t + c > line[k][0]:
-            t = max(t, line[k][1])
-            k += 1
-        end[i] = t + c
-        line.insert(k, (t, t + c))
+
+    def fill(order, cost, pre):
+        busy = {q: [] for q in "vspgy"}
+        for i in order:
+            t, c, line = max([end[j] + lat for j, lat in pre[i]] + [0.0]), cost[i], busy[queue[i]]
+            k = len(line)
+            while k and line[k - 1][1] > t:
+                k -= 1
+            while k < len(line) and t + c > line[k][0]:
+                t = max(t, line[k][1])
+                k += 1
+            end[i] = t + c
+            line.insert(k, (t, t + c))
+        place = {i: k for k, i in enumerate(order)}
+        return sorted(order, key=lambda i: (-end[i], -place[i]))
 
     def play(order):
         total, holds = 0.0, []
-        for less in LESS:
+        for cost, pre in plans:
             last = {q: -1 for q in "vspgy"}
             why = [-1] * n
             for i in order:
                 w = last[queue[i]]
                 t = end[w] if w >= 0 else 0.0
-                for j, lat in pred[i]:
-                    if lat and end[j] + lat - less > t:
-                        t, w = end[j] + lat - less, j
+                for j, lat in pre[i]:
+                    if end[j] + lat > t:
+                        t, w = end[j] + lat, j
                 end[i] = t + cost[i]
                 why[i] = w
                 last[queue[i]] = i
@@ -199,8 +218,25 @@ def arrange(ops):
                 i = why[i]
         return total, holds, order
 
-    now = best = play(sorted(range(n), key=lambda i: (end[i] - cost[i], i)))
+    posts = []
+    for cost, pre in plans:
+        posts.append([[] for i in range(n)])
+        for i in range(n):
+            for j, lat in pre[i]:
+                posts[-1][j].append((i, lat))
+    now = best = play(fill(sorted(range(n), key=lambda i: (-tail[i], i)), *plans[1])[::-1])
     seed = SEED
+    for k in range(SWEEPS):
+        cost = []
+        for c in plans[k % 3][0]:
+            seed = (seed * 1103515245 + 12345) % 2 ** 31
+            cost.append(c * (1 + SHAKE * ((seed >> 8) % 64 - 32) / 32))
+        got = play(fill(fill(now[2][::-1], cost, posts[k % 3]), cost, plans[k % 3][1])[::-1])
+        if got[0] <= now[0] + 10 * SLACK * (1 - k / SWEEPS):
+            now = got
+            if now[0] < best[0]:
+                best = now
+    now = best
     for k in range(TRIES):
         seed = (seed * 1103515245 + 12345) % 2 ** 31
         a, b = now[1][(seed >> 8) % len(now[1])]
@@ -281,7 +317,7 @@ def rank_program(g, core, T, topo):
     ops = []
 
     def add(q, fn, rd=(), wr=(), bk=(), ext=(), dma=False, c=64):
-        ops.append((q, fn, list(rd), list(wr), list(bk), list(ext), dma, max(c, 64)))
+        ops.append((q, fn, list(rd), list(wr), list(bk), list(ext), dma, c if isinstance(c, tuple) else ("", c, 0)))
 
     def ts(out, in0, s1, s2, o0, o1, rd, wr, bk=(), c=64):
         if o1 is None:
@@ -305,25 +341,27 @@ def rank_program(g, core, T, topo):
         add("v", lambda e: e.quantize_mx(qc, sc, a), rd, wr, c=15 + 1.06 * n)
 
     def act(out, a, f, rd, wr, bk=(), c=64, **kw):
-        add("s", lambda e: e.activation(out, a, f, **kw), rd, wr, bk, c=c + (24 if "accum_out" in kw else 0) + 18 * (c % 8 > 0))
+        kind, n, fixed = c if isinstance(c, tuple) else ("", c, 0)
+        add("s", lambda e: e.activation(out, a, f, **kw), rd, wr, bk, c=(kind, n, fixed + 20 * ("accum_out" in kw) + 15 * (kind != "")))
 
     def mm(b, n, lc, ls, rc, rs, rd, start=True, stop=True, ext=()):
-        add("p", lambda e: e.matmul_mx(T.ps[:, 512 * b:512 * b + n], lc, ls, rc, rs, start, stop), rd, (), [b], ext, c=1.3 * (n + 16))
+        add("p", lambda e: e.matmul_mx(T.ps[:, 512 * b:512 * b + n], lc, ls, rc, rs, start, stop), rd, (), [b], ext,
+            c=("product", n + 16, 0))
 
     def iota(out, pat, base, cm, wr, small=True):
         n = 1
         for s, k in pat:
             n *= k
         if small:
-            add("g", lambda e: e.iota(out, pat, base, cm, allow_small_or_imprecise_dtypes=True), (), wr, c=157 + 2 * n)
+            add("g", lambda e: e.iota(out, pat, base, cm, allow_small_or_imprecise_dtypes=True), (), wr, c=("one", 2 * n, 130))
         else:
-            add("g", lambda e: e.iota(out, pat, base, cm), (), wr, c=157 + 2 * n)
+            add("g", lambda e: e.iota(out, pat, base, cm), (), wr, c=("one", 2 * n, 130))
 
-    def dma(q, out, a, rd, wr):
-        add(q, lambda e: e.dma_start(out, a), rd, wr, dma=True)
+    def dma(q, out, a, rd, wr, late=0):
+        add(q, lambda e: e.dma_start(out, a), rd, wr, dma=True, c=("dma", late, 0))
 
     def gat(n):
-        return 60 + 1.56 * n
+        return "gather", n, 50
 
     def PS(b, a, n):
         return T.ps[:, 512 * b + a:512 * b + n]
@@ -335,14 +373,14 @@ def rank_program(g, core, T, topo):
         return T.s16[:, 16 * i:16 * i + 16]
 
     def quant_x(h):
-        quant(T.qX[:, HC * h:HC * (h + 1)], T.sX[:, HC * h:HC * (h + 1)], T.X[:, 4 * HC * h:4 * HC * (h + 1)], HC,
-              XK[4 * h:4 * h + 4], ["qX%d" % h])
+        a, b = PART[h]
+        quant(T.qX[:, a:b], T.sX[:, a:b], T.X[:, 4 * a:4 * b], b - a, XK[4 * h:4 * h + 4], ["qX%d" % h])
 
     XK = ["X%d%d" % (h, b) for h in range(2) for b in range(4)]
     YK = ["Y%d%d" % (h, b) for h in range(2) for b in range(4)]
-    dma("s", T.ub[:], T.u[:], (), ["ub"])
-    dma("y", T.X[:, 4 * HC:], T.x[:, 4 * HC:], (), XK[4:])
-    dma("y", T.X[:, 0:4 * HC], T.x[:, 0:4 * HC], (), XK[:4])
+    dma("y", T.ub[:], T.u[:], (), ["ub"])
+    dma("y", T.X[:, 64 * NL:], T.x[:, 64 * NL:], (), XK[4:], 400)
+    dma("y", T.X[:, 0:64 * NL], T.x[:, 0:64 * NL], (), XK[:4], 800)
     add("y", None, XK)
     dma("y", T.qW[:].bitcast(dt.uint8), T.wc[:], (), ["qW"])
     dma("y", T.sW[:], T.ws[:], (), ["sW"])
@@ -358,9 +396,9 @@ def rank_program(g, core, T, topo):
     iota(T.kp[:], [[1, 4], [0, 4]], 0, 0, ["kp"])
     iota(T.Lw[:, 4 * C:5 * C], [[1, C]], 1 + 6 * CK, 0, ["L4"])
     iota(T.Lw[:, 0:C], [[0, C]], 0, 0, ["L0"])
-    for t, a in (("B0", 96), ("B1", 0), ("A3", 48)):
+    for t, a in enumerate(ZERO):
         ms(T.Tt[:, 4 * (T0[t] + a):4 * (T0[t] + TW[t])], 0.0, ["T%s%d" % (t, e) for e in range(4)], c=2 * (TW[t] - a))
-    ms(T.K16[:], H, ["K16"], c=HC)
+    ms(T.K16[:], H, ["K16"], c=160)
     ts(T.ip[:, 2:4], T.ip[:, 0:2], 15, None, op.bitwise_and, None, ["ip0"], ["ip2"])
     ts(T.ip[:, 4:5], T.ip[:, 0:1], 2, 3, op.logical_shift_right, op.bitwise_and, ["ip0"], ["ip4"])
     ts(T.ip[:, 5:6], T.ip[:, 0:1], 3, None, op.bitwise_and, None, ["ip0"], ["ip5"])
@@ -368,7 +406,7 @@ def rank_program(g, core, T, topo):
     ms(T.ones[:], 1.0, ["ones"], c=256)
     cp(T.fp[:, 0:5], T.ip[:, 2:7], ["ip2", "ip4", "ip5", "ip6"], ["fp"])
     qc, qm, kc, rc_, gc_ = [T.fp[:, i:i + 1] for i in range(5)]
-    ms(T.K16[:, 0:HC:16], -H, ["K16"])
+    ms(T.K16[:, 0:160:16], -H, ["K16"])
     ts(s16(5), s16(0), qc, 0.5, op.is_equal, op.subtract, ["s0", "fp"], ["s5"])
     ts(T.offQ[:], T.m16[:], 0.0, qc, op.mult, op.add, ["m16", "fp"], ["offQ"])
     ts(T.col[:, 16:24], T.ofu[:, 0:8], gc_, None, op.is_equal, None, ["ofu0", "fp"], ["gcol"])
@@ -383,49 +421,40 @@ def rank_program(g, core, T, topo):
     ts(col(0), qc, -1.0, 15.0 - 1024.0, op.mult, op.add, ["fp"], ["col0"])
     ts(s16(8), s16(1), kc, -16384.0, op.is_equal, op.mult, ["s1", "fp"], ["s8"])
     ts(s16(9), s16(1), col(3), 4096.0, op.is_equal, op.mult, ["s1", "col3"], ["s9"])
-    ms(T.Kd[:, 0:HC:16], 0.0, ["Kd"])
-    for w in sorted(set(WIDTH)):
-        a, b = WIDTH.index(w), WIDTH.index(w) + WIDTH.count(w)
-        ms(T.R2[:, a:b], float(w), ["R2w%d" % w])
-    ts(T.R2[:, 9:18], T.R2[:, 0:9], float(HC), None, op.add, None, ["R2w%d" % w for w in set(WIDTH)], ["R2"])
+    ms(T.Kd[:, 0:160:16], 0.0, ["Kd"])
+    ts(T.R2[:, 0:NL], T.m16[:, 0:NL], 32.0, 112.0, op.max, op.min, ["m16"], ["R2"])
     tt(s16(4), s16(8), s16(9), op.add, ["s8", "s9"], ["s4"])
-    ts(T.Rc[:], T.R2[:], col(0), T.s16[:, 63:64], op.add, op.add, ["R2", "col0", "s3"], ["Rc"])
+    ts(T.Rc[:, 0:NL], T.R2[:, 0:NL], col(0), T.s16[:, 63:64], op.add, op.add, ["R2", "col0", "s3"], ["Rc0"])
+    ts(T.Rc[:, NL:], T.m16[:, NL:], col(0), T.s16[:, 63:64], op.add, op.add, ["m16", "col0", "s3"], ["Rc1"])
     ts(col(1), T.s16[:, 63:64], 0.0, -1.0, op.min, op.mult, ["s3"], ["col1"])
     ts(col(14), col(4), rc_, None, op.subtract, None, ["col4", "fp"], ["col14"])
-    act(T.Mk[:], s16(2).indirect(T.offQ[:, 0:9]), AF.Copy, ["s2", "offQ"], ["Mk"], c=gat(HC))
+    act(T.Mk[:], s16(2).indirect(T.offQ[:, 0:NL]), AF.Copy, ["s2", "offQ"], ["Mk"], c=gat(160))
     for j in range(8):
         act(T.Gt[:, 64 * j:64 * j + 64], T.ones[:, 0:64], AF.Copy, ["ones", "gcol"], ["Gt%d" % j], scale=col(16 + j))
     act(T.A16[:], s16(3).indirect(T.offQ[:]), AF.Copy, ["s3", "offQ"], ["A16"], c=gat(C))
     act(T.A4[:], s16(4).indirect(T.offQ[:]), AF.Copy, ["s4", "offQ"], ["A4"], c=gat(C))
     act(T.A16f[:], s16(3).indirect(T.offQ[:]), AF.Copy, ["s3", "offQ"], ["A16f"], c=gat(C), scale=1.0 / 512)
     quant(T.qG[:], T.sG[:], T.Gt[:], 128, ["Gt%d" % j for j in range(8)], ["qG"])
-    ts(col(7), qc, 128.0, None, op.add, None, ["fp"], ["col7"])
     ts(col(9), col(4), 4.0, None, op.add, None, ["col4"], ["col9"])
     ts(col(10), rc_, float(TS_), -1.0, op.mult, op.add, ["fp"], ["col10"])
     ts(col(11), col(1), -24.0 * C / 4096, 9.0 * C, op.mult, op.add, ["col1"], ["col11"])
     ts(T.offW[:, 0:1], kc, float(C), C - 1.0, op.mult, op.add, ["fp"], ["offW"])
     cp(T.offU[:, 8:40], T.ofu[:, 8:40], ["ofu1"], ["offU1"])
     ts(T.offU[:, 40:48], T.ofu[:, 40:48], kc, None, op.add, None, ["ofu2", "fp"], ["offU5"])
-    ms(T.sg[:], 0.0, ["sg"])
-    ms(T.sg[:, 0:16:4], 512.0, ["sg"])
     ms(T.NEG[:], -H, ["NEG"], c=128)
-    ms(T.LM[:, 128:144], 0.0, ["LMd"])
-    ms(T.st[:, 0:1], 1.0, ["st0"])
-    ms(T.k3[:, 1:2], 0.0, ["k31"])
-    ts(T.w1[:], T.kp[:], kc, None, op.is_ge, None, ["kp", "fp"], ["w1"])
-    ts(T.k2[:], T.kp[:], kc, -BIG / 512, op.is_lt, op.mult, ["kp", "fp"], ["k2"])
-    ms(T.sg[:, 1:16:4], -512.0, ["sg"])
-    ts(T.k3[:, 0:1], rc_, 1.0, None, op.is_equal, None, ["fp"], ["k30"])
-    ts(T.k3[:, 2:3], rc_, float(A), None, op.mult, None, ["fp"], ["k32"])
-    ts(col(8), rc_, 0.0, BIG - 95.5 * 512, op.is_equal, op.mult, ["fp"], ["col8"])
-    tt(T.k2[:], T.k2[:], T.sg[:], op.mult, ["k2", "sg"], ["k2"])
     ts(T.IC[:], T.m16[:], col(11), qc, op.add, op.add, ["m16", "col11", "fp"], ["IC"])
-    tt(T.sg[:], T.sg[:], T.w1[:], op.mult, ["w1", "sg"], ["sg"])
-    ts(T.dw[:, 16:17], col(8), -BIG, None, op.add, None, ["col8"], ["dwc"])
-    tt(T.ex[:], T.kp[:], T.sg[:], op.mult, ["kp", "sg"], ["ex"])
     ts(col(12), col(10), col(4), None, op.subtract, None, ["col10", "col4"], ["col12"])
-    ts(T.ex[:], T.ex[:], -float(CK), None, op.mult, None, ["ex"], ["ex"])
-    tt(T.ex[:], T.ex[:], T.k2[:], op.add, ["ex", "k2"], ["ex"])
+    ts(col(7), col(1), -1.0 / 32, 128.0, op.mult, op.add, ["col1"], ["col7"])
+    ts(col(8), rc_, 128.0, col(7), op.mult, op.add, ["col7", "fp"], ["col8"])
+    ts(T.k3[:, 0:1], kc, 0.25, col(8), op.mult, op.add, ["col8", "fp"], ["k30"])
+    ms(T.k3[:, 1:2], 0.75, ["k31"])
+    ts(T.k3[:, 2:3], rc_, 0.25, None, op.mult, None, ["fp"], ["k32"])
+    ts(col(5), T.ones[:, 0:1], BITE, 95.5, op.mult, op.mult, ["ones"], ["col5"])
+    ts(col(6), T.ones[:, 0:1], BITE, 2.0 ** 15, op.mult, op.mult, ["ones"], ["col6"])
+    ts(T.ex[:, 0:16], T.kp[:], float(CK), BITE, op.mult, op.mult, ["kp"], ["ex0"])
+    ts(T.ex[:, 16:32], T.kp[:], 0.0, col(5), op.is_equal, op.mult, ["kp", "col5"], ["ex1"])
+    for a in (1, 2, 512):
+        act(T.KS[:, a:a // 512 * 512 + 512:4], T.ones[:, 0:A], AF.Copy, ["ones", "col6"], ["KS%d" % a], c=A, scale=col(6))
     quant(T.qU[:], T.sU[:], T.ub[:], 128, ["ub"], ["qU"])
     quant(T.qV[:], T.sV[:], T.vb[:], 128, ["vb"], ["qV"])
 
@@ -443,7 +472,7 @@ def rank_program(g, core, T, topo):
 
     def e_tile(b):
         add("g", lambda e: e.affine_select(T.Et[:, 512 * b:512 * b + 512], T.ones[:], [[1, 128], [256, 4]], op.is_equal, 0.0,
-                                           -256 * b, -1), ["ones"], ["Et%d" % b], c=1230)
+                                           -256 * b, -1), ["ones"], ["Et%d" % b], c=("one", 1024, 170))
         quant(T.qE[:, 128 * b:128 * b + 128], T.sE[:, 128 * b:128 * b + 128], T.Et[:, 512 * b:512 * b + 512], 128,
               ["Et%d" % b], ["qE%d" % b])
     e_tile(0)
@@ -454,21 +483,13 @@ def rank_program(g, core, T, topo):
     def send(r, step):
         dst = T.cores[rank ^ step]
         hs = helpers(topo, core, dst)
-        tr = []
-        for k in range(2):
-            en = topo.engines(core, hs[k])
-            half = len(en) // 2
-            rid, pid = topo.addr(hs[k], core)
-            tr.append(RemoteDMATransfer(dst_ids=[DstId(rid=rid, pnc=pid)], dma_engine_mask=bits(en[half * k:half * k + half]),
-                                        remote_sem=T.sem["hop%d" % r],
-                                        src=T["qM%d" % r][:, 64 * k:64 * k + 64].bitcast(dt.uint8),
-                                        dst=T["qH%d" % r][:, 64 * k:64 * k + 64].bitcast(dt.uint8)))
-            n_loc[0] += half
-        add("g", lambda e: e.remote_dma_fused(tr, local_sem=T.sem.loc), ["qM%d" % r])
-        rid, pid = topo.addr(hs[2], core)
-        add("g", lambda e: e.remote_dma(T["sH%d" % r][:], T["sM%d" % r][:], T.sem["hop%d" % r], T.sem.loc, pid, rid,
-                                        topo.mask(core, hs[2])), ["qM%d" % r])
-        n_loc[0] += len(topo.engines(core, hs[2]))
+
+        def hop(h, out, a):
+            rid, pid = topo.addr(h, core)
+            add("g", lambda e: e.remote_dma(out, a, T.sem["hop%d" % r], T.sem.loc, pid, rid, topo.mask(core, h)), ["qM%d" % r], c=200)
+            n_loc[0] += len(topo.engines(core, h))
+        hop(hs[0], T["qH%d" % r][:].bitcast(dt.uint8), T["qM%d" % r][:].bitcast(dt.uint8))
+        hop(hs[1], T["sH%d" % r][:], T["sM%d" % r][:])
         return sum(len(topo.engines(h, core)) for h in helpers(topo, dst, core))
 
     QX = ["qX0", "qX1"]
@@ -479,100 +500,113 @@ def rank_program(g, core, T, topo):
     def slot(t, e, lo, hi):
         return T.Tt[:, 4 * T0[t] + 64 * lo + e:4 * T0[t] + 64 * hi:4], "T%s%d" % (t, e), "T%s%dw%d" % (t, e, lo)
 
-    def piece(bank, pivot, lo, hi, t, e, row, j0, o):
-        n = 16 * (hi - lo)
+    SB = [(4, 5), (0, 2)]
+
+    def compare(m, lo, hi, t, e, j0, alone):
+        h, n = int(lo >= NL), 16 * (hi - lo)
         view, zero, key = slot(t, e, lo, hi)
-        p = T.hold[:, 16 * pivot + 15:16 * pivot + 16]
-        if o is None:
-            act(T.rel[:, j0:j0 + n], PS(bank, 16 * lo, 16 * hi), AF.Relu, ["hold%d" % (pivot // 9)], ["rel%d" % j0], [bank], c=n,
-                bias=p, scale=-1.0)
-            act(view, T.rel[:, j0:j0 + n], AF.Sign, ["rel%d" % j0, zero], [key, "rows%d" % row], c=max(64, n),
-                accum_out=T.rows[:, row:row + 1])
-        else:
-            ts(view, PS(bank, 16 * lo, 16 * hi), p, None, o, None, ["hold%d" % (pivot // 9), zero], [key], [bank], c=n)
-            act(T.junk[:, j0:j0 + n], view, AF.Copy, [key], ["junk%d" % j0, "rows%d" % row], c=max(64, n),
-                accum_out=T.rows[:, row:row + 1])
+        p, pk, bank = T.hold[:, 16 * m + 15:16 * m + 16], "hold%d" % (m >= NL), SB[h][alone]
+        s = PS(bank, 16 * (lo - NL * h), 16 * (hi - NL * h))
+        if alone:
+            act(T.rel[:, j0:j0 + n], s, AF.Relu, [pk], ["rel%d" % j0], [bank], c=n, bias=p, scale=-1.0)
+            return "rel%d" % j0
+        ts(view, s, p, None, op.is_le if lo > m else op.is_lt, None, [pk, zero], [key], [bank], c=n)
         return key
 
-    def inner(h, bank, bank2, slots):
-        a, b = HC * h, HC * (h + 1)
-        keys = {}
-        tt(T.Bm[:, a:b], PS(bank, 0, HC), T.Mk[:], op.min, ["Mk"], ["Bm%d" % h], [bank], c=HC)
-        scan(T.hold[:, a:b], T.K16[:], T.Bm[:, a:b], -H, op.min, op.max, ["K16", "Bm%d" % h], ["hold%d" % h], c=HC)
-        view, zero, key = slot(slots[0][0], slots[0][1], 0, 9)
-        tt(view, PS(bank, 0, HC), T.hold[:, a:b], op.is_le, ["hold%d" % h, zero], [key], [bank], c=HC)
-        scan(T.dseg[:, a:b], T.Kd[:], view, 0.0, op.mult, op.add, ["Kd", key], ["dseg%d" % h], c=72)
-        keys.setdefault(slots[0][0], []).append(key)
-        j0 = 576 * h
-        for (t, e), run in zip(slots[1:], INNER):
-            for m, lo, hi in run:
-                row = 10 * h + (9 if (m, lo) == (1, 8) else m)
-                o = op.is_le if lo > m else None if m in IN_SCALAR[h] else op.is_lt
-                keys.setdefault(t, []).append(piece(bank if o else bank2, 9 * h + m, lo, hi, t, e, row, j0, o))
-                j0 += 16 * (hi - lo)
-        tt(T.R1[:, 9 * h:9 * h + 9], T.Rc[:, 9 * h:9 * h + 9], T.dseg[:, a + 15:b:16], op.subtract, ["Rc", "dseg%d" % h],
+    def wins(lo, hi, t, e, j0, alone, row, rd):
+        n = 16 * (hi - lo)
+        view, zero, key = slot(t, e, lo, hi)
+        if alone:
+            act(view, T.rel[:, j0:j0 + n], AF.Sign, rd + [zero], [key, "rows%d" % row], c=n, accum_out=T.rows[:, row:row + 1])
+            return [key]
+        act(T.junk[:, j0:j0 + n], view, AF.Copy, rd, ["junk%d" % j0, "rows%d" % row], c=n, accum_out=T.rows[:, row:row + 1])
+        return rd
+
+    def pivots(h, t):
+        a, b = PART[h]
+        n, bank = b - a, SB[h][0]
+        for bk in SB[h]:
+            mm(bk, n, u0c, u0s, T.qX[:, a:b], T.sX[:, a:b], U0 + ["qX%d" % h])
+        tt(T.Bm[:, a:b], PS(bank, 0, n), T.Mk[:, 0:n], op.min, ["Mk"], ["Bm%d" % h], [bank], c=n)
+        scan(T.hold[:, a:b], T.K16[:, 0:n], T.Bm[:, a:b], -H, op.min, op.max, ["K16", "Bm%d" % h], ["hold%d" % h], c=n)
+        view, zero, key = slot(t, 0, a // 16, b // 16)
+        tt(view, PS(bank, 0, n), T.hold[:, a:b], op.is_le, ["hold%d" % h, zero], [key], [bank], c=n)
+        scan(T.dseg[:, a:b], T.Kd[:, 0:n], view, 0.0, op.mult, op.add, ["Kd", key], ["dseg%d" % h], c=n // 2)
+        tt(T.R1[:, a // 16:b // 16], T.Rc[:, a // 16:b // 16], T.dseg[:, a + 15:b:16], op.subtract, ["Rc%d" % h, "dseg%d" % h],
            ["R1%d" % h])
-        ts(T.R1[:, 9 * h + 1:9 * h + 2], T.R1[:, 9 * h + 1:9 * h + 2], T.rows[:, 10 * h + 9:10 * h + 10], None, op.subtract, None,
-           ["R1%d" % h, "rows%d" % (10 * h + 9)], ["R1%d" % h])
-        return keys
+        return key
 
-    def sums(bank, tiles, keys):
-        for i, t in enumerate(tiles):
-            a, b = T0[t], T0[t] + TW[t]
-            quant(T.qT[:, a:b], T.sT[:, a:b], T.Tt[:, 4 * a:4 * b], TW[t], keys[t] + ["T%s%d" % (t, e) for e in range(4)], ["qT" + t])
-            mm(bank, TW[t], T.qG[:], T.sG[:], T.qT[:, a:b], T.sT[:, a:b], ["qG", "qT" + t], i == 0, i == len(tiles) - 1)
+    def run0(m):
+        return 8 * (m * (m - 1) - NL * (NL - 1))
 
-    def upper_half():
+    def upper_part():
         quant_x(1)
-        for b in (0, 2):
-            mm(b, HC, u0c, u0s, T.qX[:, HC:C], T.sX[:, HC:C], U0 + ["qX1"])
-        keys = inner(1, 0, 2, [("B0", 0), ("B0", 1), ("B0", 2), ("B0", 3), ("B1", 0), ("B1", 1), ("B1", 2)])
-        sums(1, ["B0", "B1"], keys)
-        tt(T.R2[:, 9:18], T.R1[:, 9:18], T.rows[:, 10:19], op.subtract, ["R11"] + ["rows%d" % m for m in range(10, 19)], ["R2"])
+        got = {"own": pivots(1, 0)}
+        for t, row in enumerate(UPPER):
+            for e, m in enumerate(row):
+                got[m] = [compare(m, NL, m, t, e, run0(m) + 16 * NL, m in ON_SCALAR)] if m > NL else []
+        return got
 
-    def places(h, bank, rd):
-        a, b = HC * h, HC * (h + 1)
-        off = T.offP[:, 10 * h:10 * h + 9]
-        scan(T.ext[:, a:b], PS(bank, 0, HC), T.A16[:, a:b], -4096.0, op.max, op.add, rd, ["ext%d" % h], [bank], c=HC)
+    def sums(t, keys):
+        a, b = T0[t], T0[t] + TW[t]
+        quant(T.qT[:, a:b], T.sT[:, a:b], T.Tt[:, 4 * a:4 * b], TW[t], keys + ["T%s%d" % (t, e) for e in range(4)], ["qT%d" % t])
+        if t < 2:
+            mm(1, TW[t] - UP0, T.qG[:], T.sG[:], T.qT[:, a + UP0:b], T.sT[:, a + UP0:b], ["qG", "qT%d" % t], t == 0, t == 1)
+        n = min(TW[t], 16 * NL)
+        mm(2, n, T.qG[:], T.sG[:], T.qT[:, a:a + n], T.sT[:, a:a + n], ["qG", "qT%d" % t], t == 0, t == 3)
+
+    def places(h, bank, first):
+        a, b = PART[h]
+        off = T.offP[:, a // 16:b // 16]
+        tt(T.A16[:, a + 15:b:16], T.R1[:, a // 16:b // 16], T.rows[:, a // 16:b // 16], op.subtract,
+           ["R1%d" % h, "A16"] + ["rows%d" % m for m in range(a // 16, b // 16)], ["A16%d" % h])
+        scan(T.ext[:, a:b], PS(bank, first, first + b - a), T.A16[:, a:b], -4096.0, op.max, op.add, ["A16%d" % h], ["ext%d" % h],
+             [bank], c=b - a)
         ts(off, T.ext[:, a + 15:b:16], col(1), None, op.add, None, ["ext%d" % h, "col1"], ["offP%d" % h])
-        cp(T.win[:].indirect(off), T.val[:, a:b], ["offP%d" % h, "val"], ["win"], c=60 + 3.8 * HC)
+        cp(T.win[:].indirect(off), T.val[:, a:b], ["offP%d" % h, "val"], ["win"], c=("scatter", b - a, 50))
 
-    upper_half()
+    got = upper_part()
     quant_x(0)
     for r, step in enumerate(STEPS):
         last = r == len(STEPS) - 1
-        for b in (4, 5):
-            mm(b, HC, u0c, u0s, T.qX[:, 0:HC], T.sX[:, 0:HC], U0 + ["qX0"])
+        own = pivots(0, 2)
         for k in range(4):
             mm(CB[k], C, ur(k + 1)[0], ur(k + 1)[1], T.qX[:], T.sX[:], ["qR%d" % (k + 1), "sR%d" % (k + 1)] + QX)
-        keys = {}
-        for n, m in enumerate(range(17, 8, -1)):
-            t = "A%d" % (n // 4)
-            keys.setdefault(t, []).append(piece(5 if m in ON_SCALAR else 4, m, 0, 9, t, n % 4, 11 + m, 1152 + HC * n,
-                                                None if m in ON_SCALAR else op.is_lt))
-        tt(T.A16[:, HC + 15:C:16], T.R2[:, 9:18], T.rows[:, 20:29], op.subtract,
-           ["R2", "A16"] + ["rows%d" % m for m in range(20, 29)], ["A161"])
-        for t, k in inner(0, 4, 5, [("A2", 1), ("A2", 2), ("A2", 3), ("A3", 0), ("A3", 1), ("A3", 2), ("A3", 3)]).items():
-            keys.setdefault(t, []).extend(k)
-        tt(T.A16[:, 15:HC:16], T.R1[:, 0:9], T.rows[:, 0:9], op.subtract, ["R10", "A16"] + ["rows%d" % m for m in range(9)], ["A160"])
-        sums(2, ["A0", "A1", "A2", "A3"], keys)
-        places(1, 1, ["A161"])
-        places(0, 2, ["A160"])
+        for t, row in enumerate(UPPER):
+            keys = [got["own"]] if t == 0 else []
+            for e, m in enumerate(row):
+                key = compare(m, 0, NL, t, e, run0(m), m in ON_SCALAR)
+                keys += wins(0, m, t, e, run0(m), m in ON_SCALAR, m, got[m] + [key])
+            sums(t, keys)
+        keys, j0 = [[own], []], run0(18)
+        for n, run in enumerate(INNER):
+            t, e = 2 + (n + 1) // 4, (n + 1) % 4
+            for m, lo, hi in run:
+                key = compare(m, lo, hi, t, e, j0, (m, lo) in ON_SCALAR)
+                keys[t - 2] += wins(lo, hi, t, e, j0, (m, lo) in ON_SCALAR, 18 if (m, lo) == (1, 9) else m, [key])
+                j0 += 16 * (hi - lo)
+        ts(T.R1[:, 1:2], T.R1[:, 1:2], T.rows[:, 18:19], None, op.subtract, None, ["R10", "rows18"], ["R10"])
+        sums(2, keys[0])
+        sums(3, keys[1])
+        places(1, 1, 16 * NL - UP0)
+        places(0, 2, 0)
         scan(T.ex2[:], T.A4[:, 0:A], T.win[:, 0:A], 0.0, op.add, op.max, ["A4", "win"], ["ex2"], c=A)
         ts(T.offM[:], T.ex2[:, 3:A:4], col(14), None, op.subtract, None, ["ex2", "col14"], ["offM"])
         cp(T.M[:, 0:256], T.X[:].indirect(T.offM[:, 0:16]), XK + ["offM"], ["M0"], c=gat(256))
         act(T.M[:, 256:512], T.X[:].indirect(T.offM[:, 16:32]), AF.Copy, XK + ["offM"], ["M1"], c=gat(256))
         quant(T["qM%d" % r][:], T["sM%d" % r][:], T.M[:], A, ["M0", "M1"], ["qM%d" % r])
         arr = [("arr%d" % r, send(r, step))]
+        for a in (513, 514, 515):
+            iota(T.KS[:, a:1024:4], [[0, A]], 0, 0, ["KS%d" % a])
+        act(T.KS[:, 0:512:4], T.ones[:, 0:A], AF.Copy, ["ones", "col5"], ["KS0"], c=A, scale=col(5))
         if r == 0:
             e_tile(2)
             e_tile(3)
-            iota(T.iq[:], [[0, 4], [1, 128]], 0, 0, ["iq"])
-            for j in range(4):
-                act(T.Y[:, C * j:C * j + C], T.X[:, C * j:C * j + C], AF.Copy, XK + ["offM"], YK[4 * (j // 2):4 * (j // 2) + 4], c=C,
-                    scale=32.0)
-        for j in range(4):
-            act(T.Xh[:, C * j:C * j + C], T.X[:, C * j:C * j + C], AF.Copy, XK + ["offM"], ["Xh%d" % j], c=C, scale=0.5)
+            iota(T.iq[:], [[1, 128], [0, 4]], 0, 0, ["iq"])
+        for j, (a, b) in enumerate(((0, 320), (320, 640), (640, 896), (896, 4 * C))):
+            if r == 0:
+                act(T.Y[:, a:b], T.X[:, a:b], AF.Copy, XK + ["offM"], YK[4 * (j // 2):4 * (j // 2) + 4], c=b - a, scale=32.0)
+            act(T.Xh[:, a:b], T.X[:, a:b], AF.Copy, XK + ["offM"], ["Xh%d" % j], c=b - a, scale=0.5)
         act(T.c0[:], PS(CB[0], 0, C), AF.Copy, [], ["c0"], [CB[0]], c=C)
         for h in range(2):
             a, b = HC * h, HC * (h + 1)
@@ -590,8 +624,9 @@ def rank_program(g, core, T, topo):
         LK = ["L0", "L1", "L2", "L3", "L4"]
         act(T.wlo[:], T.Lw[:, 0:4 * C].indirect(T.offW[:, 0:1]), AF.Copy, LK + ["offW"], ["wlo"], c=gat(16))
         tt(T.w1[:], T.Lw[:, C:5 * C].indirect(T.offW[:, 0:1]), T.wlo[:], op.subtract, LK + ["offW", "wlo"], ["w1"], c=gat(16))
-        tt(T.w1[:], T.w1[:], T.sg[:], op.mult, ["w1", "sg"], ["w1"])
-        tt(T.W[:, 0:16], T.w1[:], T.ex[:], op.add, ["w1", "ex"], ["W0"])
+        ts(T.w1[:], T.w1[:], -BITE, None, op.mult, None, ["w1"], ["w1"])
+        tt(T.W[:, 0:16], T.w1[:], T.ex[:, 0:16], op.add, ["w1", "ex0"], ["V0"])
+        tt(T.W[:, 16:32], T.W[:, 0:16], T.ex[:, 16:32], op.add, ["V0", "ex1"], ["U0"])
         tt(T.f1[:], T.gx[:, 15:C:16], T.gx[:, C + 15:2 * C:16], op.add, ["gx0", "gx1"], ["f1"])
         tt(T.f2[:], T.f1[:], T.gx[:, 2 * C + 15:3 * C:16], op.add, ["gx2", "f1"], ["f2"])
         ts(T.f1[:], T.f2[:], -float(C), None, op.mult, None, ["f2"], ["f1"])
@@ -617,72 +652,78 @@ def rank_program(g, core, T, topo):
         mm(2, A, ur(5)[0], ur(5)[1], qL, sL, ["qR5", "sR5"], ext=arr)
         for b in range(4):
             mm(4 + b, A, T.qE[:, 128 * b:128 * b + 128], T.sE[:, 128 * b:128 * b + 128], qL, sL, ["qE%d" % b], ext=arr)
-            act(T.Bh[:, A * b:A * b + A], PS(4 + b, 0, A), AF.Copy, [], ["Bh%d" % b], [4 + b], c=A, scale=0.5)
-        act(T.LM[:, 0:A], PS(2, 0, A), AF.Copy, [], ["LM"], [2], c=A)
+            act(T.Bh[:, b:4 * A:4], PS(4 + b, 0, A), AF.Copy, [], ["Bh%d" % b], [4 + b], c=A, scale=0.5)
+        act(T.KS[:, 3:512:4], PS(2, 0, A), AF.Copy, [], ["KS3"], [2], c=A)
         BK = ["Bh0", "Bh1", "Bh2", "Bh3"]
+        KK = ["KS%d" % a for a in (0, 1, 2, 3, 512, 513, 514, 515)]
         for t in range(NT):
             if t == 0:
                 scan(T.pm[:], PS(1, 0, A), T.NEG[:], -H, op.max, op.max, ["NEG"], ["pm"], [1], c=A)
             else:
-                scan(T.pm[:], T.LM[:, 0:A], T.NEG[:], -H, op.max, op.max, ["NEG", "LM"], ["pm"], c=A)
+                scan(T.pm[:], T.KO[:, 3:512:4], T.NEG[:], -H, op.max, op.max, ["NEG", "KO"], ["pm"], c=A)
             e = T.ee[:, t:t + 1]
             offE, offS, offT = [T.offE[:, 6 * t + 2 * j:6 * t + 2 * j + 1] for j in range(3)]
             ok = "off%d" % t
-            act(T.st[:, 1:A + 1], T.pm[:], AF.Sign, ["pm"], ["st", "ee%d" % t], c=A, bias=T.pm[:, A - 1:A], scale=-1.0, accum_out=e)
-            ts(T.offE[:, 6 * t:6 * t + 6:2], T.k3[:, 0:3], e, None, op.add, None, ["ee%d" % t, "k30", "k31", "k32"], [ok])
+            act(T.st[:], T.pm[:], AF.Sign, ["pm"], ["st", "ee%d" % t], c=A, bias=T.pm[:, A - 1:A], scale=-1.0, accum_out=e)
+            ts(T.offE[:, 6 * t:6 * t + 6:2], T.k3[:, 0:3], e, 4.0, op.add, op.mult, ["ee%d" % t, "k30", "k31", "k32"], [ok])
+            V, vk, U, uk = (T.W[:, 0:16], "V0", T.W[:, 16:32], "U0") if t == 0 else (T.W[:, 32:48], "V1", T.W[:, 48:64], "U1")
             if t < NT - 1:
-                W, wk = (T.W[:, 0:16], "W0") if t == 0 else (T.W[:, 16:32], "W1")
-                tt(T.dw[:, 0:16], T.st[:, 0:A + 1].indirect(offE), W, op.mult, ["st", "st0", wk, ok], ["dw"], c=gat(16))
-                add("v", lambda e_: e_.tensor_reduce(T.xn[:, 0:1], T.dw[:, 0:17], AxisListType.X, op.add, negate=True),
-                    ["dw", "dwc"], ["xn"])
-                ts(T.offD[:, 0:1], T.xn[:, 0:1], e, col(7), op.max, op.min, ["xn", "ee%d" % t, "col7"], ["offD"])
-                cp(T.LM[:].indirect(T.offD[:, 0:1]), T.NEG[:, 0:16], ["offD", "NEG"], ["LM", "LMd"], c=120)
+                cp(T.KS[:].indirect(offE), U, [ok, uk], KK, c=("scatter", 16, 50))
+                scan(T.KO[:], T.KS[:, 512:1024], T.KS[:, 0:512], 0.0, op.add, op.min, KK, ["KO"], c=4 * A)
             if t < NT - 2:
-                act(T.sv[:], T.LM[:].indirect(offS), AF.Relu, ["LM", "LMd", ok], ["sv"], c=100, bias=1.0, scale=2.0 ** -96)
-                tt(T.W[:, 32:48], T.sv[:], W, op.mult, ["sv", wk], ["W2"])
-                tt(T.W[:, 16:32], T.W[:, 32:48], T.W[:, 0:16], op.add, ["W2", "W0"], ["W1"])
+                act(T.sv[:], T.KO[:].indirect(offS), AF.Relu, ["KO", ok], ["sv"], c=gat(16), bias=1.0, scale=2.0 / BITE)
+                tt(T.W[:, 64:80], T.sv[:], V, op.mult, ["sv", vk], ["W2"])
+                tt(T.W[:, 48:64], T.W[:, 64:80], T.W[:, 16:32], op.add, ["W2", "U0"], ["U1"])
+                if t < NT - 3:
+                    tt(T.W[:, 32:48], T.W[:, 64:80], T.W[:, 0:16], op.add, ["W2", "V0"], ["V1"])
             out = T.tab[:, t:16 * TS_:TS_]
             src = T.Bh[:].indirect(offT)
             if t == NT - 1:
-                cp(out, src, BK + [ok], ["tab%d" % t], c=90)
+                cp(out, src, BK + [ok], ["tab%d" % t], c=gat(16))
             else:
-                act(out, src, AF.Copy, BK + [ok], ["tab%d" % t], c=100)
+                act(out, src, AF.Copy, BK + [ok], ["tab%d" % t], c=gat(16))
             if last:
-                act(T.tabE[:, t:16 * TS_:TS_], T.iq[:].indirect(offT), AF.Copy, ["iq", ok], ["tabE%d" % t], c=100)
-        TK = ["tab%d" % t for t in range(NT)]
+                act(T.tabE[:, t:16 * TS_:TS_], T.iq[:].indirect(offT), AF.Copy, ["iq", ok], ["tabE%d" % t], c=gat(16))
+        TK = ["tab%d" % t for t in range(NT)] + ["offZ"]
+        for h in (1, 0):
+            a, b = PART[h]
+            for q, i, j in ZCUT[h]:
+                z, xh, meals = T.Z[:, 16 * i:16 * j], T.Xh[:, 16 * i:16 * j], T.tab[:].indirect(T.offZ[:, i:j])
+                xk = ["Xh%d" % (2 * h), "Xh%d" % (2 * h + 1)]
+                if q == "s":
+                    act(T.Zo[:, 16 * i:16 * j], meals, AF.Copy, TK, ["Zo%d" % i], c=gat(16 * (j - i)))
+                    tt(z, T.Zo[:, 16 * i:16 * j], xh, op.add, ["Zo%d" % i] + xk, ["Z%d" % i], c=16 * (j - i))
+                else:
+                    tt(z, meals, xh, op.add, TK + xk, ["Z%d" % i], c=gat(16 * (j - i)))
+            quant(T.qZ[:, a:b], T.sZ[:, a:b], T.Z[:, 4 * a:4 * b], b - a, ["Z%d" % i for q, i, j in ZCUT[h]], ["qZ%d" % h])
         if last:
-            act(T.olw[:], T.tabE[:].indirect(T.offZ[:]), AF.Copy, ["tabE%d" % t for t in range(NT)] + ["offZ"], ["olw", "~o"],
-                c=gat(4 * C))
-            act(T.vlo[:], T.olw[:, 0:4 * C:4], AF.Copy, ["olw"], ["vlo"], c=C)
-            dma("y", T.ol[:], T.vlo[0:128:16, :], ["vlo"], ["o0"])
+            for j in range(6):
+                act(T.olw[:, 192 * j:192 * j + 192], T.tabE[:].indirect(T.offZ[:, 12 * j:12 * j + 12]), AF.Copy,
+                    ["tabE%d" % t for t in range(NT)] + ["offZ"], ["olw%d" % j], c=gat(192))
+            act(T.vlo[:], T.olw[:, 0:4 * C:4], AF.Copy, ["olw%d" % j for j in range(6)], ["vlo"], c=C)
+            dma("s", T.ol[:], T.vlo[0:128:16, :], ["vlo"], ["o0"])
         for h in (1, 0):
-            a, b = HC * h, HC * (h + 1)
-            cut = [36 * h + j for j in ZCUT[h]]
-            for i, j in zip(cut, cut[1:]):
-                tt(T.Z[:, 16 * i:16 * j], T.tab[:].indirect(T.offZ[:, i:j]), T.Xh[:, 16 * i:16 * j], op.add,
-                   TK + ["offZ", "Xh%d" % (2 * h), "Xh%d" % (2 * h + 1)], ["Z%d" % i], c=gat(16 * (j - i)))
-            quant(T.qZ[:, a:b], T.sZ[:, a:b], T.Z[:, 4 * a:4 * b], HC, ["Z%d" % i for i in cut[:-1]], ["qZ%d" % h])
-        for h in (1, 0):
+            lo, hi = PART[h]
             for b in range(4):
-                mm(4 * (1 - h) + b, HC, T.qW[:, 128 * b:128 * b + 128], T.sW[:, 128 * b:128 * b + 128],
-                   T.qZ[:, HC * h:HC * (h + 1)], T.sZ[:, HC * h:HC * (h + 1)], ["qW", "sW", "qZ%d" % h])
+                mm(4 * (1 - h) + b, hi - lo, T.qW[:, 128 * b:128 * b + 128], T.sW[:, 128 * b:128 * b + 128],
+                   T.qZ[:, lo:hi], T.sZ[:, lo:hi], ["qW", "sW", "qZ%d" % h])
         for h in (1, 0):
+            lo, hi = PART[h]
             for b in range(4):
                 bk = 4 * (1 - h) + b
-                yv = T.Y[:, 4 * HC * h + b:4 * HC * (h + 1):4]
-                tt(yv, PS(bk, 0, HC), yv, op.add, ["Y%d%d" % (h, b)], ["Y%d%d" % (h, b)], [bk], c=HC)
-                act(T.X[:, 4 * HC * h + b:4 * HC * (h + 1):4], yv, AF.Copy, ["Y%d%d" % (h, b), "~o"], ["X%d%d" % (h, b)], c=HC,
-                    scale=0.03125)
+                yv = T.Y[:, 4 * lo + b:4 * hi:4]
+                tt(yv, PS(bk, 0, hi - lo), yv, op.add, ["Y%d%d" % (h, b)], ["Y%d%d" % (h, b)], [bk], c=hi - lo)
+                act(T.X[:, 4 * lo + b:4 * hi:4], yv, AF.Copy, ["Y%d%d" % (h, b)], ["X%d%d" % (h, b)], c=hi - lo, scale=0.03125)
             if not last and h == 1:
-                upper_half()
+                got = upper_part()
             else:
                 quant_x(h)
     for h, bk, buf, key in ((1, 0, T.c0, "c0"), (0, 4, T.hold, "hold0")):
-        a, b = HC * h, HC * (h + 1)
-        mm(bk, HC, T.qV[:], T.sV[:], T.qX[:, a:b], T.sX[:, a:b], ["qV", "qX%d" % h])
+        a, b = PART[h]
+        mm(bk, b - a, T.qV[:], T.sV[:], T.qX[:, a:b], T.sX[:, a:b], ["qV", "qX%d" % h])
         dma("y", T.oc[:, 4 * a:4 * b], T.qX[:, a:b].bitcast(dt.uint8), ["qX%d" % h], ["o%d" % (1 + h)])
-        cp(buf[:, 0:HC], PS(bk, 0, HC), [], [key], [bk], c=HC)
-        dma("y", T.y[:, a:b], buf[:, 0:HC], [key], ["o%d" % (3 + h)])
+        cp(buf[:, 0:b - a], PS(bk, 0, b - a), [], [key], [bk], c=b - a)
+        dma("y", T.y[:, a:b], buf[:, 0:b - a], [key], ["o%d" % (3 + h)])
     for k in range(4):
         dma("s", T.osc[4 * k:4 * k + 4, :], T.sX[32 * k:32 * k + 4, :], QX, ["o%d" % (k + 5)])
     add("y", None, ["o%d" % k for k in range(9)])

@@ -24,6 +24,8 @@ PACES = [dict(cycle=0.83, gather=1.3, scatter=2.5, product=1.2, one=1.0, hop=200
          dict(cycle=1.0, gather=1.56, scatter=3.8, product=1.5, one=1.0, hop=200, dma=1700, first=3800, trip=2600),
          dict(cycle=1.2, gather=1.9, scatter=5.0, product=1.8, one=1.0, hop=180, dma=1900, first=4500, trip=3200)]
 SWEEPS, SHAKE, TRIES, SEED, SLACK = 1500, 0.12, 10000, 1, 60
+SWITCH = 3
+ON_VECTOR = (3, 7, 11, 15)
 BITE = float(2 ** 97)
 ORDER = []
 
@@ -41,7 +43,7 @@ SCRATCH = {
     "qX": sb(C, X4), "sX": sb(C, U8), "qZ": sb(C, X4), "sZ": sb(C, U8),
     "Gt": sb(512, BF), "qG": sb(128, X4), "sG": sb(128, U8),
     "Et": sb(2048, BF), "qE": sb(512, X4), "sE": sb(512, U8), "ones": sb(512, BF),
-    "ip": sb(8, I32), "fp": sb(8, F32), "col": sb(24, F32), "s16": sb(160, F32), "offQ": sb(18, U16),
+    "ip": sb(8, I32), "fp": sb(8, F32), "col": sb(24, F32), "s16": sb(192, F32), "offQ": sb(18, U16),
     "ofu": sb(48, F32), "offU": sb(48, U16),
     "Mk": sb(160, F32), "K16": sb(160, F32), "Kd": sb(160, BF), "A16": sb(C, F32), "A16f": sb(C, BF), "A4": sb(C, F32),
     "val": sb(C, F32), "m16": sb(18, F32), "Rc": sb(18, F32), "IC": sb(18, F32),
@@ -50,14 +52,17 @@ SCRATCH = {
     "Tt": sb(4 * 800, BF), "qT": sb(800, X4), "sT": sb(800, U8),
     "win": sb(C, F32), "offM": sb(32, U16), "c0": sb(C, F32),
     "m01": sb(C, F32), "m012": sb(C, F32), "mx": sb(C, F32), "gf": sb(3 * C, BF), "gx": sb(3 * C, BF),
-    "Lw": sb(5 * C, F32), "offW": sb(2, U16), "wlo": sb(16, F32), "w1": sb(16, F32), "W": sb(80, F32),
-    "ex": sb(32, F32), "kp": sb(16, F32), "k3": sb(4, F32), "sv": sb(16, F32), "Zo": sb(4 * C, BF),
+    "Lw": sb(5 * C, F32), "offW": sb(2, U16), "wlo": sb(16, F32), "w1": sb(16, F32), "W": sb(112, F32),
+    "ex": sb(32, F32), "kp": sb(16, F32), "k3": sb(4, F32), "four": sb(A + 4, F32), "drift": sb(A + 4, F32), "Zo": sb(4 * C, BF),
     "f1": sb(18, F32), "f2": sb(18, F32), "offK": sb(18, U16), "vlo": sb(C, F32), "vv": sb(C, F32), "v4": sb(C, F32),
     "z1": sb(72, F32), "z2": sb(72, I32), "offZ": sb(72, U16),
     "KS": sb(20 * A, F32), "KO": sb(4 * A, F32), "NEG": sb(128, F32), "pm": sb(128, F32), "st": sb(128, F32), "ee": sb(8, F32),
     "offE": sb(6 * NT, U16),
     "Bh": sb(512, BF), "tab": sb(16 * TS_, BF), "tabE": sb(16 * TS_, BF), "iq": sb(512, BF),
     "olw": sb(4 * C, F32),
+    "Mk4": sb(2 * A, F32), "Bm4": sb(A, F32), "hold4": sb(A, F32), "Rt": sb(32 * A, BF), "qK": sb(8 * A, X4),
+    "sK": sb(8 * A, U8), "G4": sb(512, BF), "qG4": sb(A, X4), "sG4": sb(A, U8),
+    "KB": sb(20 * A, BF), "KP": sb(4 * A + 16, BF), "pb": sb(A, BF),
 }
 for _r in range(3):
     for _n in ("qM", "qH", "qL"):
@@ -449,8 +454,15 @@ def rank_program(g, core, T, topo):
     ts(T.k3[:, 0:1], kc, 0.25, col(8), op.mult, op.add, ["col8", "fp"], ["k30"])
     ms(T.k3[:, 1:2], 0.75, ["k31"])
     ts(T.k3[:, 2:3], rc_, 0.25, None, op.mult, None, ["fp"], ["k32"])
+    ms(T.four[:, 0:A], 4.0, ["four"], c=A)
+    ts(T.four[:, A:A + 1], T.k3[:, 0:1], -4.0, -4.0 * (A - 1), op.mult, op.add, ["k30"], ["k40"])
+    for j in (1, 2):
+        ts(T.four[:, A + j:A + j + 1], T.k3[:, j - 1:j], T.k3[:, j:j + 1], 4.0, op.subtract, op.mult, ["k30", "k31", "k32"], ["k4%d" % j])
+    ms(T.KP[:, 4 * A:], -H, ["KPe"])
     ts(col(5), T.ones[:, 0:1], BITE, 95.5, op.mult, op.mult, ["ones"], ["col5"])
     ts(col(6), T.ones[:, 0:1], BITE, 2.0 ** 15, op.mult, op.mult, ["ones"], ["col6"])
+    ts(col(2), T.ones[:, 0:1], BITE, -2.0 ** 9, op.mult, op.mult, ["ones"], ["col2"])
+    act(T.W[:, 16:48:2], T.ones[:, 0:16], AF.Copy, ["ones", "col6"], ["Wa0"], scale=col(6))
     ts(T.ex[:, 0:16], T.kp[:], float(CK), BITE, op.mult, op.mult, ["kp"], ["ex0"])
     ts(T.ex[:, 16:32], T.kp[:], 0.0, col(5), op.is_equal, op.mult, ["kp", "col5"], ["ex1"])
     for a in (1, 2, 512):
@@ -477,6 +489,16 @@ def rank_program(g, core, T, topo):
               ["Et%d" % b], ["qE%d" % b])
     e_tile(0)
     e_tile(1)
+    add("g", lambda e: e.affine_select(T.G4[:], T.ones[:], [[-4, 32], [0, 16]], op.is_ge, 0.0, 0, 1), ["ones"], ["G4"], c=("one", 1024, 170))
+    add("g", lambda e: e.affine_select(T.G4[:], T.G4[:], [[4, 32], [0, 16]], op.is_ge, 0.0, 3, -1), ["G4"], ["G4"], c=("one", 1024, 170))
+    quant(T.qG4[:], T.sG4[:], T.G4[:], 128, ["G4"], ["qG4"])
+    ts(s16(10), s16(1), rc_, 0.5, op.is_equal, op.subtract, ["s1", "fp"], ["s10"])
+    ts(s16(11), s16(10), 2 * H, None, op.mult, None, ["s10"], ["s11"])
+    act(T.Mk4[:, 0:A], s16(11).indirect(T.offQ[:, 0:8]), AF.Copy, ["s11", "offQ"], ["Mk4"], c=gat(A))
+    ms(T.Mk4[:, A:2 * A], H, ["K4"], c=A)
+    ms(T.Mk4[:, A:2 * A:4], -H, ["K4"])
+    for a in (1, 2, 512):
+        act(T.KB[:, a:a // 512 * 512 + 512:4], T.ones[:, 0:A], AF.Copy, ["ones", "col6"], ["KB%d" % a], c=A, scale=col(6))
 
     n_loc = [0]
 
@@ -598,7 +620,10 @@ def rank_program(g, core, T, topo):
         arr = [("arr%d" % r, send(r, step))]
         for a in (513, 514, 515):
             iota(T.KS[:, a:1024:4], [[0, A]], 0, 0, ["KS%d" % a])
+        for a in (513, 514, 515):
+            iota(T.KB[:, a:1024:4], [[0, A]], 0, 0, ["KB%d" % a])
         act(T.KS[:, 0:512:4], T.ones[:, 0:A], AF.Copy, ["ones", "col5"], ["KS0"], c=A, scale=col(5))
+        act(T.KB[:, 0:512:4], T.ones[:, 0:A], AF.Copy, ["ones", "col5"], ["KB0"], c=A, scale=col(5))
         if r == 0:
             e_tile(2)
             e_tile(3)
@@ -626,7 +651,7 @@ def rank_program(g, core, T, topo):
         tt(T.w1[:], T.Lw[:, C:5 * C].indirect(T.offW[:, 0:1]), T.wlo[:], op.subtract, LK + ["offW", "wlo"], ["w1"], c=gat(16))
         ts(T.w1[:], T.w1[:], -BITE, None, op.mult, None, ["w1"], ["w1"])
         tt(T.W[:, 0:16], T.w1[:], T.ex[:, 0:16], op.add, ["w1", "ex0"], ["V0"])
-        tt(T.W[:, 16:32], T.W[:, 0:16], T.ex[:, 16:32], op.add, ["V0", "ex1"], ["U0"])
+        tt(T.W[:, 49:80:2], T.W[:, 0:16], T.ex[:, 16:32], op.add, ["V0", "ex1"], ["U0"])
         tt(T.f1[:], T.gx[:, 15:C:16], T.gx[:, C + 15:2 * C:16], op.add, ["gx0", "gx1"], ["f1"])
         tt(T.f2[:], T.f1[:], T.gx[:, 2 * C + 15:3 * C:16], op.add, ["gx2", "f1"], ["f2"])
         ts(T.f1[:], T.f2[:], -float(C), None, op.mult, None, ["f2"], ["f1"])
@@ -656,26 +681,52 @@ def rank_program(g, core, T, topo):
         act(T.KS[:, 3:512:4], PS(2, 0, A), AF.Copy, [], ["KS3"], [2], c=A)
         BK = ["Bh0", "Bh1", "Bh2", "Bh3"]
         KK = ["KS%d" % a for a in (0, 1, 2, 3, 512, 513, 514, 515)]
+        KK2 = [k.replace("KS", "KB") for k in KK]
+        tt(T.Bm4[:], PS(1, 0, A), T.Mk4[:, 0:A], op.min, ["Mk4"], ["Bm4"], [1], c=A)
+        scan(T.hold4[:], T.Mk4[:, A:2 * A], T.Bm4[:], -H, op.min, op.max, ["K4", "Bm4"], ["hold4"], c=A)
+        for n in range(8):
+            for j in range(4):
+                view, p = T.Rt[:, 512 * n + j:512 * n + 512:4], T.hold4[:, 16 * n + 4 * j + 3:16 * n + 4 * j + 4]
+                if 4 * n + j in ON_VECTOR:
+                    ts(view, PS(1, 0, A), p, None, op.is_lt, None, ["hold4"], ["Rt%d%d" % (n, j)], [1], c=A)
+                else:
+                    act(view, PS(2, 0, A), AF.Sign, ["hold4"], ["Rt%d%d" % (n, j)], [2], c=A, bias=p, scale=-1.0)
+            quant(T.qK[:, A * n:A * n + A], T.sK[:, A * n:A * n + A], T.Rt[:, 512 * n:512 * n + 512], A,
+                  ["Rt%d%d" % (n, j) for j in range(4)], ["qK%d" % n])
+            mm(3, A, T.qG4[:], T.sG4[:], T.qK[:, A * n:A * n + A], T.sK[:, A * n:A * n + A], ["qG4", "qK%d" % n], n == 0, n == 7)
         for t in range(NT):
             if t == 0:
                 scan(T.pm[:], PS(1, 0, A), T.NEG[:], -H, op.max, op.max, ["NEG"], ["pm"], [1], c=A)
-            else:
+            elif t <= SWITCH:
                 scan(T.pm[:], T.KO[:, 3:512:4], T.NEG[:], -H, op.max, op.max, ["NEG", "KO"], ["pm"], c=A)
+            else:
+                scan(T.pb[:], T.KP[:, 3:512:4], T.KP[:, 3:512:4], -H, op.max, op.max, ["KP"], ["pb"], c=A // 2)
+                scan(T.drift[:, 0:A + 3], T.four[:, 0:A + 3], T.KP[:, 3:524:4], -H, op.add, op.max,
+                     ["four", "k40", "k41", "k42", "KP", "KPe"], ["drift"], c=A + 3)
             e = T.ee[:, t:t + 1]
             offE, offS, offT = [T.offE[:, 6 * t + 2 * j:6 * t + 2 * j + 1] for j in range(3)]
             ok = "off%d" % t
-            act(T.st[:], T.pm[:], AF.Sign, ["pm"], ["st", "ee%d" % t], c=A, bias=T.pm[:, A - 1:A], scale=-1.0, accum_out=e)
-            ts(T.offE[:, 6 * t:6 * t + 6:2], T.k3[:, 0:3], e, 4.0, op.add, op.mult, ["ee%d" % t, "k30", "k31", "k32"], [ok])
-            V, vk, U, uk = (T.W[:, 0:16], "V0", T.W[:, 16:32], "U0") if t == 0 else (T.W[:, 32:48], "V1", T.W[:, 48:64], "U1")
-            if t < NT - 1:
+            if t <= SWITCH:
+                act(T.st[:], T.pm[:], AF.Sign, ["pm"], ["st", "ee%d" % t], c=A, bias=T.pm[:, A - 1:A], scale=-1.0, accum_out=e)
+                ts(T.offE[:, 6 * t:6 * t + 6:2], T.k3[:, 0:3], e, 4.0, op.add, op.mult, ["ee%d" % t, "k30", "k31", "k32"], [ok])
+            else:
+                ts(T.offE[:, 6 * t:6 * t + 6:2], T.drift[:, A:A + 3], T.pb[:, A - 1:A], -1.0, op.subtract, op.mult,
+                   ["drift", "pb"], [ok])
+            U, uk = (T.W[:, 49:80:2], "U0") if t == 0 else (T.W[:, 81:112:2], "U1")
+            KO, kk = (T.KO[:], "KO") if t < SWITCH else (T.KP[:, 0:4 * A], "KP")
+            if t < SWITCH:
                 cp(T.KS[:].indirect(offE), U, [ok, uk], KK, c=("scatter", 16, 50))
-                scan(T.KO[:], T.KS[:, 512:1024], T.KS[:, 0:512], 0.0, op.add, op.min, KK, ["KO"], c=4 * A)
+                scan(KO, T.KS[:, 512:1024], T.KS[:, 0:512], 0.0, op.add, op.min, KK, [kk], c=4 * A)
+            if t == SWITCH:
+                act(T.KB[:, 3:512:4], PS(3, 0, A), AF.Copy, [], ["KB3"], [3], c=A, scale=-512.0)
+            if t < NT - 1:
+                cp(T.KB[:].indirect(offE), U, [ok, uk], KK2, c=("scatter", 16, 50))
+            if SWITCH <= t < NT - 1:
+                scan(KO, T.KB[:, 512:1024], T.KB[:, 0:512], 0.0, op.add, op.min, KK2, [kk], c=2 * A)
             if t < NT - 2:
-                act(T.sv[:], T.KO[:].indirect(offS), AF.Relu, ["KO", ok], ["sv"], c=gat(16), bias=1.0, scale=2.0 / BITE)
-                tt(T.W[:, 64:80], T.sv[:], V, op.mult, ["sv", vk], ["W2"])
-                tt(T.W[:, 48:64], T.W[:, 64:80], T.W[:, 16:32], op.add, ["W2", "U0"], ["U1"])
-                if t < NT - 3:
-                    tt(T.W[:, 32:48], T.W[:, 64:80], T.W[:, 0:16], op.add, ["W2", "V0"], ["V1"])
+                tt(T.W[:, 17:48:2], U, T.W[:, 0:16], op.add, [uk, "V0"], ["Wa1"])
+                act(T.W[:, 48:80:2], KO.indirect(offS), AF.Identity, [kk, ok, "col2"], ["Wb0"], c=gat(16), bias=col(2), scale=-2.0 ** 11)
+                scan(T.W[:, 80:112], T.W[:, 16:48], T.W[:, 48:80], 0.0, op.max, op.min, ["Wa0", "Wa1", "Wb0", "U0"], ["U1"])
             out = T.tab[:, t:16 * TS_:TS_]
             src = T.Bh[:].indirect(offT)
             if t == NT - 1:

from concourse.bass import DstId, RemoteDMATransfer
from concourse.mybir import dt, AluOpType, AxisListType, ActivationFunctionType

C, A, NT = 288, 128, 7
HC = C // 2
STEPS = [4, 1, 2]
H = 1.0e29
BIG = float(2 ** 20)
CK = 448
TS_ = CK // 4
F32, BF, I32, U16, X4, U8 = "float32", "bfloat16", "int32", "uint16", "float8_e4m3fn_x4", "uint8"
PART = [(0, 160), (160, C)]
NL = PART[0][1] // 16
UPPER = [[10, 17, 16, 15], [14, 13, 12, 11]]
INNER = [[(2, 0, 2), (9, 2, 9), (1, 9, 10)], [(1, 0, 1), (8, 1, 8), (0, 8, 10)],
         [(7, 0, 7)], [(6, 0, 6)], [(5, 0, 5)], [(4, 0, 4)], [(3, 0, 3)]]
TW = [288, 224, 160, 128]
T0 = [0, 288, 512, 672]
ZERO = [240, 176, 112, 48]
UP0 = 96
ON_SCALAR = (10, 11, 12, 13)
ZCUT = [[("s", 0, 16), ("s", 16, 32), ("v", 32, 40)], [("v", 40, 72)]]
PACES = [dict(cycle=0.83, gather=1.3, scatter=2.5, product=1.2, one=1.0, hop=200, dma=1500, first=3300, trip=2200),
         dict(cycle=1.0, gather=1.56, scatter=3.8, product=1.5, one=1.0, hop=200, dma=1700, first=3800, trip=2600),
         dict(cycle=1.2, gather=1.9, scatter=5.0, product=1.8, one=1.0, hop=180, dma=1900, first=4500, trip=3200)]
SWEEPS, SHAKE, TRIES, SEED, SLACK = 1500, 0.12, 10000, 1, 60
SWITCH = 3
ON_VECTOR = (3, 7, 11, 15)
BITE = float(2 ** 97)
ORDER = []


def sb(n, d):
    return ("sbuf", [128, n], d)


SCRATCH = {
    "ps": ("psum", [128, 4096], F32),
    "X": sb(4 * C, BF), "Y": sb(4 * C, BF), "Xh": sb(4 * C, BF), "Z": sb(4 * C, BF), "M": sb(4 * A, BF),
    "ub": sb(512, BF), "vb": sb(512, BF),
    "qU": sb(128, X4), "sU": sb(128, U8), "qV": sb(128, X4), "sV": sb(128, U8),
    "qR": sb(768, X4), "sR": sb(768, U8), "qW": sb(512, X4), "sW": sb(512, U8),
    "qX": sb(C, X4), "sX": sb(C, U8), "qZ": sb(C, X4), "sZ": sb(C, U8),
    "Gt": sb(512, BF), "qG": sb(128, X4), "sG": sb(128, U8),
    "Et": sb(2048, BF), "qE": sb(512, X4), "sE": sb(512, U8), "ones": sb(512, BF),
    "ip": sb(8, I32), "fp": sb(8, F32), "col": sb(24, F32), "s16": sb(192, F32), "offQ": sb(18, U16),
    "ofu": sb(48, F32), "offU": sb(48, U16),
    "Mk": sb(160, F32), "K16": sb(160, F32), "Kd": sb(160, BF), "A16": sb(C, F32), "A16f": sb(C, BF), "A4": sb(C, F32),
    "val": sb(C, F32), "m16": sb(18, F32), "Rc": sb(18, F32), "IC": sb(18, F32),
    "Bm": sb(C, F32), "hold": sb(C, F32), "rel": sb(2448, F32), "junk": sb(2448, BF), "rows": sb(30, F32),
    "dseg": sb(C, BF), "R1": sb(18, F32), "R2": sb(18, F32), "ext": sb(C, F32), "ex2": sb(A, F32), "offP": sb(20, U16),
    "Tt": sb(4 * 800, BF), "qT": sb(800, X4), "sT": sb(800, U8),
    "win": sb(C, F32), "offM": sb(32, U16), "c0": sb(C, F32),
    "m01": sb(C, F32), "m012": sb(C, F32), "mx": sb(C, F32), "gf": sb(3 * C, BF), "gx": sb(3 * C, BF),
    "Lw": sb(5 * C, F32), "offW": sb(2, U16), "wlo": sb(16, F32), "w1": sb(16, F32), "W": sb(112, F32),
    "ex": sb(32, F32), "kp": sb(16, F32), "k3": sb(4, F32), "four": sb(A + 4, F32), "drift": sb(A + 4, F32), "Zo": sb(4 * C, BF),
    "f1": sb(18, F32), "f2": sb(18, F32), "offK": sb(18, U16), "vlo": sb(C, F32), "vv": sb(C, F32), "v4": sb(C, F32),
    "z1": sb(72, F32), "z2": sb(72, I32), "offZ": sb(72, U16),
    "KS": sb(20 * A, F32), "KO": sb(4 * A, F32), "NEG": sb(128, F32), "pm": sb(128, F32), "st": sb(128, F32), "ee": sb(8, F32),
    "offE": sb(6 * NT, U16),
    "Bh": sb(512, BF), "tab": sb(16 * TS_, BF), "tabE": sb(16 * TS_, BF), "iq": sb(512, BF),
    "olw": sb(4 * C, F32),
    "Mk4": sb(2 * A, F32), "Bm4": sb(A, F32), "hold4": sb(A, F32), "Rt": sb(32 * A, BF), "qK": sb(8 * A, X4),
    "sK": sb(8 * A, U8), "G4": sb(512, BF), "qG4": sb(A, X4), "sG4": sb(A, U8),
    "KB": sb(20 * A, BF), "KP": sb(4 * A + 16, BF), "pb": sb(A, BF),
}
for _r in range(3):
    for _n in ("qM", "qH", "qL"):
        SCRATCH["%s%d" % (_n, _r)] = sb(A, X4)
    for _n in ("sM", "sH", "sL"):
        SCRATCH["%s%d" % (_n, _r)] = sb(A, U8)

POOL = {"v": 55, "s": 40, "p": 16, "g": 16, "d": 16}
SEMAPHORES = ["loc"] + ["arr%d" % r for r in range(3)] + ["hop%d" % r for r in range(3)]
for _q in POOL:
    SEMAPHORES += ["%s%d" % (_q, i) for i in range(POOL[_q])]


def helpers(topo, src, dst):
    can = [h for h in topo.cores_of(src) if h != src and topo.may_write(h, dst)]
    near = [h for h in can if topo.die(h) == topo.die(src)]
    far = [h for h in can if topo.die(h) != topo.die(src)]
    return near[0], far[0]


def helper_program(g, core, T, topo):
    own = [c for c in T.cores if core in topo.cores_of(c)]
    if not own:
        return
    src = own[0]
    rank = T.rank_of(src)
    sent = 0
    for r, step in enumerate(STEPS):
        dst = T.cores[rank ^ step]
        hs = helpers(topo, src, dst)
        if core not in hs:
            continue
        k = hs.index(core)
        n_in = len(topo.engines(src, core))
        rid, pid = topo.addr(dst, core)
        mask = topo.mask(core, dst)
        g.wait_ge(T.sem["hop%d" % r], n_in)
        if k == 0:
            a = T["qH%d" % r][:].bitcast(dt.uint8)
            b = T["qL%d" % r][:].bitcast(dt.uint8)
        else:
            a = T["sH%d" % r][:]
            b = T["sL%d" % r][:]
        g.remote_dma(b, a, T.sem["arr%d" % r], T.sem.loc, pid, rid, mask)
        sent += len(topo.engines(core, dst))
    if sent:
        g.wait_ge(T.sem.loc, sent)


def depend(ops, order=False):
    last_w, readers, bank, out = {}, {}, {}, []
    for i, (q, fn, rd, wr, bk, ext, dma, c) in enumerate(ops):
        deps = set()
        rd = [k for k in rd if (k[0] == "~") == order]
        wr = [k for k in wr if (k[0] == "~") == order]
        for k in rd:
            if k in last_w:
                deps.add(last_w[k])
        for k in wr:
            if k in last_w:
                deps.add(last_w[k])
            deps.update(readers.get(k, []))
        for b in ([] if order else bk):
            now, before = bank.get(b, ([], []))
            if now and ops[now[0]][0] != q:
                now, before = [], now
            deps.update(before)
            bank[b] = (now + [i], before)
        out.append(deps)
        if fn is not None:
            for k in rd:
                readers.setdefault(k, []).append(i)
        for k in wr:
            last_w[k] = i
            readers[k] = []
    return out


def length(c, p):
    kind, n, fixed = c
    if kind == "dma":
        return 60.0
    if kind == "":
        return fixed + max(n, 64) * p["cycle"]
    return fixed + n * p[kind] * p["cycle"]


def arrange(ops):
    n = len(ops)
    pred = [[(j, "dma" if ops[j][6] else "hop") for j in d] for d in depend(ops)]
    for i, d in enumerate(depend(ops, True)):
        pred[i] += [(j, "") for j in d]
    prev, sends = {}, {}
    for i, (q, fn, rd, wr, bk, ext, dma, c) in enumerate(ops):
        keys = [q] if q in "gy" else [("p", b) for b in bk] if q == "p" else []
        for k in keys:
            if k in prev:
                pred[i].append((prev[k], ""))
            prev[k] = i
        for k in rd:
            if q == "g" and k.startswith("qM"):
                sends.setdefault("arr" + k[2:], i)
        for name, val in ext:
            if name in sends:
                pred[i].append((sends[name], "first" if name == "arr0" else "trip"))
    queue = [o[0] for o in ops]
    above = [0] * n
    for i in range(n):
        for j, lat in pred[i]:
            above[i] |= above[j] | 1 << j
    for i in range(n):
        pred[i] = [(j, lat) for j, lat in pred[i] if lat not in ("", "hop") or not any(above[k] >> j & 1 and l2 for k, l2 in pred[i])]
    plans = []
    for p in PACES:
        wait = lambda j, lat: 0 if not lat else p[lat] + (p["hop"] + ops[j][7][1] if lat == "dma" else 0)
        plans.append(([length(o[7], p) for o in ops], [[(j, wait(j, lat)) for j, lat in d] for d in pred]))
    cost, pre = plans[1]
    tail = list(cost)
    for i in range(n - 1, -1, -1):
        for j, lat in pre[i]:
            tail[j] = max(tail[j], cost[j] + lat + tail[i])
    end = [0.0] * n

    def fill(order, cost, pre):
        busy = {q: [] for q in "vspgy"}
        for i in order:
            t, c, line = max([end[j] + lat for j, lat in pre[i]] + [0.0]), cost[i], busy[queue[i]]
            k = len(line)
            while k and line[k - 1][1] > t:
                k -= 1
            while k < len(line) and t + c > line[k][0]:
                t = max(t, line[k][1])
                k += 1
            end[i] = t + c
            line.insert(k, (t, t + c))
        place = {i: k for k, i in enumerate(order)}
        return sorted(order, key=lambda i: (-end[i], -place[i]))

    def play(order):
        total, holds = 0.0, []
        for cost, pre in plans:
            last = {q: -1 for q in "vspgy"}
            why = [-1] * n
            for i in order:
                w = last[queue[i]]
                t = end[w] if w >= 0 else 0.0
                for j, lat in pre[i]:
                    if end[j] + lat > t:
                        t, w = end[j] + lat, j
                end[i] = t + cost[i]
                why[i] = w
                last[queue[i]] = i
            i = max(range(n), key=lambda i: end[i])
            total += end[i]
            while why[i] >= 0:
                if not above[i] >> why[i] & 1:
                    holds.append((why[i], i))
                i = why[i]
        return total, holds, order

    posts = []
    for cost, pre in plans:
        posts.append([[] for i in range(n)])
        for i in range(n):
            for j, lat in pre[i]:
                posts[-1][j].append((i, lat))
    now = best = play(fill(sorted(range(n), key=lambda i: (-tail[i], i)), *plans[1])[::-1])
    seed = SEED
    for k in range(SWEEPS):
        cost = []
        for c in plans[k % 3][0]:
            seed = (seed * 1103515245 + 12345) % 2 ** 31
            cost.append(c * (1 + SHAKE * ((seed >> 8) % 64 - 32) / 32))
        got = play(fill(fill(now[2][::-1], cost, posts[k % 3]), cost, plans[k % 3][1])[::-1])
        if got[0] <= now[0] + 10 * SLACK * (1 - k / SWEEPS):
            now = got
            if now[0] < best[0]:
                best = now
    now = best
    for k in range(TRIES):
        seed = (seed * 1103515245 + 12345) % 2 ** 31
        a, b = now[1][(seed >> 8) % len(now[1])]
        order = now[2]
        pa, pb = order.index(a), order.index(b)
        reach = (seed >> 5) % 8 - 3
        if seed >> 4 & 1:
            for m in range(pb + 1, n):
                if reach <= 0 or above[order[m]] >> a & 1 and queue[order[m]] == queue[a]:
                    break
                if queue[order[m]] == queue[a]:
                    pb, reach = m, reach - 1
            mid = order[pa:pb + 1]
            new = [i for i in mid if i != a and not above[i] >> a & 1] + [i for i in mid if i == a or above[i] >> a & 1]
        else:
            for m in range(pa - 1, -1, -1):
                if reach <= 0 or above[b] >> order[m] & 1 and queue[order[m]] == queue[a]:
                    break
                if queue[order[m]] == queue[a]:
                    pa, reach = m, reach - 1
            mid = order[pa:pb + 1]
            new = [i for i in mid if i == b or above[b] >> i & 1] + [i for i in mid if i != b and not above[b] >> i & 1]
        got = play(order[:pa] + new + order[pb + 1:])
        if got[0] <= now[0] + SLACK * (1 - k / TRIES) * ((seed >> 12) % 8) / 4:
            now = got
            if now[0] < best[0]:
                best = now
    return best[2]


def emit(g, T, ops):
    Q = {"v": g.vector, "s": g.scalar, "p": g.tensor, "g": g, "y": g.sync}
    known = {q: 0 for q in Q}
    closure, at_issue, waits, signal = [], [], [], set()
    for i, deps in enumerate(depend(ops)):
        q = ops[i][0]
        need = [j for j in deps if not known[q] >> j & 1]
        need = [j for j in need if not any(j2 != j and closure[j2] >> j & 1 for j2 in need)]
        for j in need:
            known[q] |= closure[j]
            signal.add(j)
        waits.append(sorted(need))
        at_issue.append(known[q])
        closure.append(known[q] | 1 << i)
    user = {q: [] for q in POOL}
    count, mark = {}, {}
    for i, (q, fn, rd, wr, bk, ext, dma, c) in enumerate(ops):
        for j in waits[i]:
            Q[q].wait_ge(T.sem[mark[j][0]], mark[j][1])
        for name, val in ext:
            Q[q].wait_ge(T.sem[name], val)
        if fn is None:
            continue
        ins = fn(Q[q])
        if i in signal:
            pool = "d" if dma else q
            free = [n for n, j in enumerate(user[pool]) if not dma and at_issue[i] >> j & 1]
            if free:
                n = free[0]
                user[pool][n] = i
            else:
                n = len(user[pool])
                user[pool].append(i)
            name = "%s%d" % (pool, n)
            inc = 16 if dma else 1
            count[name] = count.get(name, 0) + inc
            mark[i] = (name, count[name])
            ins.then_inc(T.sem[name], inc)


def rank_program(g, core, T, topo):
    rank = T.rank_of(core)
    if rank is None:
        helper_program(g, core, T, topo)
        return
    op = AluOpType
    AF = ActivationFunctionType
    ops = []

    def add(q, fn, rd=(), wr=(), bk=(), ext=(), dma=False, c=64):
        ops.append((q, fn, list(rd), list(wr), list(bk), list(ext), dma, c if isinstance(c, tuple) else ("", c, 0)))

    def ts(out, in0, s1, s2, o0, o1, rd, wr, bk=(), c=64):
        if o1 is None:
            add("v", lambda e: e.tensor_scalar(out, in0, s1, None, o0), rd, wr, bk, c=c)
        else:
            add("v", lambda e: e.tensor_scalar(out, in0, s1, s2, o0, o1), rd, wr, bk, c=c)

    def tt(out, a, b, o, rd, wr, bk=(), c=64):
        add("v", lambda e: e.tensor_tensor(out, a, b, o), rd, wr, bk, c=c)

    def cp(out, a, rd, wr, bk=(), c=64):
        add("v", lambda e: e.tensor_copy(out, a), rd, wr, bk, c=c)

    def ms(out, v, wr, c=64):
        add("v", lambda e: e.memset(out, v), (), wr, c=c)

    def scan(out, d0, d1, init, o0, o1, rd, wr, bk=(), c=64):
        add("v", lambda e: e.tensor_tensor_scan(out, d0, d1, init, o0, o1), rd, wr, bk, c=c)

    def quant(qc, sc, a, n, rd, wr):
        add("v", lambda e: e.quantize_mx(qc, sc, a), rd, wr, c=15 + 1.06 * n)

    def act(out, a, f, rd, wr, bk=(), c=64, **kw):
        kind, n, fixed = c if isinstance(c, tuple) else ("", c, 0)
        add("s", lambda e: e.activation(out, a, f, **kw), rd, wr, bk, c=(kind, n, fixed + 20 * ("accum_out" in kw) + 15 * (kind != "")))

    def mm(b, n, lc, ls, rc, rs, rd, start=True, stop=True, ext=()):
        add("p", lambda e: e.matmul_mx(T.ps[:, 512 * b:512 * b + n], lc, ls, rc, rs, start, stop), rd, (), [b], ext,
            c=("product", n + 16, 0))

    def iota(out, pat, base, cm, wr, small=True):
        n = 1
        for s, k in pat:
            n *= k
        if small:
            add("g", lambda e: e.iota(out, pat, base, cm, allow_small_or_imprecise_dtypes=True), (), wr, c=("one", 2 * n, 130))
        else:
            add("g", lambda e: e.iota(out, pat, base, cm), (), wr, c=("one", 2 * n, 130))

    def dma(q, out, a, rd, wr, late=0):
        add(q, lambda e: e.dma_start(out, a), rd, wr, dma=True, c=("dma", late, 0))

    def gat(n):
        return "gather", n, 50

    def PS(b, a, n):
        return T.ps[:, 512 * b + a:512 * b + n]

    def col(i):
        return T.col[:, i:i + 1]

    def s16(i):
        return T.s16[:, 16 * i:16 * i + 16]

    def quant_x(h):
        a, b = PART[h]
        quant(T.qX[:, a:b], T.sX[:, a:b], T.X[:, 4 * a:4 * b], b - a, XK[4 * h:4 * h + 4], ["qX%d" % h])

    XK = ["X%d%d" % (h, b) for h in range(2) for b in range(4)]
    YK = ["Y%d%d" % (h, b) for h in range(2) for b in range(4)]
    dma("y", T.ub[:], T.u[:], (), ["ub"])
    dma("y", T.X[:, 64 * NL:], T.x[:, 64 * NL:], (), XK[4:], 400)
    dma("y", T.X[:, 0:64 * NL], T.x[:, 0:64 * NL], (), XK[:4], 800)
    add("y", None, XK)
    dma("y", T.qW[:].bitcast(dt.uint8), T.wc[:], (), ["qW"])
    dma("y", T.sW[:], T.ws[:], (), ["sW"])
    dma("y", T.vb[:], T.v[:], (), ["vb"])
    iota(T.ip[:, 0:2], [[15, 2]], 0, 1, ["ip0"], small=False)
    iota(T.ofu[:, 0:8], [[16, 8]], 0, 0, ["ofu0"])
    iota(s16(0), [[1, 16]], 0, 0, ["s0"])
    iota(T.m16[:], [[16, 18]], 0, 0, ["m16"])
    iota(s16(1), [[0, 4], [1, 4]], 0, 0, ["s1"])
    iota(T.ofu[:, 8:40], [[1, 4], [16, 8]], 4, 0, ["ofu1"])
    iota(T.ofu[:, 40:48], [[16, 8]], 8, 0, ["ofu2"])
    iota(T.val[:], [[4, C]], 0, 0, ["val"])
    iota(T.kp[:], [[1, 4], [0, 4]], 0, 0, ["kp"])
    iota(T.Lw[:, 4 * C:5 * C], [[1, C]], 1 + 6 * CK, 0, ["L4"])
    iota(T.Lw[:, 0:C], [[0, C]], 0, 0, ["L0"])
    for t, a in enumerate(ZERO):
        ms(T.Tt[:, 4 * (T0[t] + a):4 * (T0[t] + TW[t])], 0.0, ["T%s%d" % (t, e) for e in range(4)], c=2 * (TW[t] - a))
    ms(T.K16[:], H, ["K16"], c=160)
    ts(T.ip[:, 2:4], T.ip[:, 0:2], 15, None, op.bitwise_and, None, ["ip0"], ["ip2"])
    ts(T.ip[:, 4:5], T.ip[:, 0:1], 2, 3, op.logical_shift_right, op.bitwise_and, ["ip0"], ["ip4"])
    ts(T.ip[:, 5:6], T.ip[:, 0:1], 3, None, op.bitwise_and, None, ["ip0"], ["ip5"])
    ts(T.ip[:, 6:7], T.ip[:, 0:1], 112, None, op.bitwise_and, None, ["ip0"], ["ip6"])
    ms(T.ones[:], 1.0, ["ones"], c=256)
    cp(T.fp[:, 0:5], T.ip[:, 2:7], ["ip2", "ip4", "ip5", "ip6"], ["fp"])
    qc, qm, kc, rc_, gc_ = [T.fp[:, i:i + 1] for i in range(5)]
    ms(T.K16[:, 0:160:16], -H, ["K16"])
    ts(s16(5), s16(0), qc, 0.5, op.is_equal, op.subtract, ["s0", "fp"], ["s5"])
    ts(T.offQ[:], T.m16[:], 0.0, qc, op.mult, op.add, ["m16", "fp"], ["offQ"])
    ts(T.col[:, 16:24], T.ofu[:, 0:8], gc_, None, op.is_equal, None, ["ofu0", "fp"], ["gcol"])
    ts(s16(2), s16(5), 2 * H, None, op.mult, None, ["s5"], ["s2"])
    cp(T.offU[:, 0:8], T.ofu[:, 0:8], ["ofu0"], ["offU0"])
    ts(s16(6), s16(0), qc, 1024.0, op.is_equal, op.mult, ["s0", "fp"], ["s6"])
    ts(s16(7), s16(0), qm, -4096.0, op.is_equal, op.mult, ["s0", "fp"], ["s7"])
    ms(T.Kd[:], 1.0, ["Kd"], c=72)
    tt(s16(3), s16(6), s16(7), op.add, ["s6", "s7"], ["s3"])
    ts(col(3), kc, 1.0, None, op.add, None, ["fp"], ["col3"])
    ts(col(4), kc, 2.5, 4096.0, op.is_lt, op.mult, ["fp"], ["col4"])
    ts(col(0), qc, -1.0, 15.0 - 1024.0, op.mult, op.add, ["fp"], ["col0"])
    ts(s16(8), s16(1), kc, -16384.0, op.is_equal, op.mult, ["s1", "fp"], ["s8"])
    ts(s16(9), s16(1), col(3), 4096.0, op.is_equal, op.mult, ["s1", "col3"], ["s9"])
    ms(T.Kd[:, 0:160:16], 0.0, ["Kd"])
    ts(T.R2[:, 0:NL], T.m16[:, 0:NL], 32.0, 112.0, op.max, op.min, ["m16"], ["R2"])
    tt(s16(4), s16(8), s16(9), op.add, ["s8", "s9"], ["s4"])
    ts(T.Rc[:, 0:NL], T.R2[:, 0:NL], col(0), T.s16[:, 63:64], op.add, op.add, ["R2", "col0", "s3"], ["Rc0"])
    ts(T.Rc[:, NL:], T.m16[:, NL:], col(0), T.s16[:, 63:64], op.add, op.add, ["m16", "col0", "s3"], ["Rc1"])
    ts(col(1), T.s16[:, 63:64], 0.0, -1.0, op.min, op.mult, ["s3"], ["col1"])
    ts(col(14), col(4), rc_, None, op.subtract, None, ["col4", "fp"], ["col14"])
    act(T.Mk[:], s16(2).indirect(T.offQ[:, 0:NL]), AF.Copy, ["s2", "offQ"], ["Mk"], c=gat(160))
    for j in range(8):
        act(T.Gt[:, 64 * j:64 * j + 64], T.ones[:, 0:64], AF.Copy, ["ones", "gcol"], ["Gt%d" % j], scale=col(16 + j))
    act(T.A16[:], s16(3).indirect(T.offQ[:]), AF.Copy, ["s3", "offQ"], ["A16"], c=gat(C))
    act(T.A4[:], s16(4).indirect(T.offQ[:]), AF.Copy, ["s4", "offQ"], ["A4"], c=gat(C))
    act(T.A16f[:], s16(3).indirect(T.offQ[:]), AF.Copy, ["s3", "offQ"], ["A16f"], c=gat(C), scale=1.0 / 512)
    quant(T.qG[:], T.sG[:], T.Gt[:], 128, ["Gt%d" % j for j in range(8)], ["qG"])
    ts(col(9), col(4), 4.0, None, op.add, None, ["col4"], ["col9"])
    ts(col(10), rc_, float(TS_), -1.0, op.mult, op.add, ["fp"], ["col10"])
    ts(col(11), col(1), -24.0 * C / 4096, 9.0 * C, op.mult, op.add, ["col1"], ["col11"])
    ts(T.offW[:, 0:1], kc, float(C), C - 1.0, op.mult, op.add, ["fp"], ["offW"])
    cp(T.offU[:, 8:40], T.ofu[:, 8:40], ["ofu1"], ["offU1"])
    ts(T.offU[:, 40:48], T.ofu[:, 40:48], kc, None, op.add, None, ["ofu2", "fp"], ["offU5"])
    ms(T.NEG[:], -H, ["NEG"], c=128)
    ts(T.IC[:], T.m16[:], col(11), qc, op.add, op.add, ["m16", "col11", "fp"], ["IC"])
    ts(col(12), col(10), col(4), None, op.subtract, None, ["col10", "col4"], ["col12"])
    ts(col(7), col(1), -1.0 / 32, 128.0, op.mult, op.add, ["col1"], ["col7"])
    ts(col(8), rc_, 128.0, col(7), op.mult, op.add, ["col7", "fp"], ["col8"])
    ts(T.k3[:, 0:1], kc, 0.25, col(8), op.mult, op.add, ["col8", "fp"], ["k30"])
    ms(T.k3[:, 1:2], 0.75, ["k31"])
    ts(T.k3[:, 2:3], rc_, 0.25, None, op.mult, None, ["fp"], ["k32"])
    ms(T.four[:, 0:A], 4.0, ["four"], c=A)
    ts(T.four[:, A:A + 1], T.k3[:, 0:1], -4.0, -4.0 * (A - 1), op.mult, op.add, ["k30"], ["k40"])
    for j in (1, 2):
        ts(T.four[:, A + j:A + j + 1], T.k3[:, j - 1:j], T.k3[:, j:j + 1], 4.0, op.subtract, op.mult, ["k30", "k31", "k32"], ["k4%d" % j])
    ms(T.KP[:, 4 * A:], -H, ["KPe"])
    ts(col(5), T.ones[:, 0:1], BITE, 95.5, op.mult, op.mult, ["ones"], ["col5"])
    ts(col(6), T.ones[:, 0:1], BITE, 2.0 ** 15, op.mult, op.mult, ["ones"], ["col6"])
    ts(col(2), T.ones[:, 0:1], BITE, -2.0 ** 9, op.mult, op.mult, ["ones"], ["col2"])
    act(T.W[:, 16:48:2], T.ones[:, 0:16], AF.Copy, ["ones", "col6"], ["Wa0"], scale=col(6))
    ts(T.ex[:, 0:16], T.kp[:], float(CK), BITE, op.mult, op.mult, ["kp"], ["ex0"])
    ts(T.ex[:, 16:32], T.kp[:], 0.0, col(5), op.is_equal, op.mult, ["kp", "col5"], ["ex1"])
    for a in (1, 2, 512):
        act(T.KS[:, a:a // 512 * 512 + 512:4], T.ones[:, 0:A], AF.Copy, ["ones", "col6"], ["KS%d" % a], c=A, scale=col(6))
    quant(T.qU[:], T.sU[:], T.ub[:], 128, ["ub"], ["qU"])
    quant(T.qV[:], T.sV[:], T.vb[:], 128, ["vb"], ["qV"])

    def pick(s):
        key = "offU%d" % (s if s in (0, 5) else 1)
        off = T.offU[:, 8 * s:8 * s + 8]
        add("v", lambda e: e.tensor_copy(T.qR[:, 128 * s:128 * s + 128].bitcast(dt.uint32), T.qU[:].bitcast(dt.uint32).indirect(off)),
            ["qU", key], ["qR%d" % s], c=gat(128))
        act(T.sR[:, 128 * s:128 * s + 128], T.sU[:].indirect(off), AF.Copy, ["qU", key], ["sR%d" % s], c=gat(128))
    for s in range(6):
        pick(s)

    def ur(s):
        return T.qR[:, 128 * s:128 * s + 128], T.sR[:, 128 * s:128 * s + 128]

    def e_tile(b):
        add("g", lambda e: e.affine_select(T.Et[:, 512 * b:512 * b + 512], T.ones[:], [[1, 128], [256, 4]], op.is_equal, 0.0,
                                           -256 * b, -1), ["ones"], ["Et%d" % b], c=("one", 1024, 170))
        quant(T.qE[:, 128 * b:128 * b + 128], T.sE[:, 128 * b:128 * b + 128], T.Et[:, 512 * b:512 * b + 512], 128,
              ["Et%d" % b], ["qE%d" % b])
    e_tile(0)
    e_tile(1)
    add("g", lambda e: e.affine_select(T.G4[:], T.ones[:], [[-4, 32], [0, 16]], op.is_ge, 0.0, 0, 1), ["ones"], ["G4"], c=("one", 1024, 170))
    add("g", lambda e: e.affine_select(T.G4[:], T.G4[:], [[4, 32], [0, 16]], op.is_ge, 0.0, 3, -1), ["G4"], ["G4"], c=("one", 1024, 170))
    quant(T.qG4[:], T.sG4[:], T.G4[:], 128, ["G4"], ["qG4"])
    ts(s16(10), s16(1), rc_, 0.5, op.is_equal, op.subtract, ["s1", "fp"], ["s10"])
    ts(s16(11), s16(10), 2 * H, None, op.mult, None, ["s10"], ["s11"])
    act(T.Mk4[:, 0:A], s16(11).indirect(T.offQ[:, 0:8]), AF.Copy, ["s11", "offQ"], ["Mk4"], c=gat(A))
    ms(T.Mk4[:, A:2 * A], H, ["K4"], c=A)
    ms(T.Mk4[:, A:2 * A:4], -H, ["K4"])
    for a in (1, 2, 512):
        act(T.KB[:, a:a // 512 * 512 + 512:4], T.ones[:, 0:A], AF.Copy, ["ones", "col6"], ["KB%d" % a], c=A, scale=col(6))

    n_loc = [0]

    def send(r, step):
        dst = T.cores[rank ^ step]
        hs = helpers(topo, core, dst)

        def hop(h, out, a):
            rid, pid = topo.addr(h, core)
            add("g", lambda e: e.remote_dma(out, a, T.sem["hop%d" % r], T.sem.loc, pid, rid, topo.mask(core, h)), ["qM%d" % r], c=200)
            n_loc[0] += len(topo.engines(core, h))
        hop(hs[0], T["qH%d" % r][:].bitcast(dt.uint8), T["qM%d" % r][:].bitcast(dt.uint8))
        hop(hs[1], T["sH%d" % r][:], T["sM%d" % r][:])
        return sum(len(topo.engines(h, core)) for h in helpers(topo, dst, core))

    QX = ["qX0", "qX1"]
    U0 = ["qR0", "sR0"]
    u0c, u0s = ur(0)
    CB = [3, 6, 7, 0]

    def slot(t, e, lo, hi):
        return T.Tt[:, 4 * T0[t] + 64 * lo + e:4 * T0[t] + 64 * hi:4], "T%s%d" % (t, e), "T%s%dw%d" % (t, e, lo)

    SB = [(4, 5), (0, 2)]

    def compare(m, lo, hi, t, e, j0, alone):
        h, n = int(lo >= NL), 16 * (hi - lo)
        view, zero, key = slot(t, e, lo, hi)
        p, pk, bank = T.hold[:, 16 * m + 15:16 * m + 16], "hold%d" % (m >= NL), SB[h][alone]
        s = PS(bank, 16 * (lo - NL * h), 16 * (hi - NL * h))
        if alone:
            act(T.rel[:, j0:j0 + n], s, AF.Relu, [pk], ["rel%d" % j0], [bank], c=n, bias=p, scale=-1.0)
            return "rel%d" % j0
        ts(view, s, p, None, op.is_le if lo > m else op.is_lt, None, [pk, zero], [key], [bank], c=n)
        return key

    def wins(lo, hi, t, e, j0, alone, row, rd):
        n = 16 * (hi - lo)
        view, zero, key = slot(t, e, lo, hi)
        if alone:
            act(view, T.rel[:, j0:j0 + n], AF.Sign, rd + [zero], [key, "rows%d" % row], c=n, accum_out=T.rows[:, row:row + 1])
            return [key]
        act(T.junk[:, j0:j0 + n], view, AF.Copy, rd, ["junk%d" % j0, "rows%d" % row], c=n, accum_out=T.rows[:, row:row + 1])
        return rd

    def pivots(h, t):
        a, b = PART[h]
        n, bank = b - a, SB[h][0]
        for bk in SB[h]:
            mm(bk, n, u0c, u0s, T.qX[:, a:b], T.sX[:, a:b], U0 + ["qX%d" % h])
        tt(T.Bm[:, a:b], PS(bank, 0, n), T.Mk[:, 0:n], op.min, ["Mk"], ["Bm%d" % h], [bank], c=n)
        scan(T.hold[:, a:b], T.K16[:, 0:n], T.Bm[:, a:b], -H, op.min, op.max, ["K16", "Bm%d" % h], ["hold%d" % h], c=n)
        view, zero, key = slot(t, 0, a // 16, b // 16)
        tt(view, PS(bank, 0, n), T.hold[:, a:b], op.is_le, ["hold%d" % h, zero], [key], [bank], c=n)
        scan(T.dseg[:, a:b], T.Kd[:, 0:n], view, 0.0, op.mult, op.add, ["Kd", key], ["dseg%d" % h], c=n // 2)
        tt(T.R1[:, a // 16:b // 16], T.Rc[:, a // 16:b // 16], T.dseg[:, a + 15:b:16], op.subtract, ["Rc%d" % h, "dseg%d" % h],
           ["R1%d" % h])
        return key

    def run0(m):
        return 8 * (m * (m - 1) - NL * (NL - 1))

    def upper_part():
        quant_x(1)
        got = {"own": pivots(1, 0)}
        for t, row in enumerate(UPPER):
            for e, m in enumerate(row):
                got[m] = [compare(m, NL, m, t, e, run0(m) + 16 * NL, m in ON_SCALAR)] if m > NL else []
        return got

    def sums(t, keys):
        a, b = T0[t], T0[t] + TW[t]
        quant(T.qT[:, a:b], T.sT[:, a:b], T.Tt[:, 4 * a:4 * b], TW[t], keys + ["T%s%d" % (t, e) for e in range(4)], ["qT%d" % t])
        if t < 2:
            mm(1, TW[t] - UP0, T.qG[:], T.sG[:], T.qT[:, a + UP0:b], T.sT[:, a + UP0:b], ["qG", "qT%d" % t], t == 0, t == 1)
        n = min(TW[t], 16 * NL)
        mm(2, n, T.qG[:], T.sG[:], T.qT[:, a:a + n], T.sT[:, a:a + n], ["qG", "qT%d" % t], t == 0, t == 3)

    def places(h, bank, first):
        a, b = PART[h]
        off = T.offP[:, a // 16:b // 16]
        tt(T.A16[:, a + 15:b:16], T.R1[:, a // 16:b // 16], T.rows[:, a // 16:b // 16], op.subtract,
           ["R1%d" % h, "A16"] + ["rows%d" % m for m in range(a // 16, b // 16)], ["A16%d" % h])
        scan(T.ext[:, a:b], PS(bank, first, first + b - a), T.A16[:, a:b], -4096.0, op.max, op.add, ["A16%d" % h], ["ext%d" % h],
             [bank], c=b - a)
        ts(off, T.ext[:, a + 15:b:16], col(1), None, op.add, None, ["ext%d" % h, "col1"], ["offP%d" % h])
        cp(T.win[:].indirect(off), T.val[:, a:b], ["offP%d" % h, "val"], ["win"], c=("scatter", b - a, 50))

    got = upper_part()
    quant_x(0)
    for r, step in enumerate(STEPS):
        last = r == len(STEPS) - 1
        own = pivots(0, 2)
        for k in range(4):
            mm(CB[k], C, ur(k + 1)[0], ur(k + 1)[1], T.qX[:], T.sX[:], ["qR%d" % (k + 1), "sR%d" % (k + 1)] + QX)
        for t, row in enumerate(UPPER):
            keys = [got["own"]] if t == 0 else []
            for e, m in enumerate(row):
                key = compare(m, 0, NL, t, e, run0(m), m in ON_SCALAR)
                keys += wins(0, m, t, e, run0(m), m in ON_SCALAR, m, got[m] + [key])
            sums(t, keys)
        keys, j0 = [[own], []], run0(18)
        for n, run in enumerate(INNER):
            t, e = 2 + (n + 1) // 4, (n + 1) % 4
            for m, lo, hi in run:
                key = compare(m, lo, hi, t, e, j0, (m, lo) in ON_SCALAR)
                keys[t - 2] += wins(lo, hi, t, e, j0, (m, lo) in ON_SCALAR, 18 if (m, lo) == (1, 9) else m, [key])
                j0 += 16 * (hi - lo)
        ts(T.R1[:, 1:2], T.R1[:, 1:2], T.rows[:, 18:19], None, op.subtract, None, ["R10", "rows18"], ["R10"])
        sums(2, keys[0])
        sums(3, keys[1])
        places(1, 1, 16 * NL - UP0)
        places(0, 2, 0)
        scan(T.ex2[:], T.A4[:, 0:A], T.win[:, 0:A], 0.0, op.add, op.max, ["A4", "win"], ["ex2"], c=A)
        ts(T.offM[:], T.ex2[:, 3:A:4], col(14), None, op.subtract, None, ["ex2", "col14"], ["offM"])
        cp(T.M[:, 0:256], T.X[:].indirect(T.offM[:, 0:16]), XK + ["offM"], ["M0"], c=gat(256))
        act(T.M[:, 256:512], T.X[:].indirect(T.offM[:, 16:32]), AF.Copy, XK + ["offM"], ["M1"], c=gat(256))
        quant(T["qM%d" % r][:], T["sM%d" % r][:], T.M[:], A, ["M0", "M1"], ["qM%d" % r])
        arr = [("arr%d" % r, send(r, step))]
        for a in (513, 514, 515):
            iota(T.KS[:, a:1024:4], [[0, A]], 0, 0, ["KS%d" % a])
        for a in (513, 514, 515):
            iota(T.KB[:, a:1024:4], [[0, A]], 0, 0, ["KB%d" % a])
        act(T.KS[:, 0:512:4], T.ones[:, 0:A], AF.Copy, ["ones", "col5"], ["KS0"], c=A, scale=col(5))
        act(T.KB[:, 0:512:4], T.ones[:, 0:A], AF.Copy, ["ones", "col5"], ["KB0"], c=A, scale=col(5))
        if r == 0:
            e_tile(2)
            e_tile(3)
            iota(T.iq[:], [[1, 128], [0, 4]], 0, 0, ["iq"])
        for j, (a, b) in enumerate(((0, 320), (320, 640), (640, 896), (896, 4 * C))):
            if r == 0:
                act(T.Y[:, a:b], T.X[:, a:b], AF.Copy, XK + ["offM"], YK[4 * (j // 2):4 * (j // 2) + 4], c=b - a, scale=32.0)
            act(T.Xh[:, a:b], T.X[:, a:b], AF.Copy, XK + ["offM"], ["Xh%d" % j], c=b - a, scale=0.5)
        act(T.c0[:], PS(CB[0], 0, C), AF.Copy, [], ["c0"], [CB[0]], c=C)
        for h in range(2):
            a, b = HC * h, HC * (h + 1)
            tt(T.m01[:, a:b], PS(CB[1], a, b), T.c0[:, a:b], op.max, ["c0"], ["m01%d" % h], [CB[1]], c=HC)
            tt(T.m012[:, a:b], PS(CB[2], a, b), T.m01[:, a:b], op.max, ["m01%d" % h], ["m012%d" % h], [CB[2]], c=HC)
            tt(T.mx[:, a:b], PS(CB[3], a, b), T.m012[:, a:b], op.max, ["m012%d" % h], ["mx%d" % h], [CB[3]], c=HC)
        tt(T.gf[:, 2 * C:3 * C], PS(CB[3], 0, C), T.m012[:], op.is_le, ["m0120", "m0121"], ["gf2"], [CB[3]], c=C)
        tt(T.gf[:, 0:C], PS(CB[0], 0, C), T.mx[:], op.is_ge, ["mx0", "mx1"], ["gf0"], [CB[0]], c=C)
        tt(T.gf[:, C:2 * C], T.m01[:], T.mx[:], op.is_ge, ["m010", "m011", "mx0", "mx1"], ["gf1"], c=2 * C)
        for j, c in ((2, 3 * CK), (0, 0), (1, CK)):
            scan(T.Lw[:, C * (j + 1):C * (j + 2)], T.gf[:, C * j:C * j + C], T.Lw[:, 0:C], float(c), op.add, op.add,
                 ["gf%d" % j, "L0"], ["L%d" % (j + 1)], c=C)
            scan(T.gx[:, C * j:C * j + C], T.gf[:, C * j:C * j + C], T.A16f[:], -8.0, op.max, op.add, ["A16f", "gf%d" % j],
                 ["gx%d" % j], c=HC)
        LK = ["L0", "L1", "L2", "L3", "L4"]
        act(T.wlo[:], T.Lw[:, 0:4 * C].indirect(T.offW[:, 0:1]), AF.Copy, LK + ["offW"], ["wlo"], c=gat(16))
        tt(T.w1[:], T.Lw[:, C:5 * C].indirect(T.offW[:, 0:1]), T.wlo[:], op.subtract, LK + ["offW", "wlo"], ["w1"], c=gat(16))
        ts(T.w1[:], T.w1[:], -BITE, None, op.mult, None, ["w1"], ["w1"])
        tt(T.W[:, 0:16], T.w1[:], T.ex[:, 0:16], op.add, ["w1", "ex0"], ["V0"])
        tt(T.W[:, 49:80:2], T.W[:, 0:16], T.ex[:, 16:32], op.add, ["V0", "ex1"], ["U0"])
        tt(T.f1[:], T.gx[:, 15:C:16], T.gx[:, C + 15:2 * C:16], op.add, ["gx0", "gx1"], ["f1"])
        tt(T.f2[:], T.f1[:], T.gx[:, 2 * C + 15:3 * C:16], op.add, ["gx2", "f1"], ["f2"])
        ts(T.f1[:], T.f2[:], -float(C), None, op.mult, None, ["f2"], ["f1"])
        tt(T.f2[:], T.f1[:], T.IC[:], op.add, ["f1", "IC"], ["f2"])
        cp(T.offK[:], T.f2[:], ["f2"], ["offK"])
        act(T.vlo[:], T.Lw[:, 0:4 * C].indirect(T.offK[:]), AF.Copy, LK + ["offK"], ["vlo"], c=gat(C))
        for j in range(3):
            a, b = 96 * j, 96 * j + 96
            tt(T.vv[:, a:b], T.Lw[:, C:5 * C].indirect(T.offK[:, 6 * j:6 * j + 6]), T.vlo[:, a:b], op.subtract,
               LK + ["offK", "vlo"], ["vv%d" % j], c=gat(96))
        for h in range(2):
            a, b = HC * h, HC * (h + 1)
            scan(T.v4[:, a:b], T.A4[:, a:b], T.vv[:, a:b], 0.0, op.add, op.max, ["A4", "vv%d" % h, "vv%d" % (h + 1)],
                 ["v4%d" % h], c=HC)
        ts(T.z1[:], T.v4[:, 3:C:4], col(9), 1.0 / 7, op.subtract, op.mult, ["v40", "v41", "col9"], ["z1"], c=72)
        cp(T.z2[:], T.z1[:], ["z1"], ["z2"], c=72)
        ts(T.z2[:], T.z2[:], 63, None, op.bitwise_and, None, ["z2"], ["z2"], c=72)
        ts(T.z1[:], T.z2[:], -7.0, col(12), op.mult, op.add, ["z2", "col12"], ["z1"], c=72)
        tt(T.z1[:], T.z1[:], T.v4[:, 3:C:4], op.add, ["z1", "v40", "v41"], ["z1"], c=144)
        cp(T.offZ[:], T.z1[:], ["z1"], ["offZ"], c=72)
        qL, sL = T["qL%d" % r][:], T["sL%d" % r][:]
        mm(1, A, ur(5)[0], ur(5)[1], qL, sL, ["qR5", "sR5"], ext=arr)
        mm(2, A, ur(5)[0], ur(5)[1], qL, sL, ["qR5", "sR5"], ext=arr)
        for b in range(4):
            mm(4 + b, A, T.qE[:, 128 * b:128 * b + 128], T.sE[:, 128 * b:128 * b + 128], qL, sL, ["qE%d" % b], ext=arr)
            act(T.Bh[:, b:4 * A:4], PS(4 + b, 0, A), AF.Copy, [], ["Bh%d" % b], [4 + b], c=A, scale=0.5)
        act(T.KS[:, 3:512:4], PS(2, 0, A), AF.Copy, [], ["KS3"], [2], c=A)
        BK = ["Bh0", "Bh1", "Bh2", "Bh3"]
        KK = ["KS%d" % a for a in (0, 1, 2, 3, 512, 513, 514, 515)]
        KK2 = [k.replace("KS", "KB") for k in KK]
        tt(T.Bm4[:], PS(1, 0, A), T.Mk4[:, 0:A], op.min, ["Mk4"], ["Bm4"], [1], c=A)
        scan(T.hold4[:], T.Mk4[:, A:2 * A], T.Bm4[:], -H, op.min, op.max, ["K4", "Bm4"], ["hold4"], c=A)
        for n in range(8):
            for j in range(4):
                view, p = T.Rt[:, 512 * n + j:512 * n + 512:4], T.hold4[:, 16 * n + 4 * j + 3:16 * n + 4 * j + 4]
                if 4 * n + j in ON_VECTOR:
                    ts(view, PS(1, 0, A), p, None, op.is_lt, None, ["hold4"], ["Rt%d%d" % (n, j)], [1], c=A)
                else:
                    act(view, PS(2, 0, A), AF.Sign, ["hold4"], ["Rt%d%d" % (n, j)], [2], c=A, bias=p, scale=-1.0)
            quant(T.qK[:, A * n:A * n + A], T.sK[:, A * n:A * n + A], T.Rt[:, 512 * n:512 * n + 512], A,
                  ["Rt%d%d" % (n, j) for j in range(4)], ["qK%d" % n])
            mm(3, A, T.qG4[:], T.sG4[:], T.qK[:, A * n:A * n + A], T.sK[:, A * n:A * n + A], ["qG4", "qK%d" % n], n == 0, n == 7)
        for t in range(NT):
            if t == 0:
                scan(T.pm[:], PS(1, 0, A), T.NEG[:], -H, op.max, op.max, ["NEG"], ["pm"], [1], c=A)
            elif t <= SWITCH:
                scan(T.pm[:], T.KO[:, 3:512:4], T.NEG[:], -H, op.max, op.max, ["NEG", "KO"], ["pm"], c=A)
            else:
                scan(T.pb[:], T.KP[:, 3:512:4], T.KP[:, 3:512:4], -H, op.max, op.max, ["KP"], ["pb"], c=A // 2)
                scan(T.drift[:, 0:A + 3], T.four[:, 0:A + 3], T.KP[:, 3:524:4], -H, op.add, op.max,
                     ["four", "k40", "k41", "k42", "KP", "KPe"], ["drift"], c=A + 3)
            e = T.ee[:, t:t + 1]
            offE, offS, offT = [T.offE[:, 6 * t + 2 * j:6 * t + 2 * j + 1] for j in range(3)]
            ok = "off%d" % t
            if t <= SWITCH:
                act(T.st[:], T.pm[:], AF.Sign, ["pm"], ["st", "ee%d" % t], c=A, bias=T.pm[:, A - 1:A], scale=-1.0, accum_out=e)
                ts(T.offE[:, 6 * t:6 * t + 6:2], T.k3[:, 0:3], e, 4.0, op.add, op.mult, ["ee%d" % t, "k30", "k31", "k32"], [ok])
            else:
                ts(T.offE[:, 6 * t:6 * t + 6:2], T.drift[:, A:A + 3], T.pb[:, A - 1:A], -1.0, op.subtract, op.mult,
                   ["drift", "pb"], [ok])
            U, uk = (T.W[:, 49:80:2], "U0") if t == 0 else (T.W[:, 81:112:2], "U1")
            KO, kk = (T.KO[:], "KO") if t < SWITCH else (T.KP[:, 0:4 * A], "KP")
            if t < SWITCH:
                cp(T.KS[:].indirect(offE), U, [ok, uk], KK, c=("scatter", 16, 50))
                scan(KO, T.KS[:, 512:1024], T.KS[:, 0:512], 0.0, op.add, op.min, KK, [kk], c=4 * A)
            if t == SWITCH:
                act(T.KB[:, 3:512:4], PS(3, 0, A), AF.Copy, [], ["KB3"], [3], c=A, scale=-512.0)
            if t < NT - 1:
                cp(T.KB[:].indirect(offE), U, [ok, uk], KK2, c=("scatter", 16, 50))
            if SWITCH <= t < NT - 1:
                scan(KO, T.KB[:, 512:1024], T.KB[:, 0:512], 0.0, op.add, op.min, KK2, [kk], c=2 * A)
            if t < NT - 2:
                tt(T.W[:, 17:48:2], U, T.W[:, 0:16], op.add, [uk, "V0"], ["Wa1"])
                act(T.W[:, 48:80:2], KO.indirect(offS), AF.Identity, [kk, ok, "col2"], ["Wb0"], c=gat(16), bias=col(2), scale=-2.0 ** 11)
                scan(T.W[:, 80:112], T.W[:, 16:48], T.W[:, 48:80], 0.0, op.max, op.min, ["Wa0", "Wa1", "Wb0", "U0"], ["U1"])
            out = T.tab[:, t:16 * TS_:TS_]
            src = T.Bh[:].indirect(offT)
            if t == NT - 1:
                cp(out, src, BK + [ok], ["tab%d" % t], c=gat(16))
            else:
                act(out, src, AF.Copy, BK + [ok], ["tab%d" % t], c=gat(16))
            if last:
                act(T.tabE[:, t:16 * TS_:TS_], T.iq[:].indirect(offT), AF.Copy, ["iq", ok], ["tabE%d" % t], c=gat(16))
        TK = ["tab%d" % t for t in range(NT)] + ["offZ"]
        for h in (1, 0):
            a, b = PART[h]
            for q, i, j in ZCUT[h]:
                z, xh, meals = T.Z[:, 16 * i:16 * j], T.Xh[:, 16 * i:16 * j], T.tab[:].indirect(T.offZ[:, i:j])
                xk = ["Xh%d" % (2 * h), "Xh%d" % (2 * h + 1)]
                if q == "s":
                    act(T.Zo[:, 16 * i:16 * j], meals, AF.Copy, TK, ["Zo%d" % i], c=gat(16 * (j - i)))
                    tt(z, T.Zo[:, 16 * i:16 * j], xh, op.add, ["Zo%d" % i] + xk, ["Z%d" % i], c=16 * (j - i))
                else:
                    tt(z, meals, xh, op.add, TK + xk, ["Z%d" % i], c=gat(16 * (j - i)))
            quant(T.qZ[:, a:b], T.sZ[:, a:b], T.Z[:, 4 * a:4 * b], b - a, ["Z%d" % i for q, i, j in ZCUT[h]], ["qZ%d" % h])
        if last:
            for j in range(6):
                act(T.olw[:, 192 * j:192 * j + 192], T.tabE[:].indirect(T.offZ[:, 12 * j:12 * j + 12]), AF.Copy,
                    ["tabE%d" % t for t in range(NT)] + ["offZ"], ["olw%d" % j], c=gat(192))
            act(T.vlo[:], T.olw[:, 0:4 * C:4], AF.Copy, ["olw%d" % j for j in range(6)], ["vlo"], c=C)
            dma("s", T.ol[:], T.vlo[0:128:16, :], ["vlo"], ["o0"])
        for h in (1, 0):
            lo, hi = PART[h]
            for b in range(4):
                mm(4 * (1 - h) + b, hi - lo, T.qW[:, 128 * b:128 * b + 128], T.sW[:, 128 * b:128 * b + 128],
                   T.qZ[:, lo:hi], T.sZ[:, lo:hi], ["qW", "sW", "qZ%d" % h])
        for h in (1, 0):
            lo, hi = PART[h]
            for b in range(4):
                bk = 4 * (1 - h) + b
                yv = T.Y[:, 4 * lo + b:4 * hi:4]
                tt(yv, PS(bk, 0, hi - lo), yv, op.add, ["Y%d%d" % (h, b)], ["Y%d%d" % (h, b)], [bk], c=hi - lo)
                act(T.X[:, 4 * lo + b:4 * hi:4], yv, AF.Copy, ["Y%d%d" % (h, b)], ["X%d%d" % (h, b)], c=hi - lo, scale=0.03125)
            if not last and h == 1:
                got = upper_part()
            else:
                quant_x(h)
    for h, bk, buf, key in ((1, 0, T.c0, "c0"), (0, 4, T.hold, "hold0")):
        a, b = PART[h]
        mm(bk, b - a, T.qV[:], T.sV[:], T.qX[:, a:b], T.sX[:, a:b], ["qV", "qX%d" % h])
        dma("y", T.oc[:, 4 * a:4 * b], T.qX[:, a:b].bitcast(dt.uint8), ["qX%d" % h], ["o%d" % (1 + h)])
        cp(buf[:, 0:b - a], PS(bk, 0, b - a), [], [key], [bk], c=b - a)
        dma("y", T.y[:, a:b], buf[:, 0:b - a], [key], ["o%d" % (3 + h)])
    for k in range(4):
        dma("s", T.osc[4 * k:4 * k + 4, :], T.sX[32 * k:32 * k + 4, :], QX, ["o%d" % (k + 5)])
    add("y", None, ["o%d" % k for k in range(9)])
    add("g", None, ext=[("loc", n_loc[0])])
    if not ORDER:
        ORDER.extend(arrange(ops))
    emit(g, T, [ops[i] for i in ORDER])
